import numpy as np
import ml_dtypes


def mxq(x, axis, fmt="e4m3"):
    dtype, down = {"e4m3": (ml_dtypes.float8_e4m3fn, 7), "e5m2": (ml_dtypes.float8_e5m2, 14)}[fmt]
    v = np.moveaxis(np.asarray(x, np.float32).astype(ml_dtypes.bfloat16).astype(np.float64), axis, -1)
    blocks = v.reshape(v.shape[:-1] + (-1, 32))
    amax = np.abs(blocks).max(-1, keepdims=True)
    byte = np.maximum(np.where(amax > 0, np.frexp(amax)[1] - 1 + 127, 0) - down, 1)
    scale = np.exp2(byte - 127.0)
    codes = (blocks / scale).astype(np.float32).astype(dtype).astype(np.float64)
    return np.moveaxis((codes * scale).reshape(v.shape), -1, axis)


WIDE = False


def mx_kscale(k):
    if not WIDE:
        return np.ones(k)
    levels = np.array([10, -10, 5, -5, 0])
    if k % 512:
        return np.exp2(np.random.permutation(np.resize(levels, k // 32))).repeat(32)
    a = np.empty((k // 512, 16))
    for p in range(k // 512):
        a[p, :8] = np.random.permutation(np.resize(levels, 8))
        for g in range(8):
            far = levels[np.abs(levels - a[p, g]) >= 10]
            a[p, g + 8] = far[np.random.randint(len(far))]
    return np.exp2(a.ravel()).repeat(32)


def f64(x):
    return np.asarray(x).astype(np.float64)


def striped(idx):
    return np.tile(idx.reshape(-1, 16).T, (8, 1)).astype(np.uint16)


def unstriped(offs):
    return offs[:16].T.reshape(-1).astype(np.int64)


E2M1 = np.array([0.0, 0.5, 1.0, 1.5, 2.0, 3.0, 4.0, 6.0, -0.0, -0.5, -1.0, -1.5, -2.0, -3.0, -4.0, -6.0])


def pack_weight(w, fmt):
    k, n = w.shape
    w = f64(np.asarray(w, np.float32).astype(ml_dtypes.bfloat16)).reshape(k // 32, 32, n)
    amax = np.abs(w).max(1)
    if fmt == "e4m3":
        byte = np.frexp(amax)[1] - 1 + 127 - 7
    else:
        mant, ex = np.frexp(amax / 6.0)
        byte = np.where(mant > 0.5, ex, ex - 1) + 127
    byte = np.clip(np.where(amax > 0, byte, 1), 1, 254)
    scaled = (w * np.exp2(127.0 - byte)[:, None, :]).reshape(k, n).astype(np.float32)
    by_word = np.ascontiguousarray(scaled.reshape(k // 512, 128, 4, n).transpose(0, 1, 3, 2))
    if fmt == "e4m3":
        words = by_word.astype(ml_dtypes.float8_e4m3fn).view(np.uint8)
    else:
        c = by_word.astype(ml_dtypes.float4_e2m1fn).view(np.uint8) & 0xF
        words = (c[..., 0::2] | (c[..., 1::2] << 4)).reshape(k // 512, 128, 2 * n)
    return np.ascontiguousarray(words), np.ascontiguousarray(byte.astype(np.uint8).reshape(k // 512, 16, n))


def unpack_weight(words, scales, fmt):
    g, _, n = scales.shape
    words = np.ascontiguousarray(words).reshape(g, 128, n, -1)
    if fmt == "e4m3":
        vals = words.view(ml_dtypes.float8_e4m3fn).astype(np.float64)
    else:
        nib = np.empty((g, 128, n, 4), np.uint8)
        nib[..., 0::2] = words & 0xF
        nib[..., 1::2] = words >> 4
        vals = E2M1[nib]
    vals = vals * np.repeat(np.exp2(scales.astype(np.float64) - 127.0), 8, axis=1)[..., None]
    return vals.transpose(0, 1, 3, 2).reshape(g * 512, n)


def gelu(v):
    return 0.5 * v * (1.0 + np.tanh(np.sqrt(2.0 / np.pi) * (v + 0.044715 * v**3)))


K, H, N, T, S, P, P2 = 1024, 1024, 512, 2048, 1024, 512, 256

def setup_inputs():
    n = np.random.standard_normal
    s = mx_kscale(K)[:, None]
    u = mx_kscale(H)[:, None]
    tab_words, tab_scales = pack_weight(n((K, T)) * s, "e4m3")
    w2_words, w2_scales = pack_weight(n((H, N)) / np.sqrt(H) / u, "e2m1")
    essays = np.random.permutation(S)
    comparisons = np.random.permutation(P)
    return {
        "tab_words": tab_words, "tab_scales": tab_scales,
        "offs": striped(np.random.permutation(T)[:S]),
        "w1": (n((K, H)) / np.sqrt(K) / s).astype(np.float32),
        "pos1": striped(essays[:P]),
        "pos2": striped(essays[P:P + P]),
        "gain": (np.exp(0.3 * n(H)) * u[:, 0]).astype(np.float32),
        "w2_words": w2_words, "w2_scales": w2_scales,
        "pos3": striped(comparisons[:P2]),
        "pos4": striped(comparisons[P2:P2 + P2]),
    }

def reference(tab_words, tab_scales, offs, w1, pos1, pos2, gain, w2_words, w2_scales, pos3, pos4):
    v = unpack_weight(tab_words, tab_scales, "e4m3")[:, unstriped(offs)]
    h = mxq(f64(w1), 0, "e4m3").T @ v
    z = f64(gain)[:, None] * np.tanh(h[:, unstriped(pos1)] - h[:, unstriped(pos2)])
    w2 = unpack_weight(w2_words, w2_scales, "e2m1")
    y = w2.T @ mxq(z, 0, "e4m3")
    left = y[:, unstriped(pos3)]
    right = y[:, unstriped(pos4)]
    return left * (1.0 + right)

@@ -1,0 +1,234 @@
+from contextlib import ExitStack
+
+import concourse.mybir as mybir
+
+K, H, N, T, S, P1, P2 = 1024, 1024, 512, 2048, 1024, 512, 256
+FLOPS = 2 * K * H * S + 2 * H * N * P1
+
+F32 = mybir.dt.float32
+BF16 = mybir.dt.bfloat16
+I32 = mybir.dt.int32
+U32 = mybir.dt.uint32
+U16 = mybir.dt.uint16
+U8 = mybir.dt.uint8
+FP8X4 = mybir.dt.float8_e4m3fn_x4
+FP4X4 = mybir.dt.float4_e2m1fn_x4
+ALU = mybir.AluOpType
+ACT = mybir.ActivationFunctionType
+
+P = 128
+PACK = 4
+KP = P * PACK
+BANK = 512
+HALF = 256
+
+
+def tile_list_peer_grading_kernel(tc, tab_words, tab_scales, offs, w1, pos1, pos2, gain,
+                                            w2_words, w2_scales, pos3, pos4, out):
+    nc = tc.nc
+    with ExitStack() as ctx:
+        keep = ctx.enter_context(tc.tile_pool(name="keep", bufs=1))
+        psum = ctx.enter_context(tc.psum_pool(name="psum", bufs=1))
+
+        def tile(shape, dtype, name):
+            return keep.tile(shape, dtype, name=name, align_bytes=64)
+
+        offs_t = tile([P, S // 16], U16, "offs_t")
+        pos1_t = tile([P, P1 // 16], U16, "pos1_t")
+        pos2_t = tile([P, P1 // 16], U16, "pos2_t")
+        pos3_t = tile([P, P2 // 16], U16, "pos3_t")
+        pos4_t = tile([P, P2 // 16], U16, "pos4_t")
+        tabw = [tile([P, T], I32, "tabw%d" % a) for a in range(2)]
+        tabs = tile([P, T], U8, "tabs")
+        vw = [tile([P, S], U32, "vw%d" % a) for a in range(2)]
+        vs = tile([P, S], U8, "vs")
+        raw = {(g, a, c): tile([P, PACK, HALF], F32, "raw%d%d%d" % (g, a, c))
+               for g in range(2) for a in range(2) for c in range(2)}
+        wb = {(g, a): tile([P, KP * PACK], BF16, "wb%d%d" % (g, a)) for g in range(2) for a in range(2)}
+        wq = {(g, a): tile([P, KP], U32, "wq%d%d" % (g, a)) for g in range(2) for a in range(2)}
+        ws = {(g, a): tile([P, KP], U8, "ws%d%d" % (g, a)) for g in range(2) for a in range(2)}
+        gain_t = tile([P, 2, PACK], F32, "gain_t")
+        w2w = tile([P, 2, 2 * N], U8, "w2w")
+        w2s = tile([P, 2, N], U8, "w2s")
+        h = [tile([P, S], F32, "h%d" % i) for i in range(8)]
+        right1 = [tile([P, P1], F32, "right1_%d" % i) for i in range(8)]
+        diff = [tile([P, P1], F32, "diff%d" % i) for i in range(8)]
+        th = [tile([P, P1], F32, "th%d" % i) for i in range(8)]
+        zb = [tile([P, PACK, P1], BF16, "zb%d" % g) for g in range(2)]
+        zi = [tile([P, P1 * PACK], BF16, "zi%d" % g) for g in range(2)]
+        zq = [tile([P, P1], U32, "zq%d" % g) for g in range(2)]
+        zs = [tile([P, P1], U8, "zs%d" % g) for g in range(2)]
+        y = [tile([P, P1], F32, "y%d" % i) for i in range(4)]
+        right2 = [tile([P, P2], F32, "right2_%d" % i) for i in range(4)]
+        plus1 = [tile([P, P2], F32, "plus1_%d" % i) for i in range(4)]
+        res = [tile([P, P2], F32, "res%d" % i) for i in range(4)]
+        ybank = [psum.tile([P, BANK], F32, name="ybank%d" % i) for i in range(4)]
+
+        nc.gpsimd.memset(tabs[:].bitcast(I32), 0)
+        nc.gpsimd.memset(w2s[:].rearrange("p a n -> p (a n)").bitcast(I32), 0)
+
+        def load_w1(g, a, c):
+            c0 = KP * g + HALF * c
+            nc.sync.dma_start(out=raw[g, a, c][:],
+                              in_=w1[KP * a:KP * (a + 1), c0:c0 + HALF].rearrange("(p j) c -> p j c", j=PACK))
+
+        nc.sync.dma_start(offs_t[:], offs)
+        for q in range(4):
+            nc.sync.dma_start(out=tabs[32 * q:32 * q + 8, :].bitcast(I32),
+                              in_=tab_scales[:, 4 * q:4 * q + 4, :].bitcast(I32))
+        for a in range(2):
+            nc.sync.dma_start(out=tabw[a][:], in_=tab_words[a].rearrange("p t i -> p (t i)").bitcast(I32))
+        for a in range(2):
+            for c in range(2):
+                load_w1(0, a, c)
+        nc.sync.dma_start(pos2_t[:], pos2)
+        nc.sync.dma_start(pos1_t[:], pos1)
+        for a in range(2):
+            for c in range(2):
+                load_w1(1, a, c)
+        nc.sync.dma_start(out=gain_t[:], in_=gain.rearrange("(g p t) -> p g t", g=2, t=PACK))
+        nc.sync.dma_start(out=w2w[:].bitcast(I32), in_=w2_words.rearrange("a p b -> p a b").bitcast(I32))
+        for q in range(4):
+            nc.sync.dma_start(out=w2s[32 * q:32 * q + 4, :, :].bitcast(I32),
+                              in_=w2_scales[:, 4 * q:4 * q + 4, :].rearrange("a r n -> r a n").bitcast(I32))
+        nc.sync.dma_start(pos4_t[:], pos4)
+        nc.sync.dma_start(pos3_t[:], pos3)
+
+        def cast_w1(g, a, c, on_vector):
+            dst = wb[g, a][:].rearrange("p (t m j) -> p m j t", t=PACK, j=PACK)[:, 64 * c:64 * (c + 1), :, :]
+            src = raw[g, a, c][:].rearrange("p j (m t) -> p m j t", t=PACK)
+            if on_vector:
+                nc.vector.tensor_copy(out=dst, in_=src)
+            else:
+                nc.scalar.copy(out=dst, in_=src)
+
+        def quant_w1(g, a):
+            nc.vector.quantize_mx(out=wq[g, a][:].bitcast(FP8X4), scales=ws[g, a][:], in_=wb[g, a][:])
+
+        def first_product(i, s, on_vector=False):
+            g, t = divmod(i, PACK)
+            bank = psum.tile([P, BANK], F32, name="hbank", tag="hbank", bufs=4)
+            cols = slice(BANK * s, BANK * (s + 1))
+            for a in range(2):
+                nc.tensor.matmul_mx(out=bank[:], lhsT=wq[g, a][:, P * t:P * (t + 1)].bitcast(FP8X4),
+                                    lhsT_scale=ws[g, a][:, P * t:P * (t + 1)],
+                                    rhs=vw[a][:, cols].bitcast(FP8X4), rhs_scale=vs[4 * a:P, cols],
+                                    start=(a == 0), stop=(a == 1))
+            if on_vector:
+                nc.vector.tensor_copy(out=h[i][:, cols], in_=bank[:])
+            else:
+                nc.scalar.copy(out=h[i][:, cols], in_=bank[:])
+
+        def product(i):
+            first_product(i, 0)
+            first_product(i, 1)
+
+        def pick_right(i, u):
+            nc.vector.tensor_copy(out=right1[i][:, HALF * u:HALF * (u + 1)],
+                                  in_=h[i][:].indirect(pos2_t[:, 16 * u:16 * (u + 1)]))
+
+        def pick_diff(i, u):
+            cols = slice(HALF * u, HALF * (u + 1))
+            nc.vector.tensor_tensor(diff[i][:, cols], h[i][:].indirect(pos1_t[:, 16 * u:16 * (u + 1)]),
+                                    right1[i][:, cols], ALU.subtract)
+
+        def picks(i):
+            pick_right(i, 0)
+            pick_right(i, 1)
+            pick_diff(i, 0)
+            pick_diff(i, 1)
+
+        def squash(i, c0, c1):
+            g, t = divmod(i, PACK)
+            nc.scalar.activation(out=th[i][:, c0:c1], in_=diff[i][:, c0:c1], func=ACT.Tanh)
+            nc.scalar.activation(out=zb[g][:, t, c0:c1], in_=th[i][:, c0:c1], func=ACT.Copy,
+                                 scale=gain_t[:, g, t:t + 1])
+
+        def weave(g, c0, c1):
+            nc.vector.tensor_copy(out=zi[g][:, PACK * c0:PACK * c1].rearrange("p (c i t) -> p c t i", i=4, t=PACK),
+                                  in_=zb[g][:, :, c0:c1].rearrange("p t (c i) -> p c t i", i=4))
+
+        def quant_z(g, c0, c1):
+            nc.vector.quantize_mx(out=zq[g][:, c0:c1].bitcast(FP8X4), scales=zs[g][:, c0:c1],
+                                  in_=zi[g][:, PACK * c0:PACK * c1])
+
+        def second_product(n, g, c0, c1, start, stop):
+            nc.tensor.matmul_mx(out=ybank[n][:, c0:c1], lhsT=w2w[:, g, 2 * P * n:2 * P * (n + 1)].bitcast(FP4X4),
+                                lhsT_scale=w2s[:, g, P * n:P * (n + 1)],
+                                rhs=zq[g][:, c0:c1].bitcast(FP8X4), rhs_scale=zs[g][:, c0:c1],
+                                start=start, stop=stop)
+
+        nc.vector.tensor_copy(out=vs[:], in_=tabs[:].indirect(offs_t[:]))
+        for a in range(2):
+            nc.vector.tensor_copy(out=vw[a][:], in_=tabw[a][:].bitcast(U32).indirect(offs_t[:]))
+        cast_w1(0, 0, 0, False)
+        cast_w1(0, 0, 1, False)
+        cast_w1(0, 1, 0, True)
+        quant_w1(0, 0)
+        cast_w1(0, 1, 1, True)
+        quant_w1(0, 1)
+        first_product(0, 0)
+        first_product(0, 1, True)
+        product(1)
+        picks(0)
+        cast_w1(1, 0, 0, False)
+        product(2)
+        cast_w1(1, 0, 1, False)
+        picks(1)
+        quant_w1(1, 0)
+        product(3)
+        cast_w1(1, 1, 0, False)
+        cast_w1(1, 1, 1, False)
+        picks(2)
+        quant_w1(1, 1)
+        squash(0, 0, P1)
+        squash(1, 0, P1)
+        picks(3)
+        product(4)
+        product(5)
+        picks(4)
+        squash(2, 0, P1)
+        product(6)
+        squash(3, 0, P1)
+        picks(5)
+        product(7)
+        weave(0, 0, P1)
+        squash(4, 0, P1)
+        pick_right(6, 0)
+        quant_z(0, 0, P1)
+        for n in range(4):
+            second_product(n, 0, 0, P1, True, False)
+        pick_right(7, 0)
+        pick_diff(6, 0)
+        pick_diff(7, 0)
+        squash(5, 0, P1)
+        squash(6, 0, HALF)
+        squash(7, 0, HALF)
+        pick_right(6, 1)
+        pick_right(7, 1)
+        pick_diff(6, 1)
+        pick_diff(7, 1)
+        squash(6, HALF, P1)
+        squash(7, HALF, P1)
+        weave(1, 0, HALF)
+        quant_z(1, 0, HALF)
+        for n in range(4):
+            for c in range(2):
+                second_product(n, 1, P * c, P * (c + 1), False, False)
+        weave(1, HALF, P1)
+        quant_z(1, HALF, P1)
+        for n in range(4):
+            for c in range(2, 4):
+                second_product(n, 1, P * c, P * (c + 1), False, c == 3)
+
+        def finish(n):
+            nc.scalar.activation(out=plus1[n][:], in_=right2[n][:], func=ACT.Copy, bias=1.0)
+            nc.vector.tensor_tensor(res[n][:], y[n][:].indirect(pos3_t[:]), plus1[n][:], ALU.mult)
+            nc.sync.dma_start(out=out[P * n:P * (n + 1), :], in_=res[n][:])
+
+        for n in range(4):
+            nc.scalar.copy(out=y[n][:], in_=ybank[n][:])
+            nc.vector.tensor_copy(out=right2[n][:], in_=y[n][:].indirect(pos4_t[:]))
+            if n > 0:
+                finish(n - 1)
+        finish(3)

@@ -21,6 +21,9 @@ PACK = 4
 KP = P * PACK
 BANK = 512
 HALF = 256
+PIECES = [(0, 128), (128, 256), (256, 512), (512, 768), (768, 1024)]
+GP_SUB = ()
+GP_GAIN = ()
 
 
 def tile_list_peer_grading_kernel(tc, tab_words, tab_scales, offs, w1, pos1, pos2, gain,
@@ -30,8 +33,8 @@ def tile_list_peer_grading_kernel(tc, tab_words, tab_scales, offs, w1, pos1, pos
         keep = ctx.enter_context(tc.tile_pool(name="keep", bufs=1))
         psum = ctx.enter_context(tc.psum_pool(name="psum", bufs=1))
 
-        def tile(shape, dtype, name):
-            return keep.tile(shape, dtype, name=name, align_bytes=64)
+        def tile(shape, dtype, name, tag=None):
+            return keep.tile(shape, dtype, name=name, tag=tag or name, align_bytes=64)
 
         offs_t = tile([P, S // 16], U16, "offs_t")
         pos1_t = tile([P, P1 // 16], U16, "pos1_t")
@@ -42,51 +45,67 @@ def tile_list_peer_grading_kernel(tc, tab_words, tab_scales, offs, w1, pos1, pos
         tabs = tile([P, T], U8, "tabs")
         vw = [tile([P, S], U32, "vw%d" % a) for a in range(2)]
         vs = tile([P, S], U8, "vs")
-        raw = {(g, a, c): tile([P, PACK, HALF], F32, "raw%d%d%d" % (g, a, c))
-               for g in range(2) for a in range(2) for c in range(2)}
+        raw = {(a, c): tile([P, PACK, c1 - c0], F32, "raw%d%d" % (a, c))
+               for a in range(2) for c, (c0, c1) in enumerate(PIECES)}
         wb = {(g, a): tile([P, KP * PACK], BF16, "wb%d%d" % (g, a)) for g in range(2) for a in range(2)}
         wq = {(g, a): tile([P, KP], U32, "wq%d%d" % (g, a)) for g in range(2) for a in range(2)}
         ws = {(g, a): tile([P, KP], U8, "ws%d%d" % (g, a)) for g in range(2) for a in range(2)}
-        gain_t = tile([P, 2, PACK], F32, "gain_t")
+        gains = [tile([P, PACK], F32, "gain%d" % g) for g in range(2)]
         w2w = tile([P, 2, 2 * N], U8, "w2w")
         w2s = tile([P, 2, N], U8, "w2s")
-        h = [tile([P, S], F32, "h%d" % i) for i in range(8)]
-        right1 = [tile([P, P1], F32, "right1_%d" % i) for i in range(8)]
-        diff = [tile([P, P1], F32, "diff%d" % i) for i in range(8)]
-        th = [tile([P, P1], F32, "th%d" % i) for i in range(8)]
+        h = {i: tile([P, S], F32, "h%d" % i) for i in range(8) if i not in (1, 2, 3)}
+        zn = [tile([P, P1], BF16, "zn%d" % i) for i in range(4)]
         zb = [tile([P, PACK, P1], BF16, "zb%d" % g) for g in range(2)]
         zi = [tile([P, P1 * PACK], BF16, "zi%d" % g) for g in range(2)]
+        right1 = [tile([P, P1], F32, "right1_%d" % i)[:] for i in range(8)]
+        diff = [tile([P, P1], F32, "diff%d" % i)[:] for i in range(7)] + [zi[0][:].bitcast(F32)[:, 0:P1]]
+        spent = raw[1, 3][:].rearrange("p j c -> p (j c)")
+        woven = zb[0][:].rearrange("p t c -> p (t c)").bitcast(F32)
+        th = [spent[:, 0:P1], spent[:, P1:2 * P1]] + [tile([P, P1], F32, "th%d" % i)[:] for i in range(2, 5)]
+        th += [woven[:, 0:P1], woven[:, P1:2 * P1], tile([P, HALF], F32, "th7")[:]]
+        left1 = {i: tile([P, P1], F32, "left1_%d" % (i % 2), "left1_%d" % (i % 2)) for i in GP_SUB[:2]}
         zq = [tile([P, P1], U32, "zq%d" % g) for g in range(2)]
         zs = [tile([P, P1], U8, "zs%d" % g) for g in range(2)]
         y = [tile([P, P1], F32, "y%d" % i) for i in range(4)]
         right2 = [tile([P, P2], F32, "right2_%d" % i) for i in range(4)]
         plus1 = [tile([P, P2], F32, "plus1_%d" % i) for i in range(4)]
         res = [tile([P, P2], F32, "res%d" % i) for i in range(4)]
+
         ybank = [psum.tile([P, BANK], F32, name="ybank%d" % i) for i in range(4)]
 
         nc.gpsimd.memset(tabs[:].bitcast(I32), 0)
         nc.gpsimd.memset(w2s[:].rearrange("p a n -> p (a n)").bitcast(I32), 0)
 
-        def load_w1(g, a, c):
-            c0 = KP * g + HALF * c
-            nc.sync.dma_start(out=raw[g, a, c][:],
-                              in_=w1[KP * a:KP * (a + 1), c0:c0 + HALF].rearrange("(p j) c -> p j c", j=PACK))
+        def load_w1(c):
+            c0, c1 = PIECES[c]
+            for a in range(2):
+                nc.sync.dma_start(out=raw[a, c][:],
+                                  in_=w1[KP * a:KP * (a + 1), c0:c1].rearrange("(p j) c -> p j c", j=PACK))
+
+        def load_words(a):
+            nc.sync.dma_start(out=tabw[a][:], in_=tab_words[a].rearrange("p t i -> p (t i)").bitcast(I32))
+
+        def load_scales():
+            for q in range(4):
+                nc.sync.dma_start(out=tabs[32 * q:32 * q + 8, :].bitcast(I32),
+                                  in_=tab_scales[:, 4 * q:4 * q + 4, :].bitcast(I32))
 
         nc.sync.dma_start(offs_t[:], offs)
-        for q in range(4):
-            nc.sync.dma_start(out=tabs[32 * q:32 * q + 8, :].bitcast(I32),
-                              in_=tab_scales[:, 4 * q:4 * q + 4, :].bitcast(I32))
-        for a in range(2):
-            nc.sync.dma_start(out=tabw[a][:], in_=tab_words[a].rearrange("p t i -> p (t i)").bitcast(I32))
-        for a in range(2):
-            for c in range(2):
-                load_w1(0, a, c)
         nc.sync.dma_start(pos2_t[:], pos2)
         nc.sync.dma_start(pos1_t[:], pos1)
+        load_scales()
+        load_words(0)
+        load_w1(0)
+        load_words(1)
+        load_w1(1)
+        load_w1(2)
         for a in range(2):
-            for c in range(2):
-                load_w1(1, a, c)
-        nc.sync.dma_start(out=gain_t[:], in_=gain.rearrange("(g p t) -> p g t", g=2, t=PACK))
+            for c in (3, 4):
+                nc.sync.dma_start(out=raw[a, c][:],
+                                  in_=w1[KP * a:KP * (a + 1), PIECES[c][0]:PIECES[c][1]].rearrange("(p j) c -> p j c", j=PACK))
+        with nc.allow_non_contiguous_dma(reason="one gain to a partition"):
+            nc.sync.dma_start(out=gains[0][:], in_=gain[0:KP].rearrange("(i p) -> p i", p=P))
+        nc.sync.dma_start(out=gains[1][:], in_=gain[KP:2 * KP].rearrange("(p t) -> p t", t=PACK))
         nc.sync.dma_start(out=w2w[:].bitcast(I32), in_=w2_words.rearrange("a p b -> p a b").bitcast(I32))
         for q in range(4):
             nc.sync.dma_start(out=w2s[32 * q:32 * q + 4, :, :].bitcast(I32),
@@ -94,59 +113,68 @@ def tile_list_peer_grading_kernel(tc, tab_words, tab_scales, offs, w1, pos1, pos
         nc.sync.dma_start(pos4_t[:], pos4)
         nc.sync.dma_start(pos3_t[:], pos3)
 
-        def cast_w1(g, a, c, on_vector):
-            dst = wb[g, a][:].rearrange("p (t m j) -> p m j t", t=PACK, j=PACK)[:, 64 * c:64 * (c + 1), :, :]
-            src = raw[g, a, c][:].rearrange("p j (m t) -> p m j t", t=PACK)
+        def cast_w1(a, c, on_vector=False):
+            c0, c1 = PIECES[c]
+            if c1 <= KP:
+                dst = wb[0, a][:, PACK * c0:PACK * c1].rearrange("p (m i j) -> p m j i", i=4, j=PACK)
+            else:
+                m0, m1 = (c0 - KP) // PACK, (c1 - KP) // PACK
+                dst = wb[1, a][:].rearrange("p (t m j) -> p m j t", t=PACK, j=PACK)[:, m0:m1, :, :]
+            src = raw[a, c][:].rearrange("p j (m t) -> p m j t", t=PACK)
             if on_vector:
                 nc.vector.tensor_copy(out=dst, in_=src)
             else:
                 nc.scalar.copy(out=dst, in_=src)
 
-        def quant_w1(g, a):
-            nc.vector.quantize_mx(out=wq[g, a][:].bitcast(FP8X4), scales=ws[g, a][:], in_=wb[g, a][:])
+        def quant_w1(g, a, c0, c1):
+            nc.vector.quantize_mx(out=wq[g, a][:, c0:c1].bitcast(FP8X4), scales=ws[g, a][:, c0:c1],
+                                  in_=wb[g, a][:, PACK * c0:PACK * c1])
 
-        def first_product(i, s, on_vector=False):
+        def product(i, cuts=(0, BANK, S)):
             g, t = divmod(i, PACK)
-            bank = psum.tile([P, BANK], F32, name="hbank", tag="hbank", bufs=4)
-            cols = slice(BANK * s, BANK * (s + 1))
-            for a in range(2):
-                nc.tensor.matmul_mx(out=bank[:], lhsT=wq[g, a][:, P * t:P * (t + 1)].bitcast(FP8X4),
-                                    lhsT_scale=ws[g, a][:, P * t:P * (t + 1)],
-                                    rhs=vw[a][:, cols].bitcast(FP8X4), rhs_scale=vs[4 * a:P, cols],
-                                    start=(a == 0), stop=(a == 1))
-            if on_vector:
-                nc.vector.tensor_copy(out=h[i][:, cols], in_=bank[:])
+            for c0, c1 in zip(cuts, cuts[1:]):
+                bank = psum.tile([P, BANK], F32, name="hbank", tag="hbank", bufs=4)
+                cols = slice(c0, c1)
+                for a in range(2):
+                    nc.tensor.matmul_mx(out=bank[:, 0:c1 - c0], lhsT=wq[g, a][:, P * t:P * (t + 1)].bitcast(FP8X4),
+                                        lhsT_scale=ws[g, a][:, P * t:P * (t + 1)],
+                                        rhs=vw[a][:, cols].bitcast(FP8X4), rhs_scale=vs[4 * a:P, cols],
+                                        start=(a == 0), stop=(a == 1))
+                nc.scalar.copy(out=h[i][:, cols], in_=bank[:, 0:c1 - c0])
+
+        def picks(i, cuts=(0, HALF, P1)):
+            if i in GP_SUB:
+                left = left1[GP_SUB[i % 2]]
+                nc.vector.tensor_copy(out=right1[i], in_=h[i][:].indirect(pos2_t[:]))
+                nc.vector.tensor_copy(out=left[:], in_=h[i][:].indirect(pos1_t[:]))
+                nc.gpsimd.tensor_tensor(diff[i], left[:], right1[i], ALU.subtract)
+                return
+            for u in range(2):
+                nc.vector.tensor_copy(out=right1[i][:, HALF * u:HALF * (u + 1)],
+                                      in_=h[i][:].indirect(pos2_t[:, 16 * u:16 * (u + 1)]))
+            for c0, c1 in zip(cuts, cuts[1:]):
+                nc.vector.tensor_tensor(diff[i][:, c0:c1], h[i][:].indirect(pos1_t[:, c0 // 16:c1 // 16]),
+                                        right1[i][:, c0:c1], ALU.subtract)
+
+        def squash(i, c0=0, c1=P1):
+            g, t = divmod(i, PACK)
+            nc.scalar.activation(out=th[i][:, 0:c1 - c0], in_=diff[i][:, c0:c1], func=ACT.Tanh)
+            dst = zn[t][:, c0:c1] if g == 0 else zb[g][:, t, c0:c1]
+            if i in GP_GAIN:
+                nc.gpsimd.tensor_scalar(dst, th[i][:, 0:c1 - c0], gains[g][:, t:t + 1], 0.0, ALU.mult, ALU.add)
             else:
-                nc.scalar.copy(out=h[i][:, cols], in_=bank[:])
+                nc.scalar.activation(out=dst, in_=th[i][:, 0:c1 - c0], func=ACT.Copy, scale=gains[g][:, t:t + 1])
+            if g == 0:
+                for r in range(PACK):
+                    nc.sync.dma_start(out=zb[0][32 * t:32 * (t + 1), r, :], in_=zn[t][r:P:PACK, :])
 
-        def product(i):
-            first_product(i, 0)
-            first_product(i, 1)
-
-        def pick_right(i, u):
-            nc.vector.tensor_copy(out=right1[i][:, HALF * u:HALF * (u + 1)],
-                                  in_=h[i][:].indirect(pos2_t[:, 16 * u:16 * (u + 1)]))
-
-        def pick_diff(i, u):
-            cols = slice(HALF * u, HALF * (u + 1))
-            nc.vector.tensor_tensor(diff[i][:, cols], h[i][:].indirect(pos1_t[:, 16 * u:16 * (u + 1)]),
-                                    right1[i][:, cols], ALU.subtract)
-
-        def picks(i):
-            pick_right(i, 0)
-            pick_right(i, 1)
-            pick_diff(i, 0)
-            pick_diff(i, 1)
-
-        def squash(i, c0, c1):
-            g, t = divmod(i, PACK)
-            nc.scalar.activation(out=th[i][:, c0:c1], in_=diff[i][:, c0:c1], func=ACT.Tanh)
-            nc.scalar.activation(out=zb[g][:, t, c0:c1], in_=th[i][:, c0:c1], func=ACT.Copy,
-                                 scale=gain_t[:, g, t:t + 1])
-
-        def weave(g, c0, c1):
-            nc.vector.tensor_copy(out=zi[g][:, PACK * c0:PACK * c1].rearrange("p (c i t) -> p c t i", i=4, t=PACK),
-                                  in_=zb[g][:, :, c0:c1].rearrange("p t (c i) -> p c t i", i=4))
+        def weave(g, c0, c1, on_vector=True):
+            dst = zi[g][:, PACK * c0:PACK * c1].rearrange("p (c i t) -> p c t i", i=4, t=PACK)
+            src = zb[g][:, :, c0:c1].rearrange("p t (c i) -> p c t i", i=4)
+            if on_vector:
+                nc.vector.tensor_copy(out=dst, in_=src)
+            else:
+                nc.scalar.copy(out=dst, in_=src)
 
         def quant_z(g, c0, c1):
             nc.vector.quantize_mx(out=zq[g][:, c0:c1].bitcast(FP8X4), scales=zs[g][:, c0:c1],
@@ -158,57 +186,67 @@ def tile_list_peer_grading_kernel(tc, tab_words, tab_scales, offs, w1, pos1, pos
                                 rhs=zq[g][:, c0:c1].bitcast(FP8X4), rhs_scale=zs[g][:, c0:c1],
                                 start=start, stop=stop)
 
-        nc.vector.tensor_copy(out=vs[:], in_=tabs[:].indirect(offs_t[:]))
-        for a in range(2):
-            nc.vector.tensor_copy(out=vw[a][:], in_=tabw[a][:].bitcast(U32).indirect(offs_t[:]))
-        cast_w1(0, 0, 0, False)
-        cast_w1(0, 0, 1, False)
-        cast_w1(0, 1, 0, True)
-        quant_w1(0, 0)
-        cast_w1(0, 1, 1, True)
-        quant_w1(0, 1)
-        first_product(0, 0)
-        first_product(0, 1, True)
-        product(1)
+        def pick_words(a, c0, c1):
+            nc.vector.tensor_copy(out=vw[a][:, c0:c1],
+                                  in_=tabw[a][:].bitcast(U32).indirect(offs_t[:, c0 // 16:c1 // 16]))
+
+        def pick_scales():
+            nc.vector.tensor_copy(out=vs[:], in_=tabs[:].indirect(offs_t[:]))
+
+        pick_scales()
+        pick_words(0, 0, S)
+        cast_w1(0, 0)
+        cast_w1(1, 0)
+        quant_w1(0, 0, 0, P)
+        quant_w1(0, 1, 0, P)
+        pick_words(1, 0, BANK)
+        pick_words(1, BANK, 768)
+        pick_words(1, 768, S)
+        product(0, (0, BANK, 768, S))
+        cast_w1(0, 1, True)
+        cast_w1(1, 1, True)
+        quant_w1(0, 0, P, HALF)
+        quant_w1(0, 1, P, HALF)
         picks(0)
-        cast_w1(1, 0, 0, False)
-        product(2)
-        cast_w1(1, 0, 1, False)
+        cast_w1(0, 2)
+        cast_w1(1, 2)
+        quant_w1(0, 0, HALF, KP)
+        quant_w1(0, 1, HALF, KP)
+        h[1] = tile([P, S], F32, "h1", "raw12")
+        product(1)
         picks(1)
-        quant_w1(1, 0)
-        product(3)
-        cast_w1(1, 1, 0, False)
-        cast_w1(1, 1, 1, False)
+        cast_w1(0, 3)
+        cast_w1(0, 4)
+        quant_w1(1, 0, 0, KP)
+        h[2] = tile([P, S], F32, "h2", "raw04")
+        product(2)
         picks(2)
-        quant_w1(1, 1)
-        squash(0, 0, P1)
-        squash(1, 0, P1)
+        cast_w1(1, 3)
+        cast_w1(1, 4)
+        quant_w1(1, 1, 0, KP)
+        h[3] = tile([P, S], F32, "h3", "raw14")
+        product(3)
         picks(3)
+        squash(0)
+        squash(1)
         product(4)
-        product(5)
         picks(4)
-        squash(2, 0, P1)
-        product(6)
-        squash(3, 0, P1)
+        product(5)
         picks(5)
+        squash(2)
+        squash(3)
+        product(6)
+        picks(6)
+        squash(4)
         product(7)
-        weave(0, 0, P1)
-        squash(4, 0, P1)
-        pick_right(6, 0)
+        weave(0, 0, P1, False)
         quant_z(0, 0, P1)
         for n in range(4):
             second_product(n, 0, 0, P1, True, False)
-        pick_right(7, 0)
-        pick_diff(6, 0)
-        pick_diff(7, 0)
-        squash(5, 0, P1)
-        squash(6, 0, HALF)
+        squash(5)
+        squash(6)
+        picks(7)
         squash(7, 0, HALF)
-        pick_right(6, 1)
-        pick_right(7, 1)
-        pick_diff(6, 1)
-        pick_diff(7, 1)
-        squash(6, HALF, P1)
         squash(7, HALF, P1)
         weave(1, 0, HALF)
         quant_z(1, 0, HALF)

@@ -18,12 +18,16 @@ ACT = mybir.ActivationFunctionType
 
 P = 128
 PACK = 4
-KP = P * PACK
+PASS = P * PACK
+PASSES = 2
 BANK = 512
-HALF = 256
+LANES = 16
+RUN = 4
+HALF = P1 // 2
+TILES = H // P
+LAST = TILES - 1
 PIECES = [(0, 128), (128, 256), (256, 512), (512, 768), (768, 1024)]
-GP_SUB = ()
-GP_GAIN = ()
+FIRST_CUTS = (0, 512, 768, 1024)
 
 
 def tile_list_peer_grading_kernel(tc, tab_words, tab_scales, offs, w1, pos1, pos2, gain,
@@ -36,237 +40,222 @@ def tile_list_peer_grading_kernel(tc, tab_words, tab_scales, offs, w1, pos1, pos
         def tile(shape, dtype, name, tag=None):
             return keep.tile(shape, dtype, name=name, tag=tag or name, align_bytes=64)
 
-        offs_t = tile([P, S // 16], U16, "offs_t")
-        pos1_t = tile([P, P1 // 16], U16, "pos1_t")
-        pos2_t = tile([P, P1 // 16], U16, "pos2_t")
-        pos3_t = tile([P, P2 // 16], U16, "pos3_t")
-        pos4_t = tile([P, P2 // 16], U16, "pos4_t")
-        tabw = [tile([P, T], I32, "tabw%d" % a) for a in range(2)]
-        tabs = tile([P, T], U8, "tabs")
-        vw = [tile([P, S], U32, "vw%d" % a) for a in range(2)]
-        vs = tile([P, S], U8, "vs")
+        offs_t = tile([P, S // LANES], U16, "offs_t")
+        pos1_t = tile([P, P1 // LANES], U16, "pos1_t")
+        pos2_t = tile([P, P1 // LANES], U16, "pos2_t")
+        pos3_t = tile([P, P2 // LANES], U16, "pos3_t")
+        pos4_t = tile([P, P2 // LANES], U16, "pos4_t")
+        table_words = [tile([P, T], I32, "table_words%d" % a) for a in range(PASSES)]
+        table_scales = tile([P, T], U8, "table_scales")
+        v_words = [tile([P, S], U32, "v_words%d" % a) for a in range(PASSES)]
+        v_scales = tile([P, S], U8, "v_scales")
         raw = {(a, c): tile([P, PACK, c1 - c0], F32, "raw%d%d" % (a, c))
-               for a in range(2) for c, (c0, c1) in enumerate(PIECES)}
-        wb = {(g, a): tile([P, KP * PACK], BF16, "wb%d%d" % (g, a)) for g in range(2) for a in range(2)}
-        wq = {(g, a): tile([P, KP], U32, "wq%d%d" % (g, a)) for g in range(2) for a in range(2)}
-        ws = {(g, a): tile([P, KP], U8, "ws%d%d" % (g, a)) for g in range(2) for a in range(2)}
-        gains = [tile([P, PACK], F32, "gain%d" % g) for g in range(2)]
-        w2w = tile([P, 2, 2 * N], U8, "w2w")
-        w2s = tile([P, 2, N], U8, "w2s")
-        h = {i: tile([P, S], F32, "h%d" % i) for i in range(8) if i not in (1, 2, 3)}
-        zn = [tile([P, P1], BF16, "zn%d" % i) for i in range(4)]
-        zb = [tile([P, PACK, P1], BF16, "zb%d" % g) for g in range(2)]
-        zi = [tile([P, P1 * PACK], BF16, "zi%d" % g) for g in range(2)]
-        right1 = [tile([P, P1], F32, "right1_%d" % i)[:] for i in range(8)]
-        diff = [tile([P, P1], F32, "diff%d" % i)[:] for i in range(7)] + [zi[0][:].bitcast(F32)[:, 0:P1]]
+               for a in range(PASSES) for c, (c0, c1) in enumerate(PIECES)}
+        widths = [2 * P, 2 * P, PASS, PASS, PASS]
+        w1_woven = [tile([P, PACK * w], BF16, "w1_woven%d" % u) for u, w in enumerate(widths)]
+        w1_words = [tile([P, w], U32, "w1_words%d" % u) for u, w in enumerate(widths)]
+        w1_scales = [tile([P, w], U8, "w1_scales%d" % u) for u, w in enumerate(widths)]
+        gains = [tile([P, PACK], F32, "gain%d" % a) for a in range(PASSES)]
+        w2_codes = tile([P, PASSES, 2 * N], U8, "w2_codes")
+        w2_bytes = tile([P, PASSES, N], U8, "w2_bytes")
+        h = {i: tile([P, S], F32, "h%d" % i) for i in range(PACK, TILES)}
+        z_rows = [tile([P, P1], BF16, "z_rows%d" % i) for i in range(PACK)]
+        z_planes = [tile([P, PACK, P1], BF16, "z_planes%d" % a) for a in range(PASSES)]
+        z_woven = [tile([P, P1 * PACK], BF16, "z_woven%d" % a) for a in range(PASSES)]
+
+        spent = raw[1, 2][:].rearrange("p j c -> p (j c)")
+        second = [spent[:, P1 * i:P1 * (i + 1)] for i in range(2)]
+        second += [tile([P, P1], F32, "second%d" % i)[:] for i in range(2, TILES)]
+        diff = [tile([P, P1], F32, "diff%d" % i)[:] for i in range(LAST)]
+        diff += [z_woven[0][:].bitcast(F32)[:, 0:P1]]
         spent = raw[1, 3][:].rearrange("p j c -> p (j c)")
-        woven = zb[0][:].rearrange("p t c -> p (t c)").bitcast(F32)
-        th = [spent[:, 0:P1], spent[:, P1:2 * P1]] + [tile([P, P1], F32, "th%d" % i)[:] for i in range(2, 5)]
-        th += [woven[:, 0:P1], woven[:, P1:2 * P1], tile([P, HALF], F32, "th7")[:]]
-        left1 = {i: tile([P, P1], F32, "left1_%d" % (i % 2), "left1_%d" % (i % 2)) for i in GP_SUB[:2]}
-        zq = [tile([P, P1], U32, "zq%d" % g) for g in range(2)]
-        zs = [tile([P, P1], U8, "zs%d" % g) for g in range(2)]
-        y = [tile([P, P1], F32, "y%d" % i) for i in range(4)]
-        right2 = [tile([P, P2], F32, "right2_%d" % i) for i in range(4)]
-        plus1 = [tile([P, P2], F32, "plus1_%d" % i) for i in range(4)]
-        res = [tile([P, P2], F32, "res%d" % i) for i in range(4)]
+        bounded = [spent[:, P1 * i:P1 * (i + 1)] for i in range(2)]
+        bounded += [tile([P, P1], F32, "bounded%d" % i)[:] for i in range(2, 5)]
+        spent = z_planes[0][:].rearrange("p t c -> p (t c)").bitcast(F32)
+        bounded += [spent[:, P1 * i:P1 * (i + 1)] for i in range(2)]
+        bounded += [tile([P, P1], F32, "bounded%d" % LAST)[:]]
 
-        ybank = [psum.tile([P, BANK], F32, name="ybank%d" % i) for i in range(4)]
+        z_words = [tile([P, P1], U32, "z_words%d" % a) for a in range(PASSES)]
+        z_scales = [tile([P, P1], U8, "z_scales%d" % a) for a in range(PASSES)]
+        y = [tile([P, P1], F32, "y%d" % n) for n in range(N // P)]
+        right = [tile([P, P2], F32, "right%d" % n) for n in range(N // P)]
+        one_plus = [tile([P, P2], F32, "one_plus%d" % n) for n in range(N // P)]
+        result = [tile([P, P2], F32, "result%d" % n) for n in range(N // P)]
+        y_bank = [psum.tile([P, BANK], F32, name="y_bank%d" % n) for n in range(N // P)]
 
-        nc.gpsimd.memset(tabs[:].bitcast(I32), 0)
-        nc.gpsimd.memset(w2s[:].rearrange("p a n -> p (a n)").bitcast(I32), 0)
+        nc.gpsimd.memset(table_scales[:].bitcast(I32), 0)
+        nc.gpsimd.memset(w2_bytes[:].rearrange("p a n -> p (a n)").bitcast(I32), 0)
 
-        def load_w1(c):
+        def load_w1(a, c):
             c0, c1 = PIECES[c]
-            for a in range(2):
-                nc.sync.dma_start(out=raw[a, c][:],
-                                  in_=w1[KP * a:KP * (a + 1), c0:c1].rearrange("(p j) c -> p j c", j=PACK))
+            nc.sync.dma_start(out=raw[a, c][:],
+                              in_=w1[PASS * a:PASS * (a + 1), c0:c1].rearrange("(p j) c -> p j c", j=PACK))
 
         def load_words(a):
-            nc.sync.dma_start(out=tabw[a][:], in_=tab_words[a].rearrange("p t i -> p (t i)").bitcast(I32))
-
-        def load_scales():
-            for q in range(4):
-                nc.sync.dma_start(out=tabs[32 * q:32 * q + 8, :].bitcast(I32),
-                                  in_=tab_scales[:, 4 * q:4 * q + 4, :].bitcast(I32))
+            nc.sync.dma_start(out=table_words[a][:], in_=tab_words[a].rearrange("p t i -> p (t i)").bitcast(I32))
 
         nc.sync.dma_start(offs_t[:], offs)
         nc.sync.dma_start(pos2_t[:], pos2)
-        nc.sync.dma_start(pos1_t[:], pos1)
-        load_scales()
-        load_words(0)
-        load_w1(0)
-        load_words(1)
-        load_w1(1)
-        load_w1(2)
-        for a in range(2):
-            for c in (3, 4):
-                nc.sync.dma_start(out=raw[a, c][:],
-                                  in_=w1[KP * a:KP * (a + 1), PIECES[c][0]:PIECES[c][1]].rearrange("(p j) c -> p j c", j=PACK))
-        with nc.allow_non_contiguous_dma(reason="one gain to a partition"):
-            nc.sync.dma_start(out=gains[0][:], in_=gain[0:KP].rearrange("(i p) -> p i", p=P))
-        nc.sync.dma_start(out=gains[1][:], in_=gain[KP:2 * KP].rearrange("(p t) -> p t", t=PACK))
-        nc.sync.dma_start(out=w2w[:].bitcast(I32), in_=w2_words.rearrange("a p b -> p a b").bitcast(I32))
         for q in range(4):
-            nc.sync.dma_start(out=w2s[32 * q:32 * q + 4, :, :].bitcast(I32),
+            nc.sync.dma_start(out=table_scales[32 * q:32 * q + 4 * PASSES, :].bitcast(I32),
+                              in_=tab_scales[:, 4 * q:4 * q + 4, :].bitcast(I32))
+        load_words(0)
+        load_w1(0, 0)
+        load_w1(1, 0)
+        load_words(1)
+        load_w1(0, 1)
+        load_w1(1, 1)
+        nc.sync.dma_start(pos1_t[:], pos1)
+        load_w1(0, 2)
+        load_w1(1, 2)
+        for a in range(PASSES):
+            load_w1(a, 3)
+            load_w1(a, 4)
+        with nc.allow_non_contiguous_dma(reason="one gain to a partition"):
+            nc.sync.dma_start(out=gains[0][:], in_=gain[0:PASS].rearrange("(i p) -> p i", p=P))
+        nc.sync.dma_start(out=gains[1][:], in_=gain[PASS:H].rearrange("(p t) -> p t", t=PACK))
+        nc.sync.dma_start(out=w2_codes[:].bitcast(I32), in_=w2_words.rearrange("a p b -> p a b").bitcast(I32))
+        for q in range(4):
+            nc.sync.dma_start(out=w2_bytes[32 * q:32 * q + 4, :, :].bitcast(I32),
                               in_=w2_scales[:, 4 * q:4 * q + 4, :].rearrange("a r n -> r a n").bitcast(I32))
         nc.sync.dma_start(pos4_t[:], pos4)
         nc.sync.dma_start(pos3_t[:], pos3)
 
-        def cast_w1(a, c, on_vector=False):
+        def cast_w1(a, c, copy):
             c0, c1 = PIECES[c]
-            if c1 <= KP:
-                dst = wb[0, a][:, PACK * c0:PACK * c1].rearrange("p (m i j) -> p m j i", i=4, j=PACK)
+            if c1 <= PASS:
+                size = PACK * (c1 - c0)
+                dst = w1_woven[c][:, size * a:size * (a + 1)].rearrange("p (m i j) -> p m j i", i=RUN, j=PACK)
             else:
-                m0, m1 = (c0 - KP) // PACK, (c1 - KP) // PACK
-                dst = wb[1, a][:].rearrange("p (t m j) -> p m j t", t=PACK, j=PACK)[:, m0:m1, :, :]
-            src = raw[a, c][:].rearrange("p j (m t) -> p m j t", t=PACK)
-            if on_vector:
-                nc.vector.tensor_copy(out=dst, in_=src)
-            else:
-                nc.scalar.copy(out=dst, in_=src)
+                m0, m1 = (c0 - PASS) // PACK, (c1 - PASS) // PACK
+                dst = w1_woven[3 + a][:].rearrange("p (t m j) -> p m j t", t=PACK, j=PACK)[:, m0:m1, :, :]
+            copy(out=dst, in_=raw[a, c][:].rearrange("p j (m i) -> p m j i", i=RUN))
 
-        def quant_w1(g, a, c0, c1):
-            nc.vector.quantize_mx(out=wq[g, a][:, c0:c1].bitcast(FP8X4), scales=ws[g, a][:, c0:c1],
-                                  in_=wb[g, a][:, PACK * c0:PACK * c1])
+        def quantise_w1(u):
+            nc.vector.quantize_mx(out=w1_words[u][:].bitcast(FP8X4), scales=w1_scales[u][:], in_=w1_woven[u][:])
 
-        def product(i, cuts=(0, BANK, S)):
-            g, t = divmod(i, PACK)
+        def stationary(i, a):
+            if i < 2:
+                return i, P * a
+            if i < PACK:
+                return 2, 2 * P * a + P * (i - 2)
+            return 3 + a, P * (i - PACK)
+
+        def first_product(i, cuts=(0, BANK, S)):
             for c0, c1 in zip(cuts, cuts[1:]):
-                bank = psum.tile([P, BANK], F32, name="hbank", tag="hbank", bufs=4)
-                cols = slice(c0, c1)
-                for a in range(2):
-                    nc.tensor.matmul_mx(out=bank[:, 0:c1 - c0], lhsT=wq[g, a][:, P * t:P * (t + 1)].bitcast(FP8X4),
-                                        lhsT_scale=ws[g, a][:, P * t:P * (t + 1)],
-                                        rhs=vw[a][:, cols].bitcast(FP8X4), rhs_scale=vs[4 * a:P, cols],
-                                        start=(a == 0), stop=(a == 1))
-                nc.scalar.copy(out=h[i][:, cols], in_=bank[:, 0:c1 - c0])
+                bank = psum.tile([P, BANK], F32, name="h_bank", tag="h_bank", bufs=4)
+                for a in range(PASSES):
+                    u, m0 = stationary(i, a)
+                    nc.tensor.matmul_mx(out=bank[:, 0:c1 - c0], lhsT=w1_words[u][:, m0:m0 + P].bitcast(FP8X4),
+                                        lhsT_scale=w1_scales[u][:, m0:m0 + P],
+                                        rhs=v_words[a][:, c0:c1].bitcast(FP8X4), rhs_scale=v_scales[4 * a:P, c0:c1],
+                                        start=(a == 0), stop=(a == PASSES - 1))
+                nc.scalar.copy(out=h[i][:, c0:c1], in_=bank[:, 0:c1 - c0])
 
-        def picks(i, cuts=(0, HALF, P1)):
-            if i in GP_SUB:
-                left = left1[GP_SUB[i % 2]]
-                nc.vector.tensor_copy(out=right1[i], in_=h[i][:].indirect(pos2_t[:]))
-                nc.vector.tensor_copy(out=left[:], in_=h[i][:].indirect(pos1_t[:]))
-                nc.gpsimd.tensor_tensor(diff[i], left[:], right1[i], ALU.subtract)
-                return
-            for u in range(2):
-                nc.vector.tensor_copy(out=right1[i][:, HALF * u:HALF * (u + 1)],
-                                      in_=h[i][:].indirect(pos2_t[:, 16 * u:16 * (u + 1)]))
-            for c0, c1 in zip(cuts, cuts[1:]):
-                nc.vector.tensor_tensor(diff[i][:, c0:c1], h[i][:].indirect(pos1_t[:, c0 // 16:c1 // 16]),
-                                        right1[i][:, c0:c1], ALU.subtract)
+        def compare(i):
+            for c0 in (0, HALF):
+                nc.vector.tensor_copy(out=second[i][:, c0:c0 + HALF],
+                                      in_=h[i][:].indirect(pos2_t[:, c0 // LANES:(c0 + HALF) // LANES]))
+            for c0 in (0, HALF):
+                nc.vector.tensor_tensor(diff[i][:, c0:c0 + HALF],
+                                        h[i][:].indirect(pos1_t[:, c0 // LANES:(c0 + HALF) // LANES]),
+                                        second[i][:, c0:c0 + HALF], ALU.subtract)
 
-        def squash(i, c0=0, c1=P1):
-            g, t = divmod(i, PACK)
-            nc.scalar.activation(out=th[i][:, 0:c1 - c0], in_=diff[i][:, c0:c1], func=ACT.Tanh)
-            dst = zn[t][:, c0:c1] if g == 0 else zb[g][:, t, c0:c1]
-            if i in GP_GAIN:
-                nc.gpsimd.tensor_scalar(dst, th[i][:, 0:c1 - c0], gains[g][:, t:t + 1], 0.0, ALU.mult, ALU.add)
-            else:
-                nc.scalar.activation(out=dst, in_=th[i][:, 0:c1 - c0], func=ACT.Copy, scale=gains[g][:, t:t + 1])
-            if g == 0:
-                for r in range(PACK):
-                    nc.sync.dma_start(out=zb[0][32 * t:32 * (t + 1), r, :], in_=zn[t][r:P:PACK, :])
+        def make_z(i):
+            a, t = divmod(i, PACK)
+            nc.scalar.activation(out=bounded[i], in_=diff[i], func=ACT.Tanh)
+            dst = z_rows[t][:] if a == 0 else z_planes[a][:, t, :]
+            nc.scalar.activation(out=dst, in_=bounded[i], func=ACT.Copy, scale=gains[a][:, t:t + 1])
+            if a == 0:
+                for plane in range(PACK):
+                    nc.sync.dma_start(out=z_planes[0][32 * i:32 * (i + 1), plane, :], in_=z_rows[i][plane:P:PACK, :])
 
-        def weave(g, c0, c1, on_vector=True):
-            dst = zi[g][:, PACK * c0:PACK * c1].rearrange("p (c i t) -> p c t i", i=4, t=PACK)
-            src = zb[g][:, :, c0:c1].rearrange("p t (c i) -> p c t i", i=4)
-            if on_vector:
-                nc.vector.tensor_copy(out=dst, in_=src)
-            else:
-                nc.scalar.copy(out=dst, in_=src)
+        def weave_z(a, planes, copy):
+            copy(out=z_woven[a][:].rearrange("p (c i t) -> p c t i", i=RUN, t=PACK)[:, :, 0:planes, :],
+                 in_=z_planes[a][:, 0:planes, :].rearrange("p t (c i) -> p c t i", i=RUN))
 
-        def quant_z(g, c0, c1):
-            nc.vector.quantize_mx(out=zq[g][:, c0:c1].bitcast(FP8X4), scales=zs[g][:, c0:c1],
-                                  in_=zi[g][:, PACK * c0:PACK * c1])
+        def quantise_z(a, c0, c1):
+            nc.vector.quantize_mx(out=z_words[a][:, c0:c1].bitcast(FP8X4), scales=z_scales[a][:, c0:c1],
+                                  in_=z_woven[a][:, PACK * c0:PACK * c1])
 
-        def second_product(n, g, c0, c1, start, stop):
-            nc.tensor.matmul_mx(out=ybank[n][:, c0:c1], lhsT=w2w[:, g, 2 * P * n:2 * P * (n + 1)].bitcast(FP4X4),
-                                lhsT_scale=w2s[:, g, P * n:P * (n + 1)],
-                                rhs=zq[g][:, c0:c1].bitcast(FP8X4), rhs_scale=zs[g][:, c0:c1],
+        def second_product(n, a, c0, c1, start, stop):
+            nc.tensor.matmul_mx(out=y_bank[n][:, c0:c1], lhsT=w2_codes[:, a, 2 * P * n:2 * P * (n + 1)].bitcast(FP4X4),
+                                lhsT_scale=w2_bytes[:, a, P * n:P * (n + 1)],
+                                rhs=z_words[a][:, c0:c1].bitcast(FP8X4), rhs_scale=z_scales[a][:, c0:c1],
                                 start=start, stop=stop)
 
         def pick_words(a, c0, c1):
-            nc.vector.tensor_copy(out=vw[a][:, c0:c1],
-                                  in_=tabw[a][:].bitcast(U32).indirect(offs_t[:, c0 // 16:c1 // 16]))
+            nc.vector.tensor_copy(out=v_words[a][:, c0:c1],
+                                  in_=table_words[a][:].bitcast(U32).indirect(offs_t[:, c0 // LANES:c1 // LANES]))
 
-        def pick_scales():
-            nc.vector.tensor_copy(out=vs[:], in_=tabs[:].indirect(offs_t[:]))
-
-        pick_scales()
+        nc.vector.tensor_copy(out=v_scales[:], in_=table_scales[:].indirect(offs_t[:]))
         pick_words(0, 0, S)
-        cast_w1(0, 0)
-        cast_w1(1, 0)
-        quant_w1(0, 0, 0, P)
-        quant_w1(0, 1, 0, P)
-        pick_words(1, 0, BANK)
-        pick_words(1, BANK, 768)
-        pick_words(1, 768, S)
-        product(0, (0, BANK, 768, S))
-        cast_w1(0, 1, True)
-        cast_w1(1, 1, True)
-        quant_w1(0, 0, P, HALF)
-        quant_w1(0, 1, P, HALF)
-        picks(0)
-        cast_w1(0, 2)
-        cast_w1(1, 2)
-        quant_w1(0, 0, HALF, KP)
-        quant_w1(0, 1, HALF, KP)
-        h[1] = tile([P, S], F32, "h1", "raw12")
-        product(1)
-        picks(1)
-        cast_w1(0, 3)
-        cast_w1(0, 4)
-        quant_w1(1, 0, 0, KP)
-        h[2] = tile([P, S], F32, "h2", "raw04")
-        product(2)
-        picks(2)
-        cast_w1(1, 3)
-        cast_w1(1, 4)
-        quant_w1(1, 1, 0, KP)
-        h[3] = tile([P, S], F32, "h3", "raw14")
-        product(3)
-        picks(3)
-        squash(0)
-        squash(1)
-        product(4)
-        picks(4)
-        product(5)
-        picks(5)
-        squash(2)
-        squash(3)
-        product(6)
-        picks(6)
-        squash(4)
-        product(7)
-        weave(0, 0, P1, False)
-        quant_z(0, 0, P1)
-        for n in range(4):
+        for a in range(PASSES):
+            cast_w1(a, 0, nc.scalar.copy)
+        quantise_w1(0)
+        for c0, c1 in zip(FIRST_CUTS, FIRST_CUTS[1:]):
+            pick_words(1, c0, c1)
+
+        for a in range(PASSES):
+            cast_w1(a, 1, nc.scalar.copy)
+        h[0] = tile([P, S], F32, "h0", "raw11")
+        first_product(0, FIRST_CUTS)
+        quantise_w1(1)
+        for a in range(PASSES):
+            cast_w1(a, 2, nc.vector.tensor_copy)
+        quantise_w1(2)
+        compare(0)
+        h[1] = tile([P, S], F32, "h1")
+        first_product(1)
+        compare(1)
+
+        for a in range(PASSES):
+            cast_w1(a, 3, nc.scalar.copy)
+            cast_w1(a, 4, nc.scalar.copy)
+            quantise_w1(3 + a)
+        h[2] = tile([P, S], F32, "h2", "raw14")
+        first_product(2)
+        compare(2)
+        h[3] = tile([P, S], F32, "h3")
+        first_product(3)
+        compare(3)
+
+        make_z(0)
+        make_z(1)
+        for i in (4, 5):
+            first_product(i)
+            compare(i)
+        make_z(2)
+        make_z(3)
+        first_product(6)
+        compare(6)
+        make_z(4)
+        first_product(LAST)
+        weave_z(0, PACK, nc.scalar.copy)
+        quantise_z(0, 0, P1)
+        for n in range(N // P):
             second_product(n, 0, 0, P1, True, False)
-        squash(5)
-        squash(6)
-        picks(7)
-        squash(7, 0, HALF)
-        squash(7, HALF, P1)
-        weave(1, 0, HALF)
-        quant_z(1, 0, HALF)
-        for n in range(4):
-            for c in range(2):
-                second_product(n, 1, P * c, P * (c + 1), False, False)
-        weave(1, HALF, P1)
-        quant_z(1, HALF, P1)
-        for n in range(4):
-            for c in range(2, 4):
-                second_product(n, 1, P * c, P * (c + 1), False, c == 3)
+        make_z(5)
+        make_z(6)
 
-        def finish(n):
-            nc.scalar.activation(out=plus1[n][:], in_=right2[n][:], func=ACT.Copy, bias=1.0)
-            nc.vector.tensor_tensor(res[n][:], y[n][:].indirect(pos3_t[:]), plus1[n][:], ALU.mult)
-            nc.sync.dma_start(out=out[P * n:P * (n + 1), :], in_=res[n][:])
+        compare(LAST)
+        for c0 in (0, HALF):
+            nc.scalar.activation(out=bounded[LAST][:, c0:c0 + HALF], in_=diff[LAST][:, c0:c0 + HALF], func=ACT.Tanh)
+        weave_z(1, PACK - 1, nc.vector.tensor_copy)
+        last_plane = z_woven[1][:].rearrange("p (m t) -> p m t", t=PACK)[:, :, PACK - 1]
+        for c0 in (0, HALF):
+            nc.vector.tensor_scalar(last_plane[:, c0:c0 + HALF], bounded[LAST][:, c0:c0 + HALF],
+                                    gains[1][:, PACK - 1:PACK], None, ALU.mult)
+        for c0 in (0, HALF):
+            quantise_z(1, c0, c0 + HALF)
+        for n in range(N // P):
+            for c0 in range(0, P1, P):
+                second_product(n, 1, c0, c0 + P, False, c0 + P == P1)
 
-        for n in range(4):
-            nc.scalar.copy(out=y[n][:], in_=ybank[n][:])
-            nc.vector.tensor_copy(out=right2[n][:], in_=y[n][:].indirect(pos4_t[:]))
-            if n > 0:
-                finish(n - 1)
-        finish(3)
+        for n in range(N // P):
+            nc.scalar.copy(out=y[n][:], in_=y_bank[n][:])
+            nc.vector.tensor_copy(out=right[n][:], in_=y[n][:].indirect(pos4_t[:]))
+        for n in range(N // P):
+            nc.scalar.activation(out=one_plus[n][:], in_=right[n][:], func=ACT.Copy, bias=1.0)
+            nc.vector.tensor_tensor(result[n][:], y[n][:].indirect(pos3_t[:]), one_plus[n][:], ALU.mult)
+            nc.sync.dma_start(out=out[P * n:P * (n + 1), :], in_=result[n][:])

@@ -26,8 +26,12 @@ RUN = 4
 HALF = P1 // 2
 TILES = H // P
 LAST = TILES - 1
+GAIN_G = (0, 1, 2, 4, 5)
+GAIN_V = ()
+SHARE = 32
 PIECES = [(0, 128), (128, 256), (256, 512), (512, 768), (768, 1024)]
 FIRST_CUTS = (0, 512, 768, 1024)
+LAST_CUTS = (0, 256, 384, 512)
 
 
 def tile_list_peer_grading_kernel(tc, tab_words, tab_scales, offs, w1, pos1, pos2, gain,
@@ -35,6 +39,7 @@ def tile_list_peer_grading_kernel(tc, tab_words, tab_scales, offs, w1, pos1, pos
     nc = tc.nc
     with ExitStack() as ctx:
         keep = ctx.enter_context(tc.tile_pool(name="keep", bufs=1))
+        placed = ctx.enter_context(tc.tile_pool(name="placed", bufs=1))
         psum = ctx.enter_context(tc.psum_pool(name="psum", bufs=1))
 
         def tile(shape, dtype, name, tag=None):
@@ -50,30 +55,30 @@ def tile_list_peer_grading_kernel(tc, tab_words, tab_scales, offs, w1, pos1, pos
         v_words = [tile([P, S], U32, "v_words%d" % a) for a in range(PASSES)]
         v_scales = tile([P, S], U8, "v_scales")
         raw = {(a, c): tile([P, PACK, c1 - c0], F32, "raw%d%d" % (a, c))
-               for a in range(PASSES) for c, (c0, c1) in enumerate(PIECES)}
+               for a in range(PASSES) for c, (c0, c1) in enumerate(PIECES) if (a, c) != (0, 2)}
+        raw[0, 2] = placed.tile([P, PACK, 2 * P], F32, name="raw02", offset=0, align_bytes=64)
         widths = [2 * P, 2 * P, PASS, PASS, PASS]
-        w1_woven = [tile([P, PACK * w], BF16, "w1_woven%d" % u) for u, w in enumerate(widths)]
+        w1_woven = [tile([P, PACK * w], BF16, "w1_woven%d" % u) for u, w in enumerate(widths[:4])]
         w1_words = [tile([P, w], U32, "w1_words%d" % u) for u, w in enumerate(widths)]
         w1_scales = [tile([P, w], U8, "w1_scales%d" % u) for u, w in enumerate(widths)]
         gains = [tile([P, PACK], F32, "gain%d" % a) for a in range(PASSES)]
         w2_codes = tile([P, PASSES, 2 * N], U8, "w2_codes")
         w2_bytes = tile([P, PASSES, N], U8, "w2_bytes")
         h = {i: tile([P, S], F32, "h%d" % i) for i in range(PACK, TILES)}
-        z_rows = [tile([P, P1], BF16, "z_rows%d" % i) for i in range(PACK)]
-        z_planes = [tile([P, PACK, P1], BF16, "z_planes%d" % a) for a in range(PASSES)]
+        z_rows = {}
+        wide = tile([P, PACK + 1, P1], BF16, "wide")
+        z_planes = [tile([P, PACK, P1], BF16, "z_planes0")[:], wide[:, 1:, :]]
         z_woven = [tile([P, P1 * PACK], BF16, "z_woven%d" % a) for a in range(PASSES)]
 
-        spent = raw[1, 2][:].rearrange("p j c -> p (j c)")
-        second = [spent[:, P1 * i:P1 * (i + 1)] for i in range(2)]
-        second += [tile([P, P1], F32, "second%d" % i)[:] for i in range(2, TILES)]
-        diff = [tile([P, P1], F32, "diff%d" % i)[:] for i in range(LAST)]
-        diff += [z_woven[0][:].bitcast(F32)[:, 0:P1]]
+        second = [tile([P, P1], F32, "second%d" % i)[:] if i in (2, 3, 4, 7) else None for i in range(TILES)]
+        second[5] = wide[:].rearrange("p t c -> p (t c)").bitcast(F32)[:, 0:P1]
+        second[6] = wide[:].rearrange("p t c -> p (t c)").bitcast(F32)[:, P1:2 * P1]
+        diff = [tile([P, P1], F32, "diff%d" % i)[:] for i in range(TILES)]
         spent = raw[1, 3][:].rearrange("p j c -> p (j c)")
-        bounded = [spent[:, P1 * i:P1 * (i + 1)] for i in range(2)]
-        bounded += [tile([P, P1], F32, "bounded%d" % i)[:] for i in range(2, 5)]
-        spent = z_planes[0][:].rearrange("p t c -> p (t c)").bitcast(F32)
+        bounded = [raw[0, 4][:].rearrange("p j c -> p (j c)")[:, 0:P1]]
         bounded += [spent[:, P1 * i:P1 * (i + 1)] for i in range(2)]
-        bounded += [tile([P, P1], F32, "bounded%d" % LAST)[:]]
+        bounded += [tile([P, P1], F32, "bounded%d" % i)[:] for i in range(3, 6)]
+        bounded += [diff[5], diff[6]]
 
         z_words = [tile([P, P1], U32, "z_words%d" % a) for a in range(PASSES)]
         z_scales = [tile([P, P1], U8, "z_scales%d" % a) for a in range(PASSES)]
@@ -83,8 +88,8 @@ def tile_list_peer_grading_kernel(tc, tab_words, tab_scales, offs, w1, pos1, pos
         result = [tile([P, P2], F32, "result%d" % n) for n in range(N // P)]
         y_bank = [psum.tile([P, BANK], F32, name="y_bank%d" % n) for n in range(N // P)]
 
-        nc.gpsimd.memset(table_scales[:].bitcast(I32), 0)
-        nc.gpsimd.memset(w2_bytes[:].rearrange("p a n -> p (a n)").bitcast(I32), 0)
+        nc.vector.memset(table_scales[:].bitcast(I32), 0)
+        nc.vector.memset(w2_bytes[:].rearrange("p a n -> p (a n)").bitcast(I32), 0)
 
         def load_w1(a, c):
             c0, c1 = PIECES[c]
@@ -108,12 +113,12 @@ def tile_list_peer_grading_kernel(tc, tab_words, tab_scales, offs, w1, pos1, pos
         nc.sync.dma_start(pos1_t[:], pos1)
         load_w1(0, 2)
         load_w1(1, 2)
-        for a in range(PASSES):
-            load_w1(a, 3)
-            load_w1(a, 4)
         with nc.allow_non_contiguous_dma(reason="one gain to a partition"):
             nc.sync.dma_start(out=gains[0][:], in_=gain[0:PASS].rearrange("(i p) -> p i", p=P))
         nc.sync.dma_start(out=gains[1][:], in_=gain[PASS:H].rearrange("(p t) -> p t", t=PACK))
+        for a in range(PASSES):
+            load_w1(a, 3)
+            load_w1(a, 4)
         nc.sync.dma_start(out=w2_codes[:].bitcast(I32), in_=w2_words.rearrange("a p b -> p a b").bitcast(I32))
         for q in range(4):
             nc.sync.dma_start(out=w2_bytes[32 * q:32 * q + 4, :, :].bitcast(I32),
@@ -152,34 +157,43 @@ def tile_list_peer_grading_kernel(tc, tab_words, tab_scales, offs, w1, pos1, pos
                                         start=(a == 0), stop=(a == PASSES - 1))
                 nc.scalar.copy(out=h[i][:, c0:c1], in_=bank[:, 0:c1 - c0])
 
-        def compare(i):
+        def compare(i, cuts=(0, HALF, P1)):
             for c0 in (0, HALF):
                 nc.vector.tensor_copy(out=second[i][:, c0:c0 + HALF],
                                       in_=h[i][:].indirect(pos2_t[:, c0 // LANES:(c0 + HALF) // LANES]))
-            for c0 in (0, HALF):
-                nc.vector.tensor_tensor(diff[i][:, c0:c0 + HALF],
-                                        h[i][:].indirect(pos1_t[:, c0 // LANES:(c0 + HALF) // LANES]),
-                                        second[i][:, c0:c0 + HALF], ALU.subtract)
+            for c0, c1 in zip(cuts, cuts[1:]):
+                nc.vector.tensor_tensor(diff[i][:, c0:c1], h[i][:].indirect(pos1_t[:, c0 // LANES:c1 // LANES]),
+                                        second[i][:, c0:c1], ALU.subtract)
 
-        def make_z(i):
-            a, t = divmod(i, PACK)
+        def bound(i):
             nc.scalar.activation(out=bounded[i], in_=diff[i], func=ACT.Tanh)
-            dst = z_rows[t][:] if a == 0 else z_planes[a][:, t, :]
-            nc.scalar.activation(out=dst, in_=bounded[i], func=ACT.Copy, scale=gains[a][:, t:t + 1])
+
+        def weigh(i):
+            a, t = divmod(i, PACK)
+            if a == 0:
+                z_rows[i] = (second[i + 1] if i < 3 else bounded[5]).bitcast(BF16)[:, 0:P1]
+            dst = z_rows[t] if a == 0 else z_planes[a][:, t, :]
+            if i in GAIN_G:
+                nc.gpsimd.tensor_scalar(dst, bounded[i], gains[a][:, t:t + 1], 0.0, ALU.mult, ALU.add)
+            elif i in GAIN_V:
+                nc.vector.tensor_scalar(dst, bounded[i], gains[a][:, t:t + 1], None, ALU.mult)
+            else:
+                nc.scalar.activation(out=dst, in_=bounded[i], func=ACT.Copy, scale=gains[a][:, t:t + 1])
             if a == 0:
                 for plane in range(PACK):
                     nc.sync.dma_start(out=z_planes[0][32 * i:32 * (i + 1), plane, :], in_=z_rows[i][plane:P:PACK, :])
 
-        def weave_z(a, planes, copy):
-            copy(out=z_woven[a][:].rearrange("p (c i t) -> p c t i", i=RUN, t=PACK)[:, :, 0:planes, :],
-                 in_=z_planes[a][:, 0:planes, :].rearrange("p t (c i) -> p c t i", i=RUN))
+        def weave_z(a, c0, c1, copy):
+            copy(out=z_woven[a][:, PACK * c0:PACK * c1].rearrange("p (c i t) -> p c t i", i=RUN, t=PACK),
+                 in_=z_planes[a][:, :, c0:c1].rearrange("p t (c i) -> p c t i", i=RUN))
 
         def quantise_z(a, c0, c1):
             nc.vector.quantize_mx(out=z_words[a][:, c0:c1].bitcast(FP8X4), scales=z_scales[a][:, c0:c1],
                                   in_=z_woven[a][:, PACK * c0:PACK * c1])
 
         def second_product(n, a, c0, c1, start, stop):
-            nc.tensor.matmul_mx(out=y_bank[n][:, c0:c1], lhsT=w2_codes[:, a, 2 * P * n:2 * P * (n + 1)].bitcast(FP4X4),
+            bank = y_end if (n, c1 - c0, c1) == (0, P, P1) else y_bank[n]
+            nc.tensor.matmul_mx(out=bank[:, c0:c1], lhsT=w2_codes[:, a, 2 * P * n:2 * P * (n + 1)].bitcast(FP4X4),
                                 lhsT_scale=w2_bytes[:, a, P * n:P * (n + 1)],
                                 rhs=z_words[a][:, c0:c1].bitcast(FP8X4), rhs_scale=z_scales[a][:, c0:c1],
                                 start=start, stop=stop)
@@ -201,59 +215,93 @@ def tile_list_peer_grading_kernel(tc, tab_words, tab_scales, offs, w1, pos1, pos
         h[0] = tile([P, S], F32, "h0", "raw11")
         first_product(0, FIRST_CUTS)
         quantise_w1(1)
-        for a in range(PASSES):
-            cast_w1(a, 2, nc.vector.tensor_copy)
-        quantise_w1(2)
+        nc.vector.tensor_copy(out=w1_woven[2][:, 0:2 * PASS].rearrange("p (m j) -> p m j", j=PACK),
+                              in_=raw[0, 2][:].rearrange("p j m -> p m j"))
+        late = placed.tile([P, 2 * PASS], BF16, name="late", offset=0, align_bytes=64)
+        nc.gpsimd.tensor_scalar(late[:].rearrange("p (m j) -> p m j", j=PACK),
+                                raw[1, 2][:].rearrange("p j m -> p m j"), 1.0, 0.0, ALU.mult, ALU.add)
+        second[0] = placed.tile([P, P1], F32, name="second0", offset=2048, align_bytes=64)[:]
         compare(0)
+        nc.vector.quantize_mx(out=w1_words[2][:, 0:2 * P].bitcast(FP8X4), scales=w1_scales[2][:, 0:2 * P],
+                              in_=w1_woven[2][:, 0:2 * PASS])
+        nc.vector.quantize_mx(out=w1_words[2][:, 2 * P:PASS].bitcast(FP8X4), scales=w1_scales[2][:, 2 * P:PASS],
+                              in_=late[:])
+        second[1] = late[:].bitcast(F32)
+        w1_woven.append(placed.tile([P, PACK * PASS], BF16, name="w1_woven4", offset=2048, align_bytes=64))
+        nc.gpsimd.tensor_scalar(w1_woven[4][:].rearrange("p (t m j) -> p t m j", t=PACK, j=PACK)[:, :, 0:SHARE, :],
+                                raw[1, 3][:].rearrange("p j (m t) -> p t m j", t=PACK)[:, :, 0:SHARE, :],
+                                1.0, 0.0, ALU.mult, ALU.add)
         h[1] = tile([P, S], F32, "h1")
         first_product(1)
         compare(1)
 
-        for a in range(PASSES):
-            cast_w1(a, 3, nc.scalar.copy)
-            cast_w1(a, 4, nc.scalar.copy)
-            quantise_w1(3 + a)
-        h[2] = tile([P, S], F32, "h2", "raw14")
+        cast_w1(0, 3, nc.scalar.copy)
+        cast_w1(0, 4, nc.scalar.copy)
+        bound(0)
+        weigh(0)
+        h[2] = tile([P, S], F32, "h2", "raw03")
         first_product(2)
+        quantise_w1(3)
         compare(2)
-        h[3] = tile([P, S], F32, "h3")
+        nc.scalar.copy(out=w1_woven[4][:].rearrange("p (t m j) -> p m j t", t=PACK, j=PACK)[:, SHARE:64, :, :],
+                       in_=raw[1, 3][:].rearrange("p j (m i) -> p m j i", i=RUN)[:, SHARE:64, :, :])
+        cast_w1(1, 4, nc.scalar.copy)
+        quantise_w1(4)
+        bound(1)
+        weigh(1)
+        h[3] = tile([P, S], F32, "h3", "raw14")
         first_product(3)
         compare(3)
-
-        make_z(0)
-        make_z(1)
-        for i in (4, 5):
-            first_product(i)
-            compare(i)
-        make_z(2)
-        make_z(3)
+        bound(2)
+        weigh(2)
+        first_product(4)
+        compare(4)
+        bound(3)
+        weigh(3)
+        first_product(5)
+        compare(5)
         first_product(6)
+        bound(4)
+        weigh(4)
         compare(6)
-        make_z(4)
         first_product(LAST)
-        weave_z(0, PACK, nc.scalar.copy)
+        weave_z(0, 0, HALF, nc.scalar.copy)
+        bound(5)
+        weigh(5)
+        weave_z(0, HALF, P1, nc.scalar.copy)
         quantise_z(0, 0, P1)
-        for n in range(N // P):
+        y_end = psum.tile([P, BANK], F32, name="h_bank", tag="h_bank", bufs=4)
+        for c0 in range(0, P1, P):
+            second_product(0, 0, c0, c0 + P, c0 in (0, P1 - P), False)
+        for n in (1, 2):
             second_product(n, 0, 0, P1, True, False)
-        make_z(5)
-        make_z(6)
+        bound(6)
+        weigh(6)
 
-        compare(LAST)
-        for c0 in (0, HALF):
-            nc.scalar.activation(out=bounded[LAST][:, c0:c0 + HALF], in_=diff[LAST][:, c0:c0 + HALF], func=ACT.Tanh)
-        weave_z(1, PACK - 1, nc.vector.tensor_copy)
-        last_plane = z_woven[1][:].rearrange("p (m t) -> p m t", t=PACK)[:, :, PACK - 1]
-        for c0 in (0, HALF):
-            nc.vector.tensor_scalar(last_plane[:, c0:c0 + HALF], bounded[LAST][:, c0:c0 + HALF],
-                                    gains[1][:, PACK - 1:PACK], None, ALU.mult)
-        for c0 in (0, HALF):
-            quantise_z(1, c0, c0 + HALF)
-        for n in range(N // P):
-            for c0 in range(0, P1, P):
-                second_product(n, 1, c0, c0 + P, False, c0 + P == P1)
+        compare(LAST, LAST_CUTS)
+        for c0, c1 in zip(LAST_CUTS, LAST_CUTS[1:]):
+            b0 = c0 % (HALF + P)
+            nc.scalar.activation(out=bounded[LAST][:, b0:b0 + c1 - c0], in_=diff[LAST][:, c0:c1], func=ACT.Tanh)
+            nc.scalar.activation(out=z_planes[1][:, PACK - 1, c0:c1], in_=bounded[LAST][:, b0:b0 + c1 - c0],
+                                 func=ACT.Copy, scale=gains[1][:, PACK - 1:PACK])
+        weave_z(1, 0, HALF, nc.vector.tensor_copy)
+        weave_z(1, HALF, HALF + P, nc.vector.tensor_copy)
+        weave_z(1, HALF + P, P1, nc.scalar.copy)
+        for c0, c1 in zip(LAST_CUTS, LAST_CUTS[1:]):
+            quantise_z(1, c0, c1)
+        for c0 in range(0, P1, P):
+            second_product(0, 1, c0, c0 + P, False, c0 + 2 * P >= P1)
+            second_product(1, 1, c0, c0 + P, False, c0 + P == P1)
+        second_product(2, 1, 0, P1, False, True)
+        second_product(3, 1, 0, P1, True, False)
+        second_product(3, 0, 0, P1, False, True)
 
         for n in range(N // P):
-            nc.scalar.copy(out=y[n][:], in_=y_bank[n][:])
+            if n == 0:
+                nc.scalar.copy(out=y[n][:, 0:P1 - P], in_=y_bank[n][:, 0:P1 - P])
+                nc.scalar.copy(out=y[n][:, P1 - P:P1], in_=y_end[:, P1 - P:P1])
+            else:
+                nc.scalar.copy(out=y[n][:], in_=y_bank[n][:])
             nc.vector.tensor_copy(out=right[n][:], in_=y[n][:].indirect(pos4_t[:]))
         for n in range(N // P):
             nc.scalar.activation(out=one_plus[n][:], in_=right[n][:], func=ACT.Copy, bias=1.0)

@@ -26,9 +26,8 @@ RUN = 4
 HALF = P1 // 2
 TILES = H // P
 LAST = TILES - 1
-GAIN_G = (0, 1, 2, 4, 5)
+GAIN_G = (0, 1, 4, 5)
 GAIN_V = ()
-SHARE = 32
 PIECES = [(0, 128), (128, 256), (256, 512), (512, 768), (768, 1024)]
 FIRST_CUTS = (0, 512, 768, 1024)
 LAST_CUTS = (0, 256, 384, 512)
@@ -39,7 +38,6 @@ def tile_list_peer_grading_kernel(tc, tab_words, tab_scales, offs, w1, pos1, pos
     nc = tc.nc
     with ExitStack() as ctx:
         keep = ctx.enter_context(tc.tile_pool(name="keep", bufs=1))
-        placed = ctx.enter_context(tc.tile_pool(name="placed", bufs=1))
         psum = ctx.enter_context(tc.psum_pool(name="psum", bufs=1))
 
         def tile(shape, dtype, name, tag=None):
@@ -55,10 +53,9 @@ def tile_list_peer_grading_kernel(tc, tab_words, tab_scales, offs, w1, pos1, pos
         v_words = [tile([P, S], U32, "v_words%d" % a) for a in range(PASSES)]
         v_scales = tile([P, S], U8, "v_scales")
         raw = {(a, c): tile([P, PACK, c1 - c0], F32, "raw%d%d" % (a, c))
-               for a in range(PASSES) for c, (c0, c1) in enumerate(PIECES) if (a, c) != (0, 2)}
-        raw[0, 2] = placed.tile([P, PACK, 2 * P], F32, name="raw02", offset=0, align_bytes=64)
+               for a in range(PASSES) for c, (c0, c1) in enumerate(PIECES)}
         widths = [2 * P, 2 * P, PASS, PASS, PASS]
-        w1_woven = [tile([P, PACK * w], BF16, "w1_woven%d" % u) for u, w in enumerate(widths[:4])]
+        w1_woven = [tile([P, PACK * w], BF16, "w1_woven%d" % u) for u, w in enumerate(widths)]
         w1_words = [tile([P, w], U32, "w1_words%d" % u) for u, w in enumerate(widths)]
         w1_scales = [tile([P, w], U8, "w1_scales%d" % u) for u, w in enumerate(widths)]
         gains = [tile([P, PACK], F32, "gain%d" % a) for a in range(PASSES)]
@@ -71,13 +68,14 @@ def tile_list_peer_grading_kernel(tc, tab_words, tab_scales, offs, w1, pos1, pos
         z_woven = [tile([P, P1 * PACK], BF16, "z_woven%d" % a) for a in range(PASSES)]
 
         second = [tile([P, P1], F32, "second%d" % i)[:] if i in (2, 3, 4, 7) else None for i in range(TILES)]
+        second[0] = raw[1, 2][:].rearrange("p j c -> p (j c)")[:, 0:P1]
+        second[1] = raw[1, 2][:].rearrange("p j c -> p (j c)")[:, P1:2 * P1]
         second[5] = wide[:].rearrange("p t c -> p (t c)").bitcast(F32)[:, 0:P1]
         second[6] = wide[:].rearrange("p t c -> p (t c)").bitcast(F32)[:, P1:2 * P1]
         diff = [tile([P, P1], F32, "diff%d" % i)[:] for i in range(TILES)]
         spent = raw[1, 3][:].rearrange("p j c -> p (j c)")
-        bounded = [raw[0, 4][:].rearrange("p j c -> p (j c)")[:, 0:P1]]
-        bounded += [spent[:, P1 * i:P1 * (i + 1)] for i in range(2)]
-        bounded += [tile([P, P1], F32, "bounded%d" % i)[:] for i in range(3, 6)]
+        bounded = [spent[:, P1 * i:P1 * (i + 1)] for i in range(2)]
+        bounded += [tile([P, P1], F32, "bounded%d" % i)[:] for i in range(2, 6)]
         bounded += [diff[5], diff[6]]
 
         z_words = [tile([P, P1], U32, "z_words%d" % a) for a in range(PASSES)]
@@ -113,12 +111,12 @@ def tile_list_peer_grading_kernel(tc, tab_words, tab_scales, offs, w1, pos1, pos
         nc.sync.dma_start(pos1_t[:], pos1)
         load_w1(0, 2)
         load_w1(1, 2)
-        with nc.allow_non_contiguous_dma(reason="one gain to a partition"):
-            nc.sync.dma_start(out=gains[0][:], in_=gain[0:PASS].rearrange("(i p) -> p i", p=P))
-        nc.sync.dma_start(out=gains[1][:], in_=gain[PASS:H].rearrange("(p t) -> p t", t=PACK))
         for a in range(PASSES):
             load_w1(a, 3)
             load_w1(a, 4)
+        with nc.allow_non_contiguous_dma(reason="one gain to a partition"):
+            nc.sync.dma_start(out=gains[0][:], in_=gain[0:PASS].rearrange("(i p) -> p i", p=P))
+        nc.sync.dma_start(out=gains[1][:], in_=gain[PASS:H].rearrange("(p t) -> p t", t=PACK))
         nc.sync.dma_start(out=w2_codes[:].bitcast(I32), in_=w2_words.rearrange("a p b -> p a b").bitcast(I32))
         for q in range(4):
             nc.sync.dma_start(out=w2_bytes[32 * q:32 * q + 4, :, :].bitcast(I32),
@@ -171,7 +169,7 @@ def tile_list_peer_grading_kernel(tc, tab_words, tab_scales, offs, w1, pos1, pos
         def weigh(i):
             a, t = divmod(i, PACK)
             if a == 0:
-                z_rows[i] = (second[i + 1] if i < 3 else bounded[5]).bitcast(BF16)[:, 0:P1]
+                z_rows[i] = [second[2], second[3], diff[0], bounded[5]][i].bitcast(BF16)[:, 0:P1]
             dst = z_rows[t] if a == 0 else z_planes[a][:, t, :]
             if i in GAIN_G:
                 nc.gpsimd.tensor_scalar(dst, bounded[i], gains[a][:, t:t + 1], 0.0, ALU.mult, ALU.add)
@@ -215,56 +213,39 @@ def tile_list_peer_grading_kernel(tc, tab_words, tab_scales, offs, w1, pos1, pos
         h[0] = tile([P, S], F32, "h0", "raw11")
         first_product(0, FIRST_CUTS)
         quantise_w1(1)
-        nc.vector.tensor_copy(out=w1_woven[2][:, 0:2 * PASS].rearrange("p (m j) -> p m j", j=PACK),
-                              in_=raw[0, 2][:].rearrange("p j m -> p m j"))
-        late = placed.tile([P, 2 * PASS], BF16, name="late", offset=0, align_bytes=64)
-        nc.gpsimd.tensor_scalar(late[:].rearrange("p (m j) -> p m j", j=PACK),
-                                raw[1, 2][:].rearrange("p j m -> p m j"), 1.0, 0.0, ALU.mult, ALU.add)
-        second[0] = placed.tile([P, P1], F32, name="second0", offset=2048, align_bytes=64)[:]
+        for a in range(PASSES):
+            nc.vector.tensor_copy(out=w1_woven[2][:, 2 * PASS * a:2 * PASS * (a + 1)].rearrange("p (m j) -> p m j", j=PACK),
+                                  in_=raw[a, 2][:].rearrange("p j m -> p m j"))
+        quantise_w1(2)
         compare(0)
-        nc.vector.quantize_mx(out=w1_words[2][:, 0:2 * P].bitcast(FP8X4), scales=w1_scales[2][:, 0:2 * P],
-                              in_=w1_woven[2][:, 0:2 * PASS])
-        nc.vector.quantize_mx(out=w1_words[2][:, 2 * P:PASS].bitcast(FP8X4), scales=w1_scales[2][:, 2 * P:PASS],
-                              in_=late[:])
-        second[1] = late[:].bitcast(F32)
-        w1_woven.append(placed.tile([P, PACK * PASS], BF16, name="w1_woven4", offset=2048, align_bytes=64))
-        nc.gpsimd.tensor_scalar(w1_woven[4][:].rearrange("p (t m j) -> p t m j", t=PACK, j=PACK)[:, :, 0:SHARE, :],
-                                raw[1, 3][:].rearrange("p j (m t) -> p t m j", t=PACK)[:, :, 0:SHARE, :],
-                                1.0, 0.0, ALU.mult, ALU.add)
         h[1] = tile([P, S], F32, "h1")
         first_product(1)
         compare(1)
-
-        cast_w1(0, 3, nc.scalar.copy)
-        cast_w1(0, 4, nc.scalar.copy)
-        bound(0)
-        weigh(0)
-        h[2] = tile([P, S], F32, "h2", "raw03")
+        for a in range(PASSES):
+            cast_w1(a, 3, nc.scalar.copy)
+            cast_w1(a, 4, nc.scalar.copy)
+            quantise_w1(3 + a)
+        h[2] = tile([P, S], F32, "h2", "raw14")
         first_product(2)
-        quantise_w1(3)
         compare(2)
-        nc.scalar.copy(out=w1_woven[4][:].rearrange("p (t m j) -> p m j t", t=PACK, j=PACK)[:, SHARE:64, :, :],
-                       in_=raw[1, 3][:].rearrange("p j (m i) -> p m j i", i=RUN)[:, SHARE:64, :, :])
-        cast_w1(1, 4, nc.scalar.copy)
-        quantise_w1(4)
-        bound(1)
-        weigh(1)
-        h[3] = tile([P, S], F32, "h3", "raw14")
+        h[3] = tile([P, S], F32, "h3")
         first_product(3)
         compare(3)
-        bound(2)
-        weigh(2)
-        first_product(4)
-        compare(4)
-        bound(3)
-        weigh(3)
-        first_product(5)
-        compare(5)
+        for i in (0, 1):
+            bound(i)
+            weigh(i)
+        for i in (4, 5):
+            first_product(i)
+            compare(i)
+        for i in (2, 3):
+            bound(i)
+        for i in (2, 3):
+            weigh(i)
         first_product(6)
-        bound(4)
-        weigh(4)
         compare(6)
         first_product(LAST)
+        bound(4)
+        weigh(4)
         weave_z(0, 0, HALF, nc.scalar.copy)
         bound(5)
         weigh(5)

@@ -26,7 +26,7 @@ RUN = 4
 HALF = P1 // 2
 TILES = H // P
 LAST = TILES - 1
-GAIN_G = (0, 1, 4, 5)
+GAIN_G = (0, 1, 2, 4, 5)
 GAIN_V = ()
 PIECES = [(0, 128), (128, 256), (256, 512), (512, 768), (768, 1024)]
 FIRST_CUTS = (0, 512, 768, 1024)
@@ -38,6 +38,7 @@ def tile_list_peer_grading_kernel(tc, tab_words, tab_scales, offs, w1, pos1, pos
     nc = tc.nc
     with ExitStack() as ctx:
         keep = ctx.enter_context(tc.tile_pool(name="keep", bufs=1))
+        placed = ctx.enter_context(tc.tile_pool(name="placed", bufs=1))
         psum = ctx.enter_context(tc.psum_pool(name="psum", bufs=1))
 
         def tile(shape, dtype, name, tag=None):
@@ -53,7 +54,9 @@ def tile_list_peer_grading_kernel(tc, tab_words, tab_scales, offs, w1, pos1, pos
         v_words = [tile([P, S], U32, "v_words%d" % a) for a in range(PASSES)]
         v_scales = tile([P, S], U8, "v_scales")
         raw = {(a, c): tile([P, PACK, c1 - c0], F32, "raw%d%d" % (a, c))
-               for a in range(PASSES) for c, (c0, c1) in enumerate(PIECES)}
+               for a in range(PASSES) for c, (c0, c1) in enumerate(PIECES) if c != 4}
+        raw[0, 4] = placed.tile([P, PACK, 2 * P], F32, name="raw04", offset=8192 + 2048, align_bytes=64)
+        raw[1, 4] = placed.tile([P, PACK, 2 * P], F32, name="raw14", offset=4032, align_bytes=64)
         widths = [2 * P, 2 * P, PASS, PASS, PASS]
         w1_woven = [tile([P, PACK * w], BF16, "w1_woven%d" % u) for u, w in enumerate(widths)]
         w1_words = [tile([P, w], U32, "w1_words%d" % u) for u, w in enumerate(widths)]
@@ -73,9 +76,8 @@ def tile_list_peer_grading_kernel(tc, tab_words, tab_scales, offs, w1, pos1, pos
         second[5] = wide[:].rearrange("p t c -> p (t c)").bitcast(F32)[:, 0:P1]
         second[6] = wide[:].rearrange("p t c -> p (t c)").bitcast(F32)[:, P1:2 * P1]
         diff = [tile([P, P1], F32, "diff%d" % i)[:] for i in range(TILES)]
-        spent = raw[1, 3][:].rearrange("p j c -> p (j c)")
-        bounded = [spent[:, P1 * i:P1 * (i + 1)] for i in range(2)]
-        bounded += [tile([P, P1], F32, "bounded%d" % i)[:] for i in range(2, 6)]
+        bounded = [None, None, None]
+        bounded += [tile([P, P1], F32, "bounded%d" % i)[:] for i in range(3, 6)]
         bounded += [diff[5], diff[6]]
 
         z_words = [tile([P, P1], U32, "z_words%d" % a) for a in range(PASSES)]
@@ -169,7 +171,7 @@ def tile_list_peer_grading_kernel(tc, tab_words, tab_scales, offs, w1, pos1, pos
         def weigh(i):
             a, t = divmod(i, PACK)
             if a == 0:
-                z_rows[i] = [second[2], second[3], diff[0], bounded[5]][i].bitcast(BF16)[:, 0:P1]
+                z_rows[i] = [second[1], second[2], second[3], bounded[5]][i].bitcast(BF16)[:, 0:P1]
             dst = z_rows[t] if a == 0 else z_planes[a][:, t, :]
             if i in GAIN_G:
                 nc.gpsimd.tensor_scalar(dst, bounded[i], gains[a][:, t:t + 1], 0.0, ALU.mult, ALU.add)
@@ -221,31 +223,37 @@ def tile_list_peer_grading_kernel(tc, tab_words, tab_scales, offs, w1, pos1, pos
         h[1] = tile([P, S], F32, "h1")
         first_product(1)
         compare(1)
-        for a in range(PASSES):
-            cast_w1(a, 3, nc.scalar.copy)
-            cast_w1(a, 4, nc.scalar.copy)
-            quantise_w1(3 + a)
-        h[2] = tile([P, S], F32, "h2", "raw14")
+        cast_w1(0, 3, nc.scalar.copy)
+        cast_w1(0, 4, nc.scalar.copy)
+        quantise_w1(3)
+        h[2] = placed.tile([P, S], F32, name="h2", offset=8192, align_bytes=64)
+        bounded[0] = placed.tile([P, P1], F32, name="bounded0", offset=8192 + 4096, align_bytes=64)[:]
         first_product(2)
+        bound(0)
+        weigh(0)
         compare(2)
-        h[3] = tile([P, S], F32, "h3")
+        cast_w1(1, 3, nc.scalar.copy)
+        cast_w1(1, 4, nc.scalar.copy)
+        quantise_w1(4)
+        h[3] = placed.tile([P, S], F32, name="h3", offset=0, align_bytes=64)
+        for i in (1, 2):
+            bounded[i] = placed.tile([P, P1], F32, name="bounded%d" % i, offset=2048 + 2048 * i, align_bytes=64)[:]
         first_product(3)
         compare(3)
-        for i in (0, 1):
+        for i in (1, 2):
             bound(i)
             weigh(i)
-        for i in (4, 5):
-            first_product(i)
-            compare(i)
-        for i in (2, 3):
-            bound(i)
-        for i in (2, 3):
-            weigh(i)
+        first_product(4)
+        compare(4)
+        bound(3)
+        first_product(5)
+        weigh(3)
+        compare(5)
         first_product(6)
         compare(6)
-        first_product(LAST)
         bound(4)
         weigh(4)
+        first_product(LAST)
         weave_z(0, 0, HALF, nc.scalar.copy)
         bound(5)
         weigh(5)

@@ -26,11 +26,17 @@ RUN = 4
 HALF = P1 // 2
 TILES = H // P
 LAST = TILES - 1
-GAIN_G = (0, 1, 2, 4, 5)
-GAIN_V = ()
+GPSIMD_GAINS = (0, 1, 4, 5)
 PIECES = [(0, 128), (128, 256), (256, 512), (512, 768), (768, 1024)]
 FIRST_CUTS = (0, 512, 768, 1024)
 LAST_CUTS = (0, 256, 384, 512)
+TAIL = P1 - P
+ROW_BYTES = 4 * S
+TANH_BYTES = 4 * P1
+H3_AT = 0
+H2_AT = H3_AT + ROW_BYTES + 2 * TANH_BYTES
+RAW14_AT = H3_AT + ROW_BYTES - 64
+RAW04_AT = H2_AT + TANH_BYTES
 
 
 def tile_list_peer_grading_kernel(tc, tab_words, tab_scales, offs, w1, pos1, pos2, gain,
@@ -55,8 +61,8 @@ def tile_list_peer_grading_kernel(tc, tab_words, tab_scales, offs, w1, pos1, pos
         v_scales = tile([P, S], U8, "v_scales")
         raw = {(a, c): tile([P, PACK, c1 - c0], F32, "raw%d%d" % (a, c))
                for a in range(PASSES) for c, (c0, c1) in enumerate(PIECES) if c != 4}
-        raw[0, 4] = placed.tile([P, PACK, 2 * P], F32, name="raw04", offset=8192 + 2048, align_bytes=64)
-        raw[1, 4] = placed.tile([P, PACK, 2 * P], F32, name="raw14", offset=4032, align_bytes=64)
+        raw[0, 4] = placed.tile([P, PACK, 2 * P], F32, name="raw04", offset=RAW04_AT, align_bytes=64)
+        raw[1, 4] = placed.tile([P, PACK, 2 * P], F32, name="raw14", offset=RAW14_AT, align_bytes=64)
         widths = [2 * P, 2 * P, PASS, PASS, PASS]
         w1_woven = [tile([P, PACK * w], BF16, "w1_woven%d" % u) for u, w in enumerate(widths)]
         w1_words = [tile([P, w], U32, "w1_words%d" % u) for u, w in enumerate(widths)]
@@ -65,20 +71,23 @@ def tile_list_peer_grading_kernel(tc, tab_words, tab_scales, offs, w1, pos1, pos
         w2_codes = tile([P, PASSES, 2 * N], U8, "w2_codes")
         w2_bytes = tile([P, PASSES, N], U8, "w2_bytes")
         h = {i: tile([P, S], F32, "h%d" % i) for i in range(PACK, TILES)}
-        z_rows = {}
-        wide = tile([P, PACK + 1, P1], BF16, "wide")
-        z_planes = [tile([P, PACK, P1], BF16, "z_planes0")[:], wide[:, 1:, :]]
+        slots = tile([P, PACK + 1, P1], BF16, "slots")
+        z_planes = [tile([P, PACK, P1], BF16, "z_planes0")[:], slots[:, 0:PACK, :]]
         z_woven = [tile([P, P1 * PACK], BF16, "z_woven%d" % a) for a in range(PASSES)]
 
-        second = [tile([P, P1], F32, "second%d" % i)[:] if i in (2, 3, 4, 7) else None for i in range(TILES)]
-        second[0] = raw[1, 2][:].rearrange("p j c -> p (j c)")[:, 0:P1]
-        second[1] = raw[1, 2][:].rearrange("p j c -> p (j c)")[:, P1:2 * P1]
-        second[5] = wide[:].rearrange("p t c -> p (t c)").bitcast(F32)[:, 0:P1]
-        second[6] = wide[:].rearrange("p t c -> p (t c)").bitcast(F32)[:, P1:2 * P1]
+        spent = raw[1, 2][:].rearrange("p j c -> p (j c)")
+        second = {i: [spent[:, P1 * i:P1 * i + HALF], spent[:, P1 * i + HALF:P1 * (i + 1)]] for i in (0, 1)}
+        for i in (2, 3, 4, LAST):
+            picks = tile([P, P1], F32, "second%d" % i)
+            second[i] = [picks[:, 0:HALF], picks[:, HALF:P1]]
+        second[5] = [slots[:, 0, :].bitcast(F32), slots[:, PACK, :].bitcast(F32)]
+        second[6] = [slots[:, 1, :].bitcast(F32), slots[:, 2, :].bitcast(F32)]
         diff = [tile([P, P1], F32, "diff%d" % i)[:] for i in range(TILES)]
-        bounded = [None, None, None]
-        bounded += [tile([P, P1], F32, "bounded%d" % i)[:] for i in range(3, 6)]
-        bounded += [diff[5], diff[6]]
+        bounded = {i: tile([P, P1], F32, "bounded%d" % i)[:] for i in (3, 4, 5)}
+        bounded[6] = diff[5]
+        bounded[LAST] = diff[6]
+        z_rows = [rows.bitcast(BF16)
+                  for rows in (second[2][1], second[3][0], diff[0][:, 0:HALF], bounded[5][:, 0:HALF])]
 
         z_words = [tile([P, P1], U32, "z_words%d" % a) for a in range(PASSES)]
         z_scales = [tile([P, P1], U8, "z_scales%d" % a) for a in range(PASSES)]
@@ -159,24 +168,21 @@ def tile_list_peer_grading_kernel(tc, tab_words, tab_scales, offs, w1, pos1, pos
 
         def compare(i, cuts=(0, HALF, P1)):
             for c0 in (0, HALF):
-                nc.vector.tensor_copy(out=second[i][:, c0:c0 + HALF],
+                nc.vector.tensor_copy(out=second[i][c0 // HALF],
                                       in_=h[i][:].indirect(pos2_t[:, c0 // LANES:(c0 + HALF) // LANES]))
             for c0, c1 in zip(cuts, cuts[1:]):
+                other = second[i][c0 // HALF][:, c0 % HALF:c0 % HALF + c1 - c0]
                 nc.vector.tensor_tensor(diff[i][:, c0:c1], h[i][:].indirect(pos1_t[:, c0 // LANES:c1 // LANES]),
-                                        second[i][:, c0:c1], ALU.subtract)
+                                        other, ALU.subtract)
 
         def bound(i):
             nc.scalar.activation(out=bounded[i], in_=diff[i], func=ACT.Tanh)
 
         def weigh(i):
             a, t = divmod(i, PACK)
-            if a == 0:
-                z_rows[i] = [second[1], second[2], second[3], bounded[5]][i].bitcast(BF16)[:, 0:P1]
             dst = z_rows[t] if a == 0 else z_planes[a][:, t, :]
-            if i in GAIN_G:
+            if i in GPSIMD_GAINS:
                 nc.gpsimd.tensor_scalar(dst, bounded[i], gains[a][:, t:t + 1], 0.0, ALU.mult, ALU.add)
-            elif i in GAIN_V:
-                nc.vector.tensor_scalar(dst, bounded[i], gains[a][:, t:t + 1], None, ALU.mult)
             else:
                 nc.scalar.activation(out=dst, in_=bounded[i], func=ACT.Copy, scale=gains[a][:, t:t + 1])
             if a == 0:
@@ -192,7 +198,7 @@ def tile_list_peer_grading_kernel(tc, tab_words, tab_scales, offs, w1, pos1, pos
                                   in_=z_woven[a][:, PACK * c0:PACK * c1])
 
         def second_product(n, a, c0, c1, start, stop):
-            bank = y_end if (n, c1 - c0, c1) == (0, P, P1) else y_bank[n]
+            bank = y_end if (n, c0) == (0, TAIL) else y_bank[n]
             nc.tensor.matmul_mx(out=bank[:, c0:c1], lhsT=w2_codes[:, a, 2 * P * n:2 * P * (n + 1)].bitcast(FP4X4),
                                 lhsT_scale=w2_bytes[:, a, P * n:P * (n + 1)],
                                 rhs=z_words[a][:, c0:c1].bitcast(FP8X4), rhs_scale=z_scales[a][:, c0:c1],
@@ -216,34 +222,38 @@ def tile_list_peer_grading_kernel(tc, tab_words, tab_scales, offs, w1, pos1, pos
         first_product(0, FIRST_CUTS)
         quantise_w1(1)
         for a in range(PASSES):
-            nc.vector.tensor_copy(out=w1_woven[2][:, 2 * PASS * a:2 * PASS * (a + 1)].rearrange("p (m j) -> p m j", j=PACK),
-                                  in_=raw[a, 2][:].rearrange("p j m -> p m j"))
+            woven = w1_woven[2][:, 2 * PASS * a:2 * PASS * (a + 1)].rearrange("p (m j) -> p m j", j=PACK)
+            nc.vector.tensor_copy(out=woven, in_=raw[a, 2][:].rearrange("p j m -> p m j"))
         quantise_w1(2)
         compare(0)
         h[1] = tile([P, S], F32, "h1")
         first_product(1)
         compare(1)
+
         cast_w1(0, 3, nc.scalar.copy)
         cast_w1(0, 4, nc.scalar.copy)
         quantise_w1(3)
-        h[2] = placed.tile([P, S], F32, name="h2", offset=8192, align_bytes=64)
-        bounded[0] = placed.tile([P, P1], F32, name="bounded0", offset=8192 + 4096, align_bytes=64)[:]
+        h[2] = placed.tile([P, S], F32, name="h2", offset=H2_AT, align_bytes=64)
+        bounded[0] = placed.tile([P, P1], F32, name="bounded0", offset=H2_AT + ROW_BYTES, align_bytes=64)[:]
         first_product(2)
         bound(0)
-        weigh(0)
         compare(2)
+        weigh(0)
         cast_w1(1, 3, nc.scalar.copy)
         cast_w1(1, 4, nc.scalar.copy)
         quantise_w1(4)
-        h[3] = placed.tile([P, S], F32, name="h3", offset=0, align_bytes=64)
+        h[3] = placed.tile([P, S], F32, name="h3", offset=H3_AT, align_bytes=64)
         for i in (1, 2):
-            bounded[i] = placed.tile([P, P1], F32, name="bounded%d" % i, offset=2048 + 2048 * i, align_bytes=64)[:]
+            bounded[i] = placed.tile([P, P1], F32, name="bounded%d" % i,
+                                     offset=H3_AT + ROW_BYTES + TANH_BYTES * (i - 1), align_bytes=64)[:]
         first_product(3)
         compare(3)
-        for i in (1, 2):
-            bound(i)
-            weigh(i)
+
+        bound(1)
+        weigh(1)
+        bound(2)
         first_product(4)
+        weigh(2)
         compare(4)
         bound(3)
         first_product(5)
@@ -254,6 +264,7 @@ def tile_list_peer_grading_kernel(tc, tab_words, tab_scales, offs, w1, pos1, pos
         bound(4)
         weigh(4)
         first_product(LAST)
+
         weave_z(0, 0, HALF, nc.scalar.copy)
         bound(5)
         weigh(5)
@@ -261,7 +272,7 @@ def tile_list_peer_grading_kernel(tc, tab_words, tab_scales, offs, w1, pos1, pos
         quantise_z(0, 0, P1)
         y_end = psum.tile([P, BANK], F32, name="h_bank", tag="h_bank", bufs=4)
         for c0 in range(0, P1, P):
-            second_product(0, 0, c0, c0 + P, c0 in (0, P1 - P), False)
+            second_product(0, 0, c0, c0 + P, c0 in (0, TAIL), False)
         for n in (1, 2):
             second_product(n, 0, 0, P1, True, False)
         bound(6)
@@ -269,26 +280,26 @@ def tile_list_peer_grading_kernel(tc, tab_words, tab_scales, offs, w1, pos1, pos
 
         compare(LAST, LAST_CUTS)
         for c0, c1 in zip(LAST_CUTS, LAST_CUTS[1:]):
-            b0 = c0 % (HALF + P)
+            b0 = c0 % TAIL
             nc.scalar.activation(out=bounded[LAST][:, b0:b0 + c1 - c0], in_=diff[LAST][:, c0:c1], func=ACT.Tanh)
             nc.scalar.activation(out=z_planes[1][:, PACK - 1, c0:c1], in_=bounded[LAST][:, b0:b0 + c1 - c0],
                                  func=ACT.Copy, scale=gains[1][:, PACK - 1:PACK])
         weave_z(1, 0, HALF, nc.vector.tensor_copy)
-        weave_z(1, HALF, HALF + P, nc.vector.tensor_copy)
-        weave_z(1, HALF + P, P1, nc.scalar.copy)
+        weave_z(1, HALF, TAIL, nc.vector.tensor_copy)
+        weave_z(1, TAIL, P1, nc.scalar.copy)
         for c0, c1 in zip(LAST_CUTS, LAST_CUTS[1:]):
             quantise_z(1, c0, c1)
         for c0 in range(0, P1, P):
-            second_product(0, 1, c0, c0 + P, False, c0 + 2 * P >= P1)
-            second_product(1, 1, c0, c0 + P, False, c0 + P == P1)
+            second_product(0, 1, c0, c0 + P, False, c0 + P >= TAIL)
+            second_product(1, 1, c0, c0 + P, False, c0 == TAIL)
         second_product(2, 1, 0, P1, False, True)
         second_product(3, 1, 0, P1, True, False)
         second_product(3, 0, 0, P1, False, True)
 
         for n in range(N // P):
             if n == 0:
-                nc.scalar.copy(out=y[n][:, 0:P1 - P], in_=y_bank[n][:, 0:P1 - P])
-                nc.scalar.copy(out=y[n][:, P1 - P:P1], in_=y_end[:, P1 - P:P1])
+                nc.scalar.copy(out=y[n][:, 0:TAIL], in_=y_bank[n][:, 0:TAIL])
+                nc.scalar.copy(out=y[n][:, TAIL:P1], in_=y_end[:, TAIL:P1])
             else:
                 nc.scalar.copy(out=y[n][:], in_=y_bank[n][:])
             nc.vector.tensor_copy(out=right[n][:], in_=y[n][:].indirect(pos4_t[:]))

@@ -26,7 +26,7 @@ RUN = 4
 HALF = P1 // 2
 TILES = H // P
 LAST = TILES - 1
-GPSIMD_GAINS = (0, 1, 4, 5)
+GPSIMD_GAINS = (0, 1, 2, 4, 5)
 PIECES = [(0, 128), (128, 256), (256, 512), (512, 768), (768, 1024)]
 FIRST_CUTS = (0, 512, 768, 1024)
 LAST_CUTS = (0, 256, 384, 512)
@@ -37,6 +37,7 @@ H3_AT = 0
 H2_AT = H3_AT + ROW_BYTES + 2 * TANH_BYTES
 RAW14_AT = H3_AT + ROW_BYTES - 64
 RAW04_AT = H2_AT + TANH_BYTES
+DIFF0_AT = H2_AT + ROW_BYTES + 2 * TANH_BYTES
 
 
 def tile_list_peer_grading_kernel(tc, tab_words, tab_scales, offs, w1, pos1, pos2, gain,
@@ -65,29 +66,42 @@ def tile_list_peer_grading_kernel(tc, tab_words, tab_scales, offs, w1, pos1, pos
         raw[1, 4] = placed.tile([P, PACK, 2 * P], F32, name="raw14", offset=RAW14_AT, align_bytes=64)
         widths = [2 * P, 2 * P, PASS, PASS, PASS]
         w1_woven = [tile([P, PACK * w], BF16, "w1_woven%d" % u) for u, w in enumerate(widths)]
-        w1_words = [tile([P, w], U32, "w1_words%d" % u) for u, w in enumerate(widths)]
+        w1_words = {u: tile([P, w], U32, "w1_words%d" % u) for u, w in enumerate(widths) if u != 3}
         w1_scales = [tile([P, w], U8, "w1_scales%d" % u) for u, w in enumerate(widths)]
         gains = [tile([P, PACK], F32, "gain%d" % a) for a in range(PASSES)]
         w2_codes = tile([P, PASSES, 2 * N], U8, "w2_codes")
         w2_bytes = tile([P, PASSES, N], U8, "w2_bytes")
         h = {i: tile([P, S], F32, "h%d" % i) for i in range(PACK, TILES)}
         slots = tile([P, PACK + 1, P1], BF16, "slots")
-        z_planes = [tile([P, PACK, P1], BF16, "z_planes0")[:], slots[:, 0:PACK, :]]
+        z_planes = [tile([P, PACK, P1], BF16, "z_planes0")[:], slots[:, 1:PACK + 1, :]]
         z_woven = [tile([P, P1 * PACK], BF16, "z_woven%d" % a) for a in range(PASSES)]
 
         spent = raw[1, 2][:].rearrange("p j c -> p (j c)")
-        second = {i: [spent[:, P1 * i:P1 * i + HALF], spent[:, P1 * i + HALF:P1 * (i + 1)]] for i in (0, 1)}
-        for i in (2, 3, 4, LAST):
+        whole = {i: spent[:, P1 * i:P1 * (i + 1)] for i in (0, 1)}
+        second = {}
+        for i in (3,):
             picks = tile([P, P1], F32, "second%d" % i)
             second[i] = [picks[:, 0:HALF], picks[:, HALF:P1]]
-        second[5] = [slots[:, 0, :].bitcast(F32), slots[:, PACK, :].bitcast(F32)]
-        second[6] = [slots[:, 1, :].bitcast(F32), slots[:, 2, :].bitcast(F32)]
-        diff = [tile([P, P1], F32, "diff%d" % i)[:] for i in range(TILES)]
-        bounded = {i: tile([P, P1], F32, "bounded%d" % i)[:] for i in (3, 4, 5)}
-        bounded[6] = diff[5]
-        bounded[LAST] = diff[6]
+        flat = slots[:].rearrange("p s c -> p (s c)")
+        whole[4] = tile([P, P1], F32, "second4")[:]
+        whole[5] = flat[:, P1:3 * P1].bitcast(F32)
+        whole[6] = tile([P, P1], F32, "second6")[:]
+        whole[2] = tile([P, P1], F32, "second2")[:]
+        strip = tile([P, (PACK + 1) * P1], F32, "strip")
+        bounded_late = strip[:, 0:PACK * P1].rearrange("p (t c) -> p t c", t=PACK)
+        second[LAST] = [tile([P, HALF], F32, "second7")[:], strip[:, PACK * P1:PACK * P1 + HALF]]
+        last_front = strip[:, PACK * P1 + HALF:(PACK + 1) * P1]
+        diff = {0: placed.tile([P, P1], F32, name="diff0", offset=DIFF0_AT, align_bytes=64)[:],
+                1: tile([P, P1], F32, "diff1")[:]}
+        diff[5] = bounded_late[:, 2, :]
+        diff[6] = bounded_late[:, 3, :]
+        diff[4] = strip[:, 4 * P1 - P:5 * P1 - P]
+        diff[3] = strip[:, 3 * P1 - 64:4 * P1 - 64]
+        bounded = {3: tile([P, P1], F32, "bounded3")[:]}
+        for t in range(PACK):
+            bounded[PACK + t] = bounded_late[:, t, :]
         z_rows = [rows.bitcast(BF16)
-                  for rows in (second[2][1], second[3][0], diff[0][:, 0:HALF], bounded[5][:, 0:HALF])]
+                  for rows in (whole[2][:, 0:HALF], second[3][0], second[3][1], bounded[5][:, 0:HALF])]
 
         z_words = [tile([P, P1], U32, "z_words%d" % a) for a in range(PASSES)]
         z_scales = [tile([P, P1], U8, "z_scales%d" % a) for a in range(PASSES)]
@@ -175,19 +189,25 @@ def tile_list_peer_grading_kernel(tc, tab_words, tab_scales, offs, w1, pos1, pos
                 nc.vector.tensor_tensor(diff[i][:, c0:c1], h[i][:].indirect(pos1_t[:, c0 // LANES:c1 // LANES]),
                                         other, ALU.subtract)
 
+        def pick(i):
+            nc.vector.tensor_copy(out=whole[i], in_=h[i][:].indirect(pos2_t[:]))
+
+        def subtract(i):
+            nc.vector.tensor_tensor(diff[i], h[i][:].indirect(pos1_t[:]), whole[i], ALU.subtract)
+
         def bound(i):
             nc.scalar.activation(out=bounded[i], in_=diff[i], func=ACT.Tanh)
 
         def weigh(i):
             a, t = divmod(i, PACK)
-            dst = z_rows[t] if a == 0 else z_planes[a][:, t, :]
+            dst = z_rows[t] if a == 0 else z_planes[a][:, t, 0:TAIL]
+            src = bounded[i] if a == 0 else bounded[i][:, 0:TAIL]
             if i in GPSIMD_GAINS:
-                nc.gpsimd.tensor_scalar(dst, bounded[i], gains[a][:, t:t + 1], 0.0, ALU.mult, ALU.add)
+                nc.gpsimd.tensor_scalar(dst, src, gains[a][:, t:t + 1], 0.0, ALU.mult, ALU.add)
             else:
-                nc.scalar.activation(out=dst, in_=bounded[i], func=ACT.Copy, scale=gains[a][:, t:t + 1])
+                nc.scalar.activation(out=dst, in_=src, func=ACT.Copy, scale=gains[a][:, t:t + 1])
             if a == 0:
-                for plane in range(PACK):
-                    nc.sync.dma_start(out=z_planes[0][32 * i:32 * (i + 1), plane, :], in_=z_rows[i][plane:P:PACK, :])
+                nc.sync.dma_start(out=z_planes[0][32 * i:32 * (i + 1), :, :], in_=z_rows[i])
 
         def weave_z(a, c0, c1, copy):
             copy(out=z_woven[a][:, PACK * c0:PACK * c1].rearrange("p (c i t) -> p c t i", i=RUN, t=PACK),
@@ -198,7 +218,7 @@ def tile_list_peer_grading_kernel(tc, tab_words, tab_scales, offs, w1, pos1, pos
                                   in_=z_woven[a][:, PACK * c0:PACK * c1])
 
         def second_product(n, a, c0, c1, start, stop):
-            bank = y_end if (n, c0) == (0, TAIL) else y_bank[n]
+            bank = y_end[n] if n < 2 and c0 == HALF else y_bank[n]
             nc.tensor.matmul_mx(out=bank[:, c0:c1], lhsT=w2_codes[:, a, 2 * P * n:2 * P * (n + 1)].bitcast(FP4X4),
                                 lhsT_scale=w2_bytes[:, a, P * n:P * (n + 1)],
                                 rhs=z_words[a][:, c0:c1].bitcast(FP8X4), rhs_scale=z_scales[a][:, c0:c1],
@@ -225,24 +245,29 @@ def tile_list_peer_grading_kernel(tc, tab_words, tab_scales, offs, w1, pos1, pos
             woven = w1_woven[2][:, 2 * PASS * a:2 * PASS * (a + 1)].rearrange("p (m j) -> p m j", j=PACK)
             nc.vector.tensor_copy(out=woven, in_=raw[a, 2][:].rearrange("p j m -> p m j"))
         quantise_w1(2)
-        compare(0)
+        pick(0)
         h[1] = tile([P, S], F32, "h1")
         first_product(1)
-        compare(1)
+        pick(1)
+        subtract(0)
+        subtract(1)
 
         cast_w1(0, 3, nc.scalar.copy)
         cast_w1(0, 4, nc.scalar.copy)
-        quantise_w1(3)
-        h[2] = placed.tile([P, S], F32, name="h2", offset=H2_AT, align_bytes=64)
+        h[2] = tile([P, S], F32, "h2")
         bounded[0] = placed.tile([P, P1], F32, name="bounded0", offset=H2_AT + ROW_BYTES, align_bytes=64)[:]
         first_product(2)
+        pick(2)
         bound(0)
-        compare(2)
+        w1_words[3] = placed.tile([P, PASS], U32, name="w1_words3", offset=DIFF0_AT + 64 - TANH_BYTES, align_bytes=64)
+        diff[2] = placed.tile([P, P1], F32, name="diff2", offset=DIFF0_AT + 64, align_bytes=64)[:]
+        quantise_w1(3)
+        subtract(2)
         weigh(0)
         cast_w1(1, 3, nc.scalar.copy)
         cast_w1(1, 4, nc.scalar.copy)
         quantise_w1(4)
-        h[3] = placed.tile([P, S], F32, name="h3", offset=H3_AT, align_bytes=64)
+        h[3] = tile([P, S], F32, "h3", "raw13")
         for i in (1, 2):
             bounded[i] = placed.tile([P, P1], F32, name="bounded%d" % i,
                                      offset=H3_AT + ROW_BYTES + TANH_BYTES * (i - 1), align_bytes=64)[:]
@@ -253,53 +278,69 @@ def tile_list_peer_grading_kernel(tc, tab_words, tab_scales, offs, w1, pos1, pos
         weigh(1)
         bound(2)
         first_product(4)
+        pick(4)
         weigh(2)
-        compare(4)
-        bound(3)
         first_product(5)
+        pick(5)
+        bound(3)
         weigh(3)
-        compare(5)
+        subtract(4)
+        subtract(5)
         first_product(6)
-        compare(6)
-        bound(4)
-        weigh(4)
+        pick(6)
         first_product(LAST)
+        nc.vector.tensor_copy(out=second[LAST][0], in_=h[LAST][:].indirect(pos2_t[:, 0:HALF // LANES]))
+        bound(4)
+        subtract(6)
+        weigh(4)
 
-        weave_z(0, 0, HALF, nc.scalar.copy)
         bound(5)
         weigh(5)
-        weave_z(0, HALF, P1, nc.scalar.copy)
-        quantise_z(0, 0, P1)
-        y_end = psum.tile([P, BANK], F32, name="h_bank", tag="h_bank", bufs=4)
-        for c0 in range(0, P1, P):
-            second_product(0, 0, c0, c0 + P, c0 in (0, TAIL), False)
-        for n in (1, 2):
-            second_product(n, 0, 0, P1, True, False)
+        weave_z(0, 0, P1, nc.scalar.copy)
         bound(6)
         weigh(6)
 
-        compare(LAST, LAST_CUTS)
-        for c0, c1 in zip(LAST_CUTS, LAST_CUTS[1:]):
-            b0 = c0 % TAIL
-            nc.scalar.activation(out=bounded[LAST][:, b0:b0 + c1 - c0], in_=diff[LAST][:, c0:c1], func=ACT.Tanh)
-            nc.scalar.activation(out=z_planes[1][:, PACK - 1, c0:c1], in_=bounded[LAST][:, b0:b0 + c1 - c0],
-                                 func=ACT.Copy, scale=gains[1][:, PACK - 1:PACK])
+        nc.vector.tensor_copy(out=second[LAST][1], in_=h[LAST][:].indirect(pos2_t[:, HALF // LANES:P1 // LANES]))
+        nc.vector.tensor_tensor(last_front, h[LAST][:].indirect(pos1_t[:, 0:HALF // LANES]), second[LAST][0], ALU.subtract)
+        quantise_z(0, 0, P1)
+        y_end = [psum.tile([P, BANK], F32, name="h_bank", tag="h_bank", bufs=4) for n in range(2)]
+        for n in range(2):
+            for c0 in range(0, P1, P):
+                second_product(n, 0, c0, c0 + P, c0 in (0, HALF), False)
+        for n in (2, 3):
+            second_product(n, 0, 0, P1, True, False)
+        last_back = tile([P, HALF], F32, "last_back", "z_planes0")[:]
+        for c0 in (HALF, TAIL):
+            nc.vector.tensor_tensor(last_back[:, c0 - HALF:c0 - HALF + P], h[LAST][:].indirect(pos1_t[:, c0 // LANES:(c0 + P) // LANES]),
+                                    second[LAST][1][:, c0 - HALF:c0 - HALF + P], ALU.subtract)
+        nc.scalar.activation(out=bounded[LAST][:, HALF:P1], in_=last_front, func=ACT.Tanh)
+        nc.scalar.activation(out=z_planes[1][:, PACK - 1, 0:HALF], in_=bounded[LAST][:, HALF:P1],
+                             func=ACT.Copy, scale=gains[1][:, PACK - 1:PACK])
+        for c0 in (HALF, TAIL):
+            nc.scalar.activation(out=bounded[LAST][:, c0:c0 + P], in_=last_back[:, c0 - HALF:c0 - HALF + P], func=ACT.Tanh)
+        nc.scalar.activation(out=z_planes[1][:, PACK - 1, HALF:TAIL], in_=bounded[LAST][:, HALF:TAIL],
+                             func=ACT.Copy, scale=gains[1][:, PACK - 1:PACK])
         weave_z(1, 0, HALF, nc.vector.tensor_copy)
-        weave_z(1, HALF, TAIL, nc.vector.tensor_copy)
-        weave_z(1, TAIL, P1, nc.scalar.copy)
-        for c0, c1 in zip(LAST_CUTS, LAST_CUTS[1:]):
-            quantise_z(1, c0, c1)
-        for c0 in range(0, P1, P):
-            second_product(0, 1, c0, c0 + P, False, c0 + P >= TAIL)
-            second_product(1, 1, c0, c0 + P, False, c0 == TAIL)
-        second_product(2, 1, 0, P1, False, True)
-        second_product(3, 1, 0, P1, True, False)
-        second_product(3, 0, 0, P1, False, True)
+        weave_z(1, HALF, TAIL, nc.scalar.copy)
+        nc.vector.tensor_tensor(z_woven[1][:, PACK * TAIL:PACK * P1].rearrange("p (c i t) -> p c t i", i=2, t=PACK),
+                                bounded_late[:, :, TAIL:P1].rearrange("p t (c i) -> p c t i", i=2),
+                                gains[1][:].unsqueeze(1).unsqueeze(3).to_broadcast([P, P // 2, PACK, 2]), ALU.mult)
+        quantise_z(1, 0, HALF)
+        quantise_z(1, TAIL, P1)
+        quantise_z(1, HALF, TAIL)
+        for n in range(2):
+            for c0 in (0, P, TAIL):
+                second_product(n, 1, c0, c0 + P, False, c0 == TAIL)
+        for n in range(2):
+            second_product(n, 1, HALF, TAIL, False, True)
+        for n in (2, 3):
+            second_product(n, 1, 0, P1, False, True)
 
         for n in range(N // P):
-            if n == 0:
-                nc.scalar.copy(out=y[n][:, 0:TAIL], in_=y_bank[n][:, 0:TAIL])
-                nc.scalar.copy(out=y[n][:, TAIL:P1], in_=y_end[:, TAIL:P1])
+            if n < 2:
+                nc.scalar.copy(out=y[n][:, 0:HALF], in_=y_bank[n][:, 0:HALF])
+                nc.scalar.copy(out=y[n][:, TAIL:P1], in_=y_bank[n][:, TAIL:P1])
+                nc.scalar.copy(out=y[n][:, HALF:TAIL], in_=y_end[n][:, HALF:TAIL])
             else:
                 nc.scalar.copy(out=y[n][:], in_=y_bank[n][:])
             nc.vector.tensor_copy(out=right[n][:], in_=y[n][:].indirect(pos4_t[:]))

@@ -33,11 +33,10 @@ LAST_CUTS = (0, 256, 384, 512)
 TAIL = P1 - P
 ROW_BYTES = 4 * S
 TANH_BYTES = 4 * P1
-H3_AT = 0
-H2_AT = H3_AT + ROW_BYTES + 2 * TANH_BYTES
-RAW14_AT = H3_AT + ROW_BYTES - 64
-RAW04_AT = H2_AT + TANH_BYTES
-DIFF0_AT = H2_AT + ROW_BYTES + 2 * TANH_BYTES
+SPAN = 2 * ROW_BYTES + 2 * TANH_BYTES
+RAW_AT = {key: SPAN * u + TANH_BYTES for u, key in enumerate([(1, 3), (1, 4), (0, 3)])}
+RAW11_AT = 3 * SPAN + ROW_BYTES
+HALF_AT = RAW11_AT + 2 * ROW_BYTES + ROW_BYTES
 
 
 def tile_list_peer_grading_kernel(tc, tab_words, tab_scales, offs, w1, pos1, pos2, gain,
@@ -59,13 +58,23 @@ def tile_list_peer_grading_kernel(tc, tab_words, tab_scales, offs, w1, pos1, pos
         table_words = [tile([P, T], I32, "table_words%d" % a) for a in range(PASSES)]
         table_scales = tile([P, T], U8, "table_scales")
         v_words = [tile([P, S], U32, "v_words%d" % a) for a in range(PASSES)]
-        v_scales = tile([P, S], U8, "v_scales")
+        picked_scales = tile([P, S], U8, "picked_scales")
+        v_scales = tile([P, PASSES, S], U8, "v_scales")
         raw = {(a, c): tile([P, PACK, c1 - c0], F32, "raw%d%d" % (a, c))
-               for a in range(PASSES) for c, (c0, c1) in enumerate(PIECES) if c != 4}
-        raw[0, 4] = placed.tile([P, PACK, 2 * P], F32, name="raw04", offset=RAW04_AT, align_bytes=64)
-        raw[1, 4] = placed.tile([P, PACK, 2 * P], F32, name="raw14", offset=RAW14_AT, align_bytes=64)
+               for a in range(PASSES) for c, (c0, c1) in enumerate(PIECES) if (a, c) not in RAW_AT and c != 2 and (a, c) != (1, 1)}
+        raw[1, 1] = placed.tile([P, PACK, P], F32, name="raw11", offset=RAW11_AT, align_bytes=64)
+        around = tile([P, 2 * S - 2 * P], F32, "around")
+        raw[0, 2] = around[:, TAIL:TAIL + S].rearrange("p (j c) -> p j c", j=PACK)
+        halves = [tile([P, PACK, P], F32, "raw120"),
+                  placed.tile([P, PACK, P], F32, name="raw121", offset=HALF_AT, align_bytes=64)]
+        for key in RAW_AT:
+            raw[key] = placed.tile([P, PACK, 2 * P], F32, name="raw%d%d" % key, offset=RAW_AT[key], align_bytes=64)
+
+        def after_cast(key, place, shape, dtype, name):
+            return placed.tile(shape, dtype, name=name, offset=RAW_AT[key] + 64 + TANH_BYTES * (place - 1), align_bytes=64)
+
         widths = [2 * P, 2 * P, PASS, PASS, PASS]
-        w1_woven = [tile([P, PACK * w], BF16, "w1_woven%d" % u) for u, w in enumerate(widths)]
+        w1_woven = {u: tile([P, PACK * w], BF16, "w1_woven%d" % u) for u, w in enumerate(widths) if u != 2}
         w1_words = {u: tile([P, w], U32, "w1_words%d" % u) for u, w in enumerate(widths) if u != 3}
         w1_scales = [tile([P, w], U8, "w1_scales%d" % u) for u, w in enumerate(widths)]
         gains = [tile([P, PACK], F32, "gain%d" % a) for a in range(PASSES)]
@@ -76,8 +85,7 @@ def tile_list_peer_grading_kernel(tc, tab_words, tab_scales, offs, w1, pos1, pos
         z_planes = [tile([P, PACK, P1], BF16, "z_planes0")[:], slots[:, 1:PACK + 1, :]]
         z_woven = [tile([P, P1 * PACK], BF16, "z_woven%d" % a) for a in range(PASSES)]
 
-        spent = raw[1, 2][:].rearrange("p j c -> p (j c)")
-        whole = {i: spent[:, P1 * i:P1 * (i + 1)] for i in (0, 1)}
+        whole = {0: around[:, 0:P1], 1: around[:, 2 * S - 2 * P - P1:2 * S - 2 * P]}
         second = {}
         for i in (3,):
             picks = tile([P, P1], F32, "second%d" % i)
@@ -91,8 +99,7 @@ def tile_list_peer_grading_kernel(tc, tab_words, tab_scales, offs, w1, pos1, pos
         bounded_late = strip[:, 0:PACK * P1].rearrange("p (t c) -> p t c", t=PACK)
         second[LAST] = [tile([P, HALF], F32, "second7")[:], strip[:, PACK * P1:PACK * P1 + HALF]]
         last_front = strip[:, PACK * P1 + HALF:(PACK + 1) * P1]
-        diff = {0: placed.tile([P, P1], F32, name="diff0", offset=DIFF0_AT, align_bytes=64)[:],
-                1: tile([P, P1], F32, "diff1")[:]}
+        diff = {}
         diff[5] = bounded_late[:, 2, :]
         diff[6] = bounded_late[:, 3, :]
         diff[4] = strip[:, 4 * P1 - P:5 * P1 - P]
@@ -101,7 +108,7 @@ def tile_list_peer_grading_kernel(tc, tab_words, tab_scales, offs, w1, pos1, pos
         for t in range(PACK):
             bounded[PACK + t] = bounded_late[:, t, :]
         z_rows = [rows.bitcast(BF16)
-                  for rows in (whole[2][:, 0:HALF], second[3][0], second[3][1], bounded[5][:, 0:HALF])]
+                  for rows in (second[3][0], second[3][1], whole[2][:, 0:HALF], bounded[5][:, 0:HALF])]
 
         z_words = [tile([P, P1], U32, "z_words%d" % a) for a in range(PASSES)]
         z_scales = [tile([P, P1], U8, "z_scales%d" % a) for a in range(PASSES)]
@@ -111,31 +118,37 @@ def tile_list_peer_grading_kernel(tc, tab_words, tab_scales, offs, w1, pos1, pos
         result = [tile([P, P2], F32, "result%d" % n) for n in range(N // P)]
         y_bank = [psum.tile([P, BANK], F32, name="y_bank%d" % n) for n in range(N // P)]
 
-        nc.vector.memset(table_scales[:].bitcast(I32), 0)
+        for p0, p1 in ((32, 64), (64, P)):
+            nc.vector.memset(table_scales[p0:p1, :].bitcast(I32), 0)
+        nc.vector.memset(v_scales[:].rearrange("p a n -> p (a n)").bitcast(I32), 0)
         nc.vector.memset(w2_bytes[:].rearrange("p a n -> p (a n)").bitcast(I32), 0)
 
         def load_w1(a, c):
             c0, c1 = PIECES[c]
-            nc.sync.dma_start(out=raw[a, c][:],
+            nc.sync.dma_start(out=raw[a, c][:, :, :],
                               in_=w1[PASS * a:PASS * (a + 1), c0:c1].rearrange("(p j) c -> p j c", j=PACK))
 
         def load_words(a):
             nc.sync.dma_start(out=table_words[a][:], in_=tab_words[a].rearrange("p t i -> p (t i)").bitcast(I32))
 
         nc.sync.dma_start(offs_t[:], offs)
-        nc.sync.dma_start(pos2_t[:], pos2)
-        for q in range(4):
-            nc.sync.dma_start(out=table_scales[32 * q:32 * q + 4 * PASSES, :].bitcast(I32),
-                              in_=tab_scales[:, 4 * q:4 * q + 4, :].bitcast(I32))
+        for a in range(PASSES):
+            nc.sync.dma_start(out=table_scales[a:32:PASSES, :].bitcast(I32), in_=tab_scales[a].bitcast(I32))
         load_words(0)
         load_w1(0, 0)
         load_w1(1, 0)
         load_words(1)
+        nc.vector.tensor_copy(out=picked_scales[:], in_=table_scales[:].indirect(offs_t[:]))
+        for q in range(4):
+            nc.sync.dma_start(out=v_scales[32 * q:32 * q + 4, :, :].bitcast(I32),
+                              in_=picked_scales[8 * q:8 * q + 8, :].bitcast(I32))
         load_w1(0, 1)
         load_w1(1, 1)
-        nc.sync.dma_start(pos1_t[:], pos1)
+        nc.sync.dma_start(out=halves[0][:], in_=w1[PASS:H, 2 * P:3 * P].rearrange("(p j) c -> p j c", j=PACK))
         load_w1(0, 2)
-        load_w1(1, 2)
+        nc.sync.dma_start(pos2_t[:], pos2)
+        nc.sync.dma_start(pos1_t[:], pos1)
+        nc.sync.dma_start(out=halves[1][:], in_=w1[PASS:H, 3 * P:4 * P].rearrange("(p j) c -> p j c", j=PACK))
         for a in range(PASSES):
             load_w1(a, 3)
             load_w1(a, 4)
@@ -162,11 +175,16 @@ def tile_list_peer_grading_kernel(tc, tab_words, tab_scales, offs, w1, pos1, pos
         def quantise_w1(u):
             nc.vector.quantize_mx(out=w1_words[u][:].bitcast(FP8X4), scales=w1_scales[u][:], in_=w1_woven[u][:])
 
+        def quantise_part(v):
+            nc.vector.quantize_mx(out=w1_words[2][:, 2 * P * v:2 * P * (v + 1)].bitcast(FP8X4),
+                                  scales=w1_scales[2][:, 2 * P * v:2 * P * (v + 1)],
+                                  in_=w1_woven[2][:, 2 * PASS * v:2 * PASS * (v + 1)])
+
         def stationary(i, a):
             if i < 2:
                 return i, P * a
             if i < PACK:
-                return 2, 2 * P * a + P * (i - 2)
+                return 2, P * (1 - a if i == 2 else 2 + a)
             return 3 + a, P * (i - PACK)
 
         def first_product(i, cuts=(0, BANK, S)):
@@ -176,7 +194,7 @@ def tile_list_peer_grading_kernel(tc, tab_words, tab_scales, offs, w1, pos1, pos
                     u, m0 = stationary(i, a)
                     nc.tensor.matmul_mx(out=bank[:, 0:c1 - c0], lhsT=w1_words[u][:, m0:m0 + P].bitcast(FP8X4),
                                         lhsT_scale=w1_scales[u][:, m0:m0 + P],
-                                        rhs=v_words[a][:, c0:c1].bitcast(FP8X4), rhs_scale=v_scales[4 * a:P, c0:c1],
+                                        rhs=v_words[a][:, c0:c1].bitcast(FP8X4), rhs_scale=v_scales[:, a, c0:c1],
                                         start=(a == 0), stop=(a == PASSES - 1))
                 nc.scalar.copy(out=h[i][:, c0:c1], in_=bank[:, 0:c1 - c0])
 
@@ -228,7 +246,6 @@ def tile_list_peer_grading_kernel(tc, tab_words, tab_scales, offs, w1, pos1, pos
             nc.vector.tensor_copy(out=v_words[a][:, c0:c1],
                                   in_=table_words[a][:].bitcast(U32).indirect(offs_t[:, c0 // LANES:c1 // LANES]))
 
-        nc.vector.tensor_copy(out=v_scales[:], in_=table_scales[:].indirect(offs_t[:]))
         pick_words(0, 0, S)
         for a in range(PASSES):
             cast_w1(a, 0, nc.scalar.copy)
@@ -238,50 +255,55 @@ def tile_list_peer_grading_kernel(tc, tab_words, tab_scales, offs, w1, pos1, pos
 
         for a in range(PASSES):
             cast_w1(a, 1, nc.scalar.copy)
-        h[0] = tile([P, S], F32, "h0", "raw11")
+        h[0] = placed.tile([P, S], F32, name="h0", offset=RAW11_AT + 64, align_bytes=64)
+        w1_woven[2] = placed.tile([P, PACK * PASS], BF16, name="w1_woven2", offset=RAW11_AT + 64 - ROW_BYTES, align_bytes=64)
         first_product(0, FIRST_CUTS)
         quantise_w1(1)
-        for a in range(PASSES):
-            woven = w1_woven[2][:, 2 * PASS * a:2 * PASS * (a + 1)].rearrange("p (m j) -> p m j", j=PACK)
-            nc.vector.tensor_copy(out=woven, in_=raw[a, 2][:].rearrange("p j m -> p m j"))
-        quantise_w1(2)
+        for u, src in enumerate((halves[0][:], raw[0, 2][:, :, 0:P], raw[0, 2][:, :, P:2 * P])):
+            nc.vector.tensor_copy(out=w1_woven[2][:, PASS * u:PASS * (u + 1)].rearrange("p (m j) -> p m j", j=PACK),
+                                  in_=src.rearrange("p j m -> p m j"))
+        quantise_part(0)
         pick(0)
         h[1] = tile([P, S], F32, "h1")
         first_product(1)
         pick(1)
+        nc.scalar.copy(out=w1_woven[2][:, PASS * 3:PASS * 4].rearrange("p (m i j) -> p m j i", i=RUN, j=PACK),
+                       in_=halves[1][:].rearrange("p j (m i) -> p m j i", i=RUN))
+        quantise_part(1)
+        first_diffs = placed.tile([P, 2 * P1], F32, name="first_diffs", offset=HALF_AT, align_bytes=64)
+        for i in (0, 1):
+            diff[i] = first_diffs[:, P1 * i:P1 * (i + 1)]
         subtract(0)
         subtract(1)
 
         cast_w1(0, 3, nc.scalar.copy)
         cast_w1(0, 4, nc.scalar.copy)
-        h[2] = tile([P, S], F32, "h2")
-        bounded[0] = placed.tile([P, P1], F32, name="bounded0", offset=H2_AT + ROW_BYTES, align_bytes=64)[:]
+        h[2] = after_cast((0, 3), 1, [P, S], F32, "h2")
         first_product(2)
         pick(2)
-        bound(0)
-        w1_words[3] = placed.tile([P, PASS], U32, name="w1_words3", offset=DIFF0_AT + 64 - TANH_BYTES, align_bytes=64)
-        diff[2] = placed.tile([P, P1], F32, name="diff2", offset=DIFF0_AT + 64, align_bytes=64)[:]
+        cast_w1(1, 3, nc.scalar.copy)
+        w1_words[3] = after_cast((1, 3), 0, [P, PASS], U32, "w1_words3")
+        diff[2] = after_cast((1, 3), 1, [P, P1], F32, "diff2")[:]
+        h[3] = after_cast((1, 3), 2, [P, S], F32, "h3")
         quantise_w1(3)
         subtract(2)
-        weigh(0)
-        cast_w1(1, 3, nc.scalar.copy)
         cast_w1(1, 4, nc.scalar.copy)
         quantise_w1(4)
-        h[3] = tile([P, S], F32, "h3", "raw13")
-        for i in (1, 2):
-            bounded[i] = placed.tile([P, P1], F32, name="bounded%d" % i,
-                                     offset=H3_AT + ROW_BYTES + TANH_BYTES * (i - 1), align_bytes=64)[:]
+        for i in range(3):
+            bounded[i] = after_cast((1, 4), i, [P, P1], F32, "bounded%d" % i)[:]
         first_product(3)
         compare(3)
 
+        bound(0)
+        weigh(0)
         bound(1)
         weigh(1)
-        bound(2)
         first_product(4)
         pick(4)
-        weigh(2)
         first_product(5)
         pick(5)
+        bound(2)
+        weigh(2)
         bound(3)
         weigh(3)
         subtract(4)

@@ -82,7 +82,9 @@ def tile_list_peer_grading_kernel(tc, tab_words, tab_scales, offs, w1, pos1, pos
         w2_bytes = tile([P, PASSES, N], U8, "w2_bytes")
         h = {i: tile([P, S], F32, "h%d" % i) for i in range(PACK, TILES)}
         slots = tile([P, PACK + 1, P1], BF16, "slots")
-        z_planes = [tile([P, PACK, P1], BF16, "z_planes0")[:], slots[:, 1:PACK + 1, :]]
+        z_halves = tile([P, 2, PACK, HALF], BF16, "z_halves")
+        spent = z_halves[:].rearrange("p u t c -> p (u t c)").bitcast(F32)
+        z_planes = [None, slots[:, 1:PACK + 1, :]]
         z_woven = [tile([P, P1 * PACK], BF16, "z_woven%d" % a) for a in range(PASSES)]
 
         whole = {0: around[:, 0:P1], 1: around[:, 2 * S - 2 * P - P1:2 * S - 2 * P]}
@@ -95,10 +97,10 @@ def tile_list_peer_grading_kernel(tc, tab_words, tab_scales, offs, w1, pos1, pos
         whole[5] = flat[:, P1:3 * P1].bitcast(F32)
         whole[6] = tile([P, P1], F32, "second6")[:]
         whole[2] = tile([P, P1], F32, "second2")[:]
-        strip = tile([P, (PACK + 1) * P1], F32, "strip")
+        strip = tile([P, (PACK + 1) * P1 - P], F32, "strip")
         bounded_late = strip[:, 0:PACK * P1].rearrange("p (t c) -> p t c", t=PACK)
-        second[LAST] = [tile([P, HALF], F32, "second7")[:], strip[:, PACK * P1:PACK * P1 + HALF]]
-        last_front = strip[:, PACK * P1 + HALF:(PACK + 1) * P1]
+        second[LAST] = [tile([P, HALF], F32, "second7")[:], spent[:, 0:HALF]]
+        last_front = spent[:, HALF:P1]
         diff = {}
         diff[5] = bounded_late[:, 2, :]
         diff[6] = bounded_late[:, 3, :]
@@ -108,7 +110,7 @@ def tile_list_peer_grading_kernel(tc, tab_words, tab_scales, offs, w1, pos1, pos
         for t in range(PACK):
             bounded[PACK + t] = bounded_late[:, t, :]
         z_rows = [rows.bitcast(BF16)
-                  for rows in (second[3][0], second[3][1], whole[2][:, 0:HALF], bounded[5][:, 0:HALF])]
+                  for rows in (whole[2][:, 0:HALF], second[3][0], second[3][1], bounded[5][:, 0:HALF])]
 
         z_words = [tile([P, P1], U32, "z_words%d" % a) for a in range(PASSES)]
         z_scales = [tile([P, P1], U8, "z_scales%d" % a) for a in range(PASSES)]
@@ -225,11 +227,12 @@ def tile_list_peer_grading_kernel(tc, tab_words, tab_scales, offs, w1, pos1, pos
             else:
                 nc.scalar.activation(out=dst, in_=src, func=ACT.Copy, scale=gains[a][:, t:t + 1])
             if a == 0:
-                nc.sync.dma_start(out=z_planes[0][32 * i:32 * (i + 1), :, :], in_=z_rows[i])
+                for u in range(2):
+                    nc.sync.dma_start(out=z_halves[32 * i:32 * (i + 1), u, :, :], in_=z_rows[i][:, HALF * u:HALF * (u + 1)])
 
         def weave_z(a, c0, c1, copy):
             copy(out=z_woven[a][:, PACK * c0:PACK * c1].rearrange("p (c i t) -> p c t i", i=RUN, t=PACK),
-                 in_=z_planes[a][:, :, c0:c1].rearrange("p t (c i) -> p c t i", i=RUN))
+                 in_=(z_halves[:, c0 // HALF, :, :] if a == 0 else z_planes[a][:, :, c0:c1]).rearrange("p t (c i) -> p c t i", i=RUN))
 
         def quantise_z(a, c0, c1):
             nc.vector.quantize_mx(out=z_words[a][:, c0:c1].bitcast(FP8X4), scales=z_scales[a][:, c0:c1],
@@ -318,24 +321,25 @@ def tile_list_peer_grading_kernel(tc, tab_words, tab_scales, offs, w1, pos1, pos
 
         bound(5)
         weigh(5)
-        weave_z(0, 0, P1, nc.scalar.copy)
+        weave_z(0, 0, HALF, nc.scalar.copy)
+        weave_z(0, HALF, P1, nc.scalar.copy)
         bound(6)
-        weigh(6)
 
-        nc.vector.tensor_copy(out=second[LAST][1], in_=h[LAST][:].indirect(pos2_t[:, HALF // LANES:P1 // LANES]))
+        quantise_z(0, 0, HALF)
         nc.vector.tensor_tensor(last_front, h[LAST][:].indirect(pos1_t[:, 0:HALF // LANES]), second[LAST][0], ALU.subtract)
-        quantise_z(0, 0, P1)
+        nc.vector.tensor_copy(out=second[LAST][1], in_=h[LAST][:].indirect(pos2_t[:, HALF // LANES:P1 // LANES]))
+        quantise_z(0, HALF, P1)
         y_end = [psum.tile([P, BANK], F32, name="h_bank", tag="h_bank", bufs=4) for n in range(2)]
-        for n in range(2):
-            for c0 in range(0, P1, P):
-                second_product(n, 0, c0, c0 + P, c0 in (0, HALF), False)
-        for n in (2, 3):
-            second_product(n, 0, 0, P1, True, False)
-        last_back = tile([P, HALF], F32, "last_back", "z_planes0")[:]
+        for half in (0, HALF):
+            for n in range(N // P):
+                for c0 in (half, half + P):
+                    second_product(n, 0, c0, c0 + P, c0 == 0 or (n < 2 and c0 == HALF), False)
+        last_back = spent[:, P1:P1 + HALF]
         for c0 in (HALF, TAIL):
             nc.vector.tensor_tensor(last_back[:, c0 - HALF:c0 - HALF + P], h[LAST][:].indirect(pos1_t[:, c0 // LANES:(c0 + P) // LANES]),
                                     second[LAST][1][:, c0 - HALF:c0 - HALF + P], ALU.subtract)
         nc.scalar.activation(out=bounded[LAST][:, HALF:P1], in_=last_front, func=ACT.Tanh)
+        weigh(6)
         nc.scalar.activation(out=z_planes[1][:, PACK - 1, 0:HALF], in_=bounded[LAST][:, HALF:P1],
                              func=ACT.Copy, scale=gains[1][:, PACK - 1:PACK])
         for c0 in (HALF, TAIL):

@@ -63,7 +63,7 @@ def tile_list_peer_grading_kernel(tc, tab_words, tab_scales, offs, w1, pos1, pos
         raw = {(a, c): tile([P, PACK, c1 - c0], F32, "raw%d%d" % (a, c))
                for a in range(PASSES) for c, (c0, c1) in enumerate(PIECES) if (a, c) not in RAW_AT and c != 2 and (a, c) != (1, 1)}
         raw[1, 1] = placed.tile([P, PACK, P], F32, name="raw11", offset=RAW11_AT, align_bytes=64)
-        around = tile([P, 2 * S - 2 * P], F32, "around")
+        around = tile([P, TAIL + S], F32, "around")
         raw[0, 2] = around[:, TAIL:TAIL + S].rearrange("p (j c) -> p j c", j=PACK)
         halves = [tile([P, PACK, P], F32, "raw120"),
                   placed.tile([P, PACK, P], F32, name="raw121", offset=HALF_AT, align_bytes=64)]
@@ -87,7 +87,7 @@ def tile_list_peer_grading_kernel(tc, tab_words, tab_scales, offs, w1, pos1, pos
         z_planes = [None, slots[:, 1:PACK + 1, :]]
         z_woven = [tile([P, P1 * PACK], BF16, "z_woven%d" % a) for a in range(PASSES)]
 
-        whole = {0: around[:, 0:P1], 1: around[:, 2 * S - 2 * P - P1:2 * S - 2 * P]}
+        whole = {0: around[:, 0:P1], 1: halves[0][:].rearrange("p j c -> p (j c)")}
         second = {}
         for i in (3,):
             picks = tile([P, P1], F32, "second%d" % i)
@@ -177,10 +177,10 @@ def tile_list_peer_grading_kernel(tc, tab_words, tab_scales, offs, w1, pos1, pos
         def quantise_w1(u):
             nc.vector.quantize_mx(out=w1_words[u][:].bitcast(FP8X4), scales=w1_scales[u][:], in_=w1_woven[u][:])
 
-        def quantise_part(v):
+        def quantise_part(v, src):
             nc.vector.quantize_mx(out=w1_words[2][:, 2 * P * v:2 * P * (v + 1)].bitcast(FP8X4),
                                   scales=w1_scales[2][:, 2 * P * v:2 * P * (v + 1)],
-                                  in_=w1_woven[2][:, 2 * PASS * v:2 * PASS * (v + 1)])
+                                  in_=src[:])
 
         def stationary(i, a):
             if i < 2:
@@ -259,20 +259,22 @@ def tile_list_peer_grading_kernel(tc, tab_words, tab_scales, offs, w1, pos1, pos
         for a in range(PASSES):
             cast_w1(a, 1, nc.scalar.copy)
         h[0] = placed.tile([P, S], F32, name="h0", offset=RAW11_AT + 64, align_bytes=64)
-        w1_woven[2] = placed.tile([P, PACK * PASS], BF16, name="w1_woven2", offset=RAW11_AT + 64 - ROW_BYTES, align_bytes=64)
+        w1_woven[2] = placed.tile([P, 2 * PASS], BF16, name="w1_woven2", offset=RAW11_AT + 64 - TANH_BYTES, align_bytes=64)
         first_product(0, FIRST_CUTS)
         quantise_w1(1)
-        for u, src in enumerate((halves[0][:], raw[0, 2][:, :, 0:P], raw[0, 2][:, :, P:2 * P])):
+        for u, src in enumerate((halves[0][:], raw[0, 2][:, :, 0:P])):
             nc.vector.tensor_copy(out=w1_woven[2][:, PASS * u:PASS * (u + 1)].rearrange("p (m j) -> p m j", j=PACK),
                                   in_=src.rearrange("p j m -> p m j"))
-        quantise_part(0)
+        quantise_part(0, w1_woven[2])
+        side = placed.tile([P, 2 * PASS], BF16, name="side", offset=RAW11_AT + 64 - 2 * TANH_BYTES + 64, align_bytes=64)
+        for u, src in enumerate((raw[0, 2][:, :, P:2 * P], halves[1][:])):
+            nc.gpsimd.tensor_scalar(side[:, PASS * u:PASS * (u + 1)].rearrange("p (m j) -> p m j", j=PACK),
+                                    src.rearrange("p j m -> p m j"), 1.0, 0.0, ALU.mult, ALU.add)
         pick(0)
         h[1] = tile([P, S], F32, "h1")
         first_product(1)
         pick(1)
-        nc.scalar.copy(out=w1_woven[2][:, PASS * 3:PASS * 4].rearrange("p (m i j) -> p m j i", i=RUN, j=PACK),
-                       in_=halves[1][:].rearrange("p j (m i) -> p m j i", i=RUN))
-        quantise_part(1)
+        quantise_part(1, side)
         first_diffs = placed.tile([P, 2 * P1], F32, name="first_diffs", offset=HALF_AT, align_bytes=64)
         for i in (0, 1):
             diff[i] = first_diffs[:, P1 * i:P1 * (i + 1)]

@@ -26,17 +26,12 @@ RUN = 4
 HALF = P1 // 2
 TILES = H // P
 LAST = TILES - 1
-GPSIMD_GAINS = (0, 1, 2, 4, 5)
-PIECES = [(0, 128), (128, 256), (256, 512), (512, 768), (768, 1024)]
-FIRST_CUTS = (0, 512, 768, 1024)
-LAST_CUTS = (0, 256, 384, 512)
 TAIL = P1 - P
-ROW_BYTES = 4 * S
-TANH_BYTES = 4 * P1
-SPAN = 2 * ROW_BYTES + 2 * TANH_BYTES
-RAW_AT = {key: SPAN * u + TANH_BYTES for u, key in enumerate([(1, 3), (1, 4), (0, 3)])}
-RAW11_AT = 3 * SPAN + ROW_BYTES
-HALF_AT = RAW11_AT + 2 * ROW_BYTES + ROW_BYTES
+KB = 1024
+EDGE = 64
+CUT = 768
+LATE = 3712
+POOL_SHARE = 32
 
 
 def tile_list_peer_grading_kernel(tc, tab_words, tab_scales, offs, w1, pos1, pos2, gain,
@@ -50,67 +45,78 @@ def tile_list_peer_grading_kernel(tc, tab_words, tab_scales, offs, w1, pos1, pos
         def tile(shape, dtype, name, tag=None):
             return keep.tile(shape, dtype, name=name, tag=tag or name, align_bytes=64)
 
+        def place(shape, dtype, name, offset):
+            return placed.tile(shape, dtype, name=name, offset=offset, align_bytes=64)
+
         offs_t = tile([P, S // LANES], U16, "offs_t")
         pos1_t = tile([P, P1 // LANES], U16, "pos1_t")
         pos2_t = tile([P, P1 // LANES], U16, "pos2_t")
         pos3_t = tile([P, P2 // LANES], U16, "pos3_t")
         pos4_t = tile([P, P2 // LANES], U16, "pos4_t")
-        table_words = [tile([P, T], I32, "table_words%d" % a) for a in range(PASSES)]
+        table_words = [tile([P, T], I32, "table_words0"), place([P, T], I32, "table_words1", 4 * KB)]
         table_scales = tile([P, T], U8, "table_scales")
-        v_words = [tile([P, S], U32, "v_words%d" % a) for a in range(PASSES)]
+        v_words = [tile([P, S], U32, "v_words0"), tile([P, CUT], U32, "v_words1")]
         picked_scales = tile([P, S], U8, "picked_scales")
         v_scales = tile([P, PASSES, S], U8, "v_scales")
-        raw = {(a, c): tile([P, PACK, c1 - c0], F32, "raw%d%d" % (a, c))
-               for a in range(PASSES) for c, (c0, c1) in enumerate(PIECES) if (a, c) not in RAW_AT and c != 2 and (a, c) != (1, 1)}
-        raw[1, 1] = placed.tile([P, PACK, P], F32, name="raw11", offset=RAW11_AT, align_bytes=64)
-        around = tile([P, TAIL + S], F32, "around")
-        raw[0, 2] = around[:, TAIL:TAIL + S].rearrange("p (j c) -> p j c", j=PACK)
-        halves = [tile([P, PACK, P], F32, "raw120"),
-                  placed.tile([P, PACK, P], F32, name="raw121", offset=HALF_AT, align_bytes=64)]
-        for key in RAW_AT:
-            raw[key] = placed.tile([P, PACK, 2 * P], F32, name="raw%d%d" % key, offset=RAW_AT[key], align_bytes=64)
-
-        def after_cast(key, place, shape, dtype, name):
-            return placed.tile(shape, dtype, name=name, offset=RAW_AT[key] + 64 + TANH_BYTES * (place - 1), align_bytes=64)
-
-        widths = [2 * P, 2 * P, PASS, PASS, PASS]
-        w1_woven = {u: tile([P, PACK * w], BF16, "w1_woven%d" % u) for u, w in enumerate(widths) if u != 2}
-        w1_words = {u: tile([P, w], U32, "w1_words%d" % u) for u, w in enumerate(widths) if u != 3}
-        w1_scales = [tile([P, w], U8, "w1_scales%d" % u) for u, w in enumerate(widths)]
         gains = [tile([P, PACK], F32, "gain%d" % a) for a in range(PASSES)]
         w2_codes = tile([P, PASSES, 2 * N], U8, "w2_codes")
         w2_bytes = tile([P, PASSES, N], U8, "w2_bytes")
-        h = {i: tile([P, S], F32, "h%d" % i) for i in range(PACK, TILES)}
+
+        Z = 0
+        A = 2 * KB
+        B = A + 10 * KB - EDGE
+        D = B + 7 * KB
+        E2 = D + 4 * KB
+        C = E2 + 4 * KB
+        D1 = C + 10 * KB
+        W = D1 + 4 * KB
+        E = W + 7 * KB
+        F = E + 9 * KB
+        Y = F + 8 * KB - EDGE
+        X = F + 18 * KB
+        raw = {(a, i): tile([P, PACK, P], F32, "raw%d%d" % (a, i)) for a, i in ((0, 0), (0, 1))}
+        raw[1, 0] = place([P, PACK, P], F32, "raw10", Z)
+        v_end = place([P, S - CUT], U32, "v_end", Z)
+        raw[1, 1] = place([P, PACK, P], F32, "raw11", A)
+        raw[0, 2] = place([P, PACK, P], F32, "raw02", D)
+        raw[0, 3] = place([P, PACK, P], F32, "raw03", D + 2 * KB)
+        raw_mid = place([P, PACK, 2 * P], F32, "raw_mid", D1)
+        for i in (2, 3):
+            raw[1, i] = raw_mid[:, :, P * (i - 2):P * (i - 1)]
+        raw_late0 = [place([P, S + 32], F32, "raw_late00", E)[:, 0:S].rearrange("p (j c) -> p j c", j=PACK),
+                     place([P, PACK, 2 * P], F32, "raw_late01", E2)[:]]
+        raw_late1 = place([P, PACK, PASS], F32, "raw_late1", F)
+
+        woven1 = place([P, 2 * PASS], BF16, "woven1", B)
+        woven = {(a, 0): tile([P, PASS], BF16, "woven%d0" % a)[:] for a in range(PASSES)}
+        for a in range(PASSES):
+            woven[a, 1] = woven1[:, PASS * a:PASS * (a + 1)]
+        words1 = place([P, 2 * P], U32, "words1", C)
+        words_mid = tile([P, 2 * P], U32, "words_mid")
+        words = {(0, 0): tile([P, P], U32, "words00")[:], (1, 0): place([P, P], U32, "words10", B + 2 * KB)[:],
+                 (0, 1): words1[:, 0:P], (1, 1): words1[:, P:2 * P], (0, 2): words_mid[:, 0:P], (0, 3): words_mid[:, P:2 * P],
+                 (1, 2): tile([P, P], U32, "words12")[:], (1, 3): place([P, P], U32, "words13", E - 2 * KB - 6 * EDGE)[:]}
+        scales_early = tile([P, TILES * P], U8, "scales_early")
+        column = {(0, 0): 0, (1, 0): 1, (0, 1): 2, (1, 1): 3, (0, 2): 4, (0, 3): 5, (1, 2): 6, (1, 3): 7}
+        scales = {key: scales_early[:, P * c:P * (c + 1)] for key, c in column.items()}
+        words_late = {}
+        scales_late = [tile([P, PASS], U8, "scales_late%d" % a) for a in range(PASSES)]
+        h = {i: tile([P, S], F32, "h%d" % i) for i in (0, 4, 5, 6, 7)}
+
         slots = tile([P, PACK + 1, P1], BF16, "slots")
         z_halves = tile([P, 2, PACK, HALF], BF16, "z_halves")
         spent = z_halves[:].rearrange("p u t c -> p (u t c)").bitcast(F32)
         z_planes = [None, slots[:, 1:PACK + 1, :]]
-        z_woven = [tile([P, P1 * PACK], BF16, "z_woven%d" % a) for a in range(PASSES)]
-
-        whole = {0: around[:, 0:P1], 1: halves[0][:].rearrange("p j c -> p (j c)")}
-        second = {}
-        for i in (3,):
-            picks = tile([P, P1], F32, "second%d" % i)
-            second[i] = [picks[:, 0:HALF], picks[:, HALF:P1]]
+        z_woven = {1: tile([P, P1 * PACK], BF16, "z_woven1")}
         flat = slots[:].rearrange("p s c -> p (s c)")
+        whole = {}
+        whole[3] = tile([P, P1], F32, "second3")[:]
         whole[4] = tile([P, P1], F32, "second4")[:]
         whole[5] = flat[:, P1:3 * P1].bitcast(F32)
-        whole[6] = tile([P, P1], F32, "second6")[:]
-        whole[2] = tile([P, P1], F32, "second2")[:]
-        strip = tile([P, (PACK + 1) * P1 - P], F32, "strip")
-        bounded_late = strip[:, 0:PACK * P1].rearrange("p (t c) -> p t c", t=PACK)
-        second[LAST] = [tile([P, HALF], F32, "second7")[:], spent[:, 0:HALF]]
+        second_last = [tile([P, HALF], F32, "second7")[:], spent[:, 0:HALF]]
         last_front = spent[:, HALF:P1]
         diff = {}
-        diff[5] = bounded_late[:, 2, :]
-        diff[6] = bounded_late[:, 3, :]
-        diff[4] = strip[:, 4 * P1 - P:5 * P1 - P]
-        diff[3] = strip[:, 3 * P1 - 64:4 * P1 - 64]
-        bounded = {3: tile([P, P1], F32, "bounded3")[:]}
-        for t in range(PACK):
-            bounded[PACK + t] = bounded_late[:, t, :]
-        z_rows = [rows.bitcast(BF16)
-                  for rows in (whole[2][:, 0:HALF], second[3][0], second[3][1], bounded[5][:, 0:HALF])]
+        bounded = {}
 
         z_words = [tile([P, P1], U32, "z_words%d" % a) for a in range(PASSES)]
         z_scales = [tile([P, P1], U8, "z_scales%d" % a) for a in range(PASSES)]
@@ -118,17 +124,17 @@ def tile_list_peer_grading_kernel(tc, tab_words, tab_scales, offs, w1, pos1, pos
         right = [tile([P, P2], F32, "right%d" % n) for n in range(N // P)]
         one_plus = [tile([P, P2], F32, "one_plus%d" % n) for n in range(N // P)]
         result = [tile([P, P2], F32, "result%d" % n) for n in range(N // P)]
-        y_bank = [psum.tile([P, BANK], F32, name="y_bank%d" % n) for n in range(N // P)]
 
         for p0, p1 in ((32, 64), (64, P)):
             nc.vector.memset(table_scales[p0:p1, :].bitcast(I32), 0)
         nc.vector.memset(v_scales[:].rearrange("p a n -> p (a n)").bitcast(I32), 0)
         nc.vector.memset(w2_bytes[:].rearrange("p a n -> p (a n)").bitcast(I32), 0)
 
-        def load_w1(a, c):
-            c0, c1 = PIECES[c]
-            nc.sync.dma_start(out=raw[a, c][:, :, :],
-                              in_=w1[PASS * a:PASS * (a + 1), c0:c1].rearrange("(p j) c -> p j c", j=PACK))
+        def load_w1(dst, a, c0, c1):
+            nc.sync.dma_start(out=dst[:], in_=w1[PASS * a:PASS * (a + 1), c0:c1].rearrange("(p j) c -> p j c", j=PACK))
+
+        def load_early(a, i):
+            load_w1(raw[a, i], a, P * i, P * (i + 1))
 
         def load_words(a):
             nc.sync.dma_start(out=table_words[a][:], in_=tab_words[a].rearrange("p t i -> p (t i)").bitcast(I32))
@@ -137,77 +143,94 @@ def tile_list_peer_grading_kernel(tc, tab_words, tab_scales, offs, w1, pos1, pos
         for a in range(PASSES):
             nc.sync.dma_start(out=table_scales[a:32:PASSES, :].bitcast(I32), in_=tab_scales[a].bitcast(I32))
         load_words(0)
-        load_w1(0, 0)
-        load_w1(1, 0)
+        load_early(0, 0)
         load_words(1)
         nc.vector.tensor_copy(out=picked_scales[:], in_=table_scales[:].indirect(offs_t[:]))
-        for q in range(4):
+        for q in (0, 2, 1, 3):
             nc.sync.dma_start(out=v_scales[32 * q:32 * q + 4, :, :].bitcast(I32),
                               in_=picked_scales[8 * q:8 * q + 8, :].bitcast(I32))
-        load_w1(0, 1)
-        load_w1(1, 1)
-        nc.sync.dma_start(out=halves[0][:], in_=w1[PASS:H, 2 * P:3 * P].rearrange("(p j) c -> p j c", j=PACK))
-        load_w1(0, 2)
+        load_early(1, 0)
+        load_early(0, 1)
+        load_early(1, 1)
         nc.sync.dma_start(pos2_t[:], pos2)
         nc.sync.dma_start(pos1_t[:], pos1)
-        nc.sync.dma_start(out=halves[1][:], in_=w1[PASS:H, 3 * P:4 * P].rearrange("(p j) c -> p j c", j=PACK))
-        for a in range(PASSES):
-            load_w1(a, 3)
-            load_w1(a, 4)
+        load_early(0, 2)
+        load_early(0, 3)
+        load_w1(raw_mid, 1, 2 * P, PASS)
+        for u in range(2):
+            load_w1(raw_late0[u], 0, PASS + 2 * P * u, PASS + 2 * P * (u + 1))
+        load_w1(raw_late1, 1, PASS, H)
         with nc.allow_non_contiguous_dma(reason="one gain to a partition"):
             nc.sync.dma_start(out=gains[0][:], in_=gain[0:PASS].rearrange("(i p) -> p i", p=P))
         nc.sync.dma_start(out=gains[1][:], in_=gain[PASS:H].rearrange("(p t) -> p t", t=PACK))
         nc.sync.dma_start(out=w2_codes[:].bitcast(I32), in_=w2_words.rearrange("a p b -> p a b").bitcast(I32))
-        for q in range(4):
+        for q in (0, 2, 1, 3):
             nc.sync.dma_start(out=w2_bytes[32 * q:32 * q + 4, :, :].bitcast(I32),
                               in_=w2_scales[:, 4 * q:4 * q + 4, :].rearrange("a r n -> r a n").bitcast(I32))
         nc.sync.dma_start(pos4_t[:], pos4)
         nc.sync.dma_start(pos3_t[:], pos3)
 
-        def cast_w1(a, c, copy):
-            c0, c1 = PIECES[c]
-            if c1 <= PASS:
-                size = PACK * (c1 - c0)
-                dst = w1_woven[c][:, size * a:size * (a + 1)].rearrange("p (m i j) -> p m j i", i=RUN, j=PACK)
+        def on_scalar(out, in_):
+            nc.scalar.copy(out=out, in_=in_)
+
+        def on_vector(out, in_):
+            nc.vector.tensor_copy(out=out, in_=in_)
+
+        def on_pool(out, in_):
+            nc.gpsimd.tensor_scalar(out, in_, 1.0, 0.0, ALU.mult, ALU.add)
+
+        def cast_early(a, i, copy, c0=0, c1=P):
+            dst = woven[a, i][:, PACK * c0:PACK * c1]
+            if copy is not on_scalar:
+                copy(dst.rearrange("p (m j) -> p m j", j=PACK), raw[a, i][:, :, c0:c1].rearrange("p j m -> p m j"))
             else:
-                m0, m1 = (c0 - PASS) // PACK, (c1 - PASS) // PACK
-                dst = w1_woven[3 + a][:].rearrange("p (t m j) -> p m j t", t=PACK, j=PACK)[:, m0:m1, :, :]
-            copy(out=dst, in_=raw[a, c][:].rearrange("p j (m i) -> p m j i", i=RUN))
+                copy(dst.rearrange("p (m i j) -> p m j i", i=RUN, j=PACK),
+                     raw[a, i][:, :, c0:c1].rearrange("p j (m i) -> p m j i", i=RUN))
 
-        def quantise_w1(u):
-            nc.vector.quantize_mx(out=w1_words[u][:].bitcast(FP8X4), scales=w1_scales[u][:], in_=w1_woven[u][:])
+        woven_late = {}
 
-        def quantise_part(v, src):
-            nc.vector.quantize_mx(out=w1_words[2][:, 2 * P * v:2 * P * (v + 1)].bitcast(FP8X4),
-                                  scales=w1_scales[2][:, 2 * P * v:2 * P * (v + 1)],
-                                  in_=src[:])
+        def cast_late(a, m0, m1, src, copy):
+            walk = "p m t j" if copy is on_pool else "p m j t"
+            dst = woven_late[a].rearrange("p (t m j) -> " + walk, t=PACK, j=PACK)[:, m0:m1, :, :]
+            copy(dst, src.rearrange("p j (m t) -> " + walk, t=PACK))
+
+        def quantise(codes, planes, src):
+            nc.vector.quantize_mx(out=codes.bitcast(FP8X4), scales=planes, in_=src)
+
+        def quantise_early(a, i):
+            quantise(words[a, i], scales[a, i], woven[a, i])
+
+        def quantise_late(a, t0, t1, codes):
+            for t in range(t0, t1):
+                words_late[a, t] = codes[:, P * (t - t0):P * (t - t0 + 1)]
+            quantise(codes[:], scales_late[a][:, P * t0:P * t1], woven_late[a][:, PASS * t0:PASS * t1])
 
         def stationary(i, a):
-            if i < 2:
-                return i, P * a
             if i < PACK:
-                return 2, P * (1 - a if i == 2 else 2 + a)
-            return 3 + a, P * (i - PACK)
+                return words[a, i], scales[a, i]
+            return words_late[a, i - PACK], scales_late[a][:, P * (i - PACK):P * (i - PACK + 1)]
 
-        def first_product(i, cuts=(0, BANK, S)):
-            for c0, c1 in zip(cuts, cuts[1:]):
-                bank = psum.tile([P, BANK], F32, name="h_bank", tag="h_bank", bufs=4)
-                for a in range(PASSES):
-                    u, m0 = stationary(i, a)
-                    nc.tensor.matmul_mx(out=bank[:, 0:c1 - c0], lhsT=w1_words[u][:, m0:m0 + P].bitcast(FP8X4),
-                                        lhsT_scale=w1_scales[u][:, m0:m0 + P],
-                                        rhs=v_words[a][:, c0:c1].bitcast(FP8X4), rhs_scale=v_scales[:, a, c0:c1],
-                                        start=(a == 0), stop=(a == PASSES - 1))
-                nc.scalar.copy(out=h[i][:, c0:c1], in_=bank[:, 0:c1 - c0])
+        def moving(a, c0, c1):
+            return v_end[:, c0 - CUT:c1 - CUT] if a == 1 and c0 >= CUT else v_words[a][:, c0:c1]
 
-        def compare(i, cuts=(0, HALF, P1)):
-            for c0 in (0, HALF):
-                nc.vector.tensor_copy(out=second[i][c0 // HALF],
-                                      in_=h[i][:].indirect(pos2_t[:, c0 // LANES:(c0 + HALF) // LANES]))
-            for c0, c1 in zip(cuts, cuts[1:]):
-                other = second[i][c0 // HALF][:, c0 % HALF:c0 % HALF + c1 - c0]
-                nc.vector.tensor_tensor(diff[i][:, c0:c1], h[i][:].indirect(pos1_t[:, c0 // LANES:c1 // LANES]),
-                                        other, ALU.subtract)
+        def first_pass(bank, i, a, c0, c1):
+            codes, planes = stationary(i, a)
+            cuts = (c0, CUT, c1) if a == 1 and c0 < CUT < c1 else (c0, c1)
+            for b0, b1 in zip(cuts, cuts[1:]):
+                nc.tensor.matmul_mx(out=bank[:, b0 - c0:b1 - c0], lhsT=codes.bitcast(FP8X4), lhsT_scale=planes,
+                                    rhs=moving(a, b0, b1).bitcast(FP8X4), rhs_scale=v_scales[:, a, b0:b1],
+                                    start=(a == 0), stop=(a == PASSES - 1 and b1 == c1))
+
+        def first_product(i, ahead=True):
+            banks = [psum.tile([P, BANK], F32, name="h_bank", tag="h_bank", bufs=4) for u in range(2)]
+            if ahead:
+                for u in range(2):
+                    first_pass(banks[u], i, 0, BANK * u, BANK * (u + 1))
+            for u in range(2):
+                if not ahead:
+                    first_pass(banks[u], i, 0, BANK * u, BANK * (u + 1))
+                first_pass(banks[u], i, 1, BANK * u, BANK * (u + 1))
+                nc.scalar.copy(out=h[i][:, BANK * u:BANK * (u + 1)], in_=banks[u][:])
 
         def pick(i):
             nc.vector.tensor_copy(out=whole[i], in_=h[i][:].indirect(pos2_t[:]))
@@ -218,11 +241,13 @@ def tile_list_peer_grading_kernel(tc, tab_words, tab_scales, offs, w1, pos1, pos
         def bound(i):
             nc.scalar.activation(out=bounded[i], in_=diff[i], func=ACT.Tanh)
 
-        def weigh(i):
+        z_rows = {}
+
+        def weigh(i, on_gpsimd):
             a, t = divmod(i, PACK)
             dst = z_rows[t] if a == 0 else z_planes[a][:, t, 0:TAIL]
             src = bounded[i] if a == 0 else bounded[i][:, 0:TAIL]
-            if i in GPSIMD_GAINS:
+            if on_gpsimd:
                 nc.gpsimd.tensor_scalar(dst, src, gains[a][:, t:t + 1], 0.0, ALU.mult, ALU.add)
             else:
                 nc.scalar.activation(out=dst, in_=src, func=ACT.Copy, scale=gains[a][:, t:t + 1])
@@ -235,8 +260,7 @@ def tile_list_peer_grading_kernel(tc, tab_words, tab_scales, offs, w1, pos1, pos
                  in_=(z_halves[:, c0 // HALF, :, :] if a == 0 else z_planes[a][:, :, c0:c1]).rearrange("p t (c i) -> p c t i", i=RUN))
 
         def quantise_z(a, c0, c1):
-            nc.vector.quantize_mx(out=z_words[a][:, c0:c1].bitcast(FP8X4), scales=z_scales[a][:, c0:c1],
-                                  in_=z_woven[a][:, PACK * c0:PACK * c1])
+            quantise(z_words[a][:, c0:c1], z_scales[a][:, c0:c1], z_woven[a][:, PACK * c0:PACK * c1])
 
         def second_product(n, a, c0, c1, start, stop):
             bank = y_end[n] if n < 2 and c0 == HALF else y_bank[n]
@@ -246,91 +270,122 @@ def tile_list_peer_grading_kernel(tc, tab_words, tab_scales, offs, w1, pos1, pos
                                 start=start, stop=stop)
 
         def pick_words(a, c0, c1):
-            nc.vector.tensor_copy(out=v_words[a][:, c0:c1],
+            nc.vector.tensor_copy(out=moving(a, c0, c1),
                                   in_=table_words[a][:].bitcast(U32).indirect(offs_t[:, c0 // LANES:c1 // LANES]))
 
         pick_words(0, 0, S)
+        cast_early(0, 0, on_scalar)
+        quantise_early(0, 0)
+        pick_words(1, 0, CUT)
+        cast_early(1, 0, on_scalar)
+        quantise_early(1, 0)
+        pick_words(1, CUT, S)
+        quarters = [psum.tile([P, BANK], F32, name="quarter%d" % n, tag="y_bank%d" % n) for n in range(PACK)]
+        for n in range(PACK):
+            first_pass(quarters[n], 0, 0, HALF * n, HALF * (n + 1))
+        for n in range(PACK):
+            first_pass(quarters[n], 0, 1, HALF * n, HALF * (n + 1))
+            nc.scalar.copy(out=h[0][:, HALF * n:HALF * (n + 1)], in_=quarters[n][:, 0:HALF])
         for a in range(PASSES):
-            cast_w1(a, 0, nc.scalar.copy)
-        quantise_w1(0)
-        for c0, c1 in zip(FIRST_CUTS, FIRST_CUTS[1:]):
-            pick_words(1, c0, c1)
-
-        for a in range(PASSES):
-            cast_w1(a, 1, nc.scalar.copy)
-        h[0] = placed.tile([P, S], F32, name="h0", offset=RAW11_AT + 64, align_bytes=64)
-        w1_woven[2] = placed.tile([P, 2 * PASS], BF16, name="w1_woven2", offset=RAW11_AT + 64 - TANH_BYTES, align_bytes=64)
-        first_product(0, FIRST_CUTS)
-        quantise_w1(1)
-        for u, src in enumerate((halves[0][:], raw[0, 2][:, :, 0:P])):
-            nc.vector.tensor_copy(out=w1_woven[2][:, PASS * u:PASS * (u + 1)].rearrange("p (m j) -> p m j", j=PACK),
-                                  in_=src.rearrange("p j m -> p m j"))
-        quantise_part(0, w1_woven[2])
-        side = placed.tile([P, 2 * PASS], BF16, name="side", offset=RAW11_AT + 64 - 2 * TANH_BYTES + 64, align_bytes=64)
-        for u, src in enumerate((raw[0, 2][:, :, P:2 * P], halves[1][:])):
-            nc.gpsimd.tensor_scalar(side[:, PASS * u:PASS * (u + 1)].rearrange("p (m j) -> p m j", j=PACK),
-                                    src.rearrange("p j m -> p m j"), 1.0, 0.0, ALU.mult, ALU.add)
+            cast_early(a, 1, on_vector)
+        quantise(words1[:], scales_early[:, 2 * P:4 * P], woven1[:])
+        whole[0] = place([P, P1], F32, "second0", A)[:]
+        woven_mid = place([P, 2 * PASS], BF16, "woven_mid", B + EDGE)
+        woven[0, 2], woven[0, 3] = woven_mid[:, 0:PASS], woven_mid[:, PASS:2 * PASS]
+        cast_early(0, 2, on_scalar)
+        cast_early(0, 3, on_pool)
         pick(0)
-        h[1] = tile([P, S], F32, "h1")
-        first_product(1)
-        pick(1)
-        quantise_part(1, side)
-        first_diffs = placed.tile([P, 2 * P1], F32, name="first_diffs", offset=HALF_AT, align_bytes=64)
-        for i in (0, 1):
-            diff[i] = first_diffs[:, P1 * i:P1 * (i + 1)]
+        quantise(words_mid[:], scales_early[:, 4 * P:6 * P], woven_mid[:])
+        diff[0] = place([P, P1], F32, "diff0", D + KB)[:]
         subtract(0)
+
+        h[1] = place([P, S], F32, "h1", D - 4 * KB + EDGE)
+        first_product(1, False)
+        late = place([P, LATE], BF16, "late", C)
+        woven_late[0] = late[:, 0:2048]
+        woven[1, 3] = late[:, 1792:2304]
+        woven[1, 2] = late[:, 2240:2752]
+        whole[1] = late[:, 2688:3712].bitcast(F32)
+        cast_early(1, 2, on_scalar)
+        quantise_early(1, 2)
+        cast_early(1, 3, on_pool)
+        pick(1)
+        quantise_early(1, 3)
+        diff[1] = place([P, P1], F32, "diff1", D1)[:]
         subtract(1)
 
-        cast_w1(0, 3, nc.scalar.copy)
-        cast_w1(0, 4, nc.scalar.copy)
-        h[2] = after_cast((0, 3), 1, [P, S], F32, "h2")
+        cast_late(0, 0, P // 2, raw_late0[0], on_scalar)
+        h[2] = place([P, S], F32, "h2", E + EDGE)
+        h[3] = place([P, S], F32, "h3", E + 4 * KB + EDGE)
         first_product(2)
+        cast_late(0, P // 2, P, raw_late0[1], on_pool)
+        whole[2] = place([P, P1], F32, "second2", D1 + 2 * KB)[:]
         pick(2)
-        cast_w1(1, 3, nc.scalar.copy)
-        w1_words[3] = after_cast((1, 3), 0, [P, PASS], U32, "w1_words3")
-        diff[2] = after_cast((1, 3), 1, [P, P1], F32, "diff2")[:]
-        h[3] = after_cast((1, 3), 2, [P, S], F32, "h3")
-        quantise_w1(3)
-        subtract(2)
-        cast_w1(1, 4, nc.scalar.copy)
-        quantise_w1(4)
-        for i in range(3):
-            bounded[i] = after_cast((1, 4), i, [P, P1], F32, "bounded%d" % i)[:]
         first_product(3)
-        compare(3)
-
+        pick(3)
+        bounded[0] = place([P, P1], F32, "bounded0", E - 2 * KB + EDGE)[:]
         bound(0)
-        weigh(0)
+        late1 = place([P, PACK * PASS], BF16, "late1", E - 6 * KB - 5 * EDGE)
+        woven_late[1] = late1[:]
+        cast_late(1, POOL_SHARE, P, raw_late1[:, :, PACK * POOL_SHARE:PASS], on_scalar)
+        cast_late(1, 0, POOL_SHARE, raw_late1[:, :, 0:PACK * POOL_SHARE], on_pool)
+        quantise_late(0, 0, 1, place([P, P], U32, "words04", D + KB))
+        diff[2] = place([P, P1], F32, "diff2", D + 3 * KB - EDGE)[:]
+        subtract(2)
+        quantise_late(1, 0, 1, tile([P, P], U32, "words14"))
+        quantise_late(0, 1, PACK, place([P, 3 * P], U32, "words05", Y))
+        quantise_late(1, 1, 2, place([P, P], U32, "words15", X))
+        quantise_late(1, 2, PACK, place([P, 2 * P], U32, "words16", X + 2 * KB))
+        diff[3] = place([P, P1], F32, "diff3", F + 6 * KB - EDGE)[:]
+        subtract(3)
+        bounded[1] = place([P, P1], F32, "bounded1", F)[:]
+        bounded[2] = place([P, P1], F32, "bounded2", F + 2 * KB)[:]
+        for i in range(3):
+            z_rows[i] = place([P, P1], BF16, "z_rows%d" % i, W + KB * (i + 1))[:]
+
         bound(1)
-        weigh(1)
+        bound(2)
+        weigh(0, True)
+        weigh(1, True)
+        weigh(2, True)
         first_product(4)
         pick(4)
-        first_product(5)
+        first_product(5, False)
         pick(5)
-        bound(2)
-        weigh(2)
+        bounded[3] = place([P, P1], F32, "bounded3", X)[:]
         bound(3)
-        weigh(3)
+        diff[4] = place([P, P1], F32, "diff4", Y - 2 * KB + EDGE)[:]
+        diff[5] = place([P, P1], F32, "diff5", Y + KB + KB // 2 - EDGE)[:]
+        strip = tile([P, PACK * P1], F32, "strip")
+        bounded_late = strip[:].rearrange("p (t c) -> p t c", t=PACK)
+        for t in range(PACK):
+            bounded[PACK + t] = bounded_late[:, t, :]
+        z_rows[3] = bounded[6][:, 0:HALF].bitcast(BF16)
+        first_product(6, False)
+        weigh(3, False)
+        first_product(LAST, False)
         subtract(4)
         subtract(5)
-        first_product(6)
+        whole[6] = place([P, P1], F32, "second6", X + 2 * KB)[:]
         pick(6)
-        first_product(LAST)
-        nc.vector.tensor_copy(out=second[LAST][0], in_=h[LAST][:].indirect(pos2_t[:, 0:HALF // LANES]))
+        nc.vector.tensor_copy(out=second_last[0], in_=h[LAST][:].indirect(pos2_t[:, 0:HALF // LANES]))
         bound(4)
+        diff[6] = place([P, P1], F32, "diff6", Y - 2 * KB + 2 * EDGE)[:]
         subtract(6)
-        weigh(4)
+        weigh(4, True)
 
         bound(5)
-        weigh(5)
+        weigh(5, True)
+        z_woven[0] = place([P, P1 * PACK], BF16, "z_woven0", Y - 6 * KB + 2 * EDGE)
         weave_z(0, 0, HALF, nc.scalar.copy)
         weave_z(0, HALF, P1, nc.scalar.copy)
         bound(6)
 
         quantise_z(0, 0, HALF)
-        nc.vector.tensor_tensor(last_front, h[LAST][:].indirect(pos1_t[:, 0:HALF // LANES]), second[LAST][0], ALU.subtract)
-        nc.vector.tensor_copy(out=second[LAST][1], in_=h[LAST][:].indirect(pos2_t[:, HALF // LANES:P1 // LANES]))
+        nc.vector.tensor_tensor(last_front, h[LAST][:].indirect(pos1_t[:, 0:HALF // LANES]), second_last[0], ALU.subtract)
+        nc.vector.tensor_copy(out=second_last[1], in_=h[LAST][:].indirect(pos2_t[:, HALF // LANES:P1 // LANES]))
         quantise_z(0, HALF, P1)
+        y_bank = [psum.tile([P, BANK], F32, name="y_bank%d" % n, tag="y_bank%d" % n) for n in range(N // P)]
         y_end = [psum.tile([P, BANK], F32, name="h_bank", tag="h_bank", bufs=4) for n in range(2)]
         for half in (0, HALF):
             for n in range(N // P):
@@ -339,10 +394,10 @@ def tile_list_peer_grading_kernel(tc, tab_words, tab_scales, offs, w1, pos1, pos
         last_back = spent[:, P1:P1 + HALF]
         for c0 in (HALF, TAIL):
             nc.vector.tensor_tensor(last_back[:, c0 - HALF:c0 - HALF + P], h[LAST][:].indirect(pos1_t[:, c0 // LANES:(c0 + P) // LANES]),
-                                    second[LAST][1][:, c0 - HALF:c0 - HALF + P], ALU.subtract)
-        nc.scalar.activation(out=bounded[LAST][:, HALF:P1], in_=last_front, func=ACT.Tanh)
-        weigh(6)
-        nc.scalar.activation(out=z_planes[1][:, PACK - 1, 0:HALF], in_=bounded[LAST][:, HALF:P1],
+                                    second_last[1][:, c0 - HALF:c0 - HALF + P], ALU.subtract)
+        nc.scalar.activation(out=bounded[LAST][:, 0:HALF], in_=last_front, func=ACT.Tanh)
+        weigh(6, False)
+        nc.scalar.activation(out=z_planes[1][:, PACK - 1, 0:HALF], in_=bounded[LAST][:, 0:HALF],
                              func=ACT.Copy, scale=gains[1][:, PACK - 1:PACK])
         for c0 in (HALF, TAIL):
             nc.scalar.activation(out=bounded[LAST][:, c0:c0 + P], in_=last_back[:, c0 - HALF:c0 - HALF + P], func=ACT.Tanh)

@@ -30,7 +30,7 @@ TAIL = P1 - P
 KB = 1024
 EDGE = 64
 CUT = 768
-LATE = 3712
+LATE = 2816
 POOL_SHARE = 32
 
 
@@ -65,11 +65,11 @@ def tile_list_peer_grading_kernel(tc, tab_words, tab_scales, offs, w1, pos1, pos
         Z = 0
         A = 2 * KB
         B = A + 10 * KB - EDGE
-        D = B + 7 * KB
-        E2 = D + 4 * KB
-        C = E2 + 4 * KB
-        D1 = C + 10 * KB
-        W = D1 + 4 * KB
+        LATE_AT = B + 2 * KB
+        D0 = B + 12 * KB
+        D = D0 + 6 * KB
+        D1 = D + 8 * KB
+        W = D1 + 5 * KB
         E = W + 7 * KB
         F = E + 9 * KB
         Y = F + 8 * KB - EDGE
@@ -78,27 +78,26 @@ def tile_list_peer_grading_kernel(tc, tab_words, tab_scales, offs, w1, pos1, pos
         raw[1, 0] = place([P, PACK, P], F32, "raw10", Z)
         v_end = place([P, S - CUT], U32, "v_end", Z)
         raw[1, 1] = place([P, PACK, P], F32, "raw11", A)
-        raw[0, 2] = place([P, PACK, P], F32, "raw02", D)
-        raw[0, 3] = place([P, PACK, P], F32, "raw03", D + 2 * KB)
-        raw_mid = place([P, PACK, 2 * P], F32, "raw_mid", D1)
-        for i in (2, 3):
-            raw[1, i] = raw_mid[:, :, P * (i - 2):P * (i - 1)]
+        raw[0, 2] = place([P, PACK, P], F32, "raw02", D0)
+        raw[1, 2] = place([P, PASS + 32], F32, "raw12", D)[:, 0:PASS].rearrange("p (j c) -> p j c", j=PACK)
+        for a in range(PASSES):
+            raw[a, 3] = place([P, PACK, P], F32, "raw%d3" % a, D1 + 2 * KB * a)
         raw_late0 = [place([P, S + 32], F32, "raw_late00", E)[:, 0:S].rearrange("p (j c) -> p j c", j=PACK),
-                     place([P, PACK, 2 * P], F32, "raw_late01", E2)[:]]
+                     place([P, PACK, 2 * P], F32, "raw_late01", D - 4 * KB)[:]]
         raw_late1 = place([P, PACK, PASS], F32, "raw_late1", F)
 
         woven1 = place([P, 2 * PASS], BF16, "woven1", B)
         woven = {(a, 0): tile([P, PASS], BF16, "woven%d0" % a)[:] for a in range(PASSES)}
         for a in range(PASSES):
             woven[a, 1] = woven1[:, PASS * a:PASS * (a + 1)]
-        words1 = place([P, 2 * P], U32, "words1", C)
-        words_mid = tile([P, 2 * P], U32, "words_mid")
-        words = {(0, 0): tile([P, P], U32, "words00")[:], (1, 0): place([P, P], U32, "words10", B + 2 * KB)[:],
-                 (0, 1): words1[:, 0:P], (1, 1): words1[:, P:2 * P], (0, 2): words_mid[:, 0:P], (0, 3): words_mid[:, P:2 * P],
-                 (1, 2): tile([P, P], U32, "words12")[:], (1, 3): place([P, P], U32, "words13", E - 2 * KB - 6 * EDGE)[:]}
+        both = {1: tile([P, 2 * P], U32, "words1"), 2: tile([P, 2 * P], U32, "words2"),
+                3: place([P, 2 * P], U32, "words3", E - 3 * KB + 2 * EDGE)}
+        words = {(0, 0): tile([P, P], U32, "words00")[:], (1, 0): place([P, P], U32, "words10", B + 2 * KB)[:]}
+        for i in (1, 2, 3):
+            for a in range(PASSES):
+                words[a, i] = both[i][:, P * a:P * (a + 1)]
         scales_early = tile([P, TILES * P], U8, "scales_early")
-        column = {(0, 0): 0, (1, 0): 1, (0, 1): 2, (1, 1): 3, (0, 2): 4, (0, 3): 5, (1, 2): 6, (1, 3): 7}
-        scales = {key: scales_early[:, P * c:P * (c + 1)] for key, c in column.items()}
+        scales = {(a, i): scales_early[:, P * (2 * i + a):P * (2 * i + a + 1)] for a in range(PASSES) for i in range(PACK)}
         words_late = {}
         scales_late = [tile([P, PASS], U8, "scales_late%d" % a) for a in range(PASSES)]
         h = {i: tile([P, S], F32, "h%d" % i) for i in (0, 4, 5, 6, 7)}
@@ -154,9 +153,9 @@ def tile_list_peer_grading_kernel(tc, tab_words, tab_scales, offs, w1, pos1, pos
         load_early(1, 1)
         nc.sync.dma_start(pos2_t[:], pos2)
         nc.sync.dma_start(pos1_t[:], pos1)
-        load_early(0, 2)
-        load_early(0, 3)
-        load_w1(raw_mid, 1, 2 * P, PASS)
+        for i in (2, 3):
+            for a in range(PASSES):
+                load_early(a, i)
         for u in range(2):
             load_w1(raw_late0[u], 0, PASS + 2 * P * u, PASS + 2 * P * (u + 1))
         load_w1(raw_late1, 1, PASS, H)
@@ -199,6 +198,9 @@ def tile_list_peer_grading_kernel(tc, tab_words, tab_scales, offs, w1, pos1, pos
 
         def quantise_early(a, i):
             quantise(words[a, i], scales[a, i], woven[a, i])
+
+        def quantise_both(i, src):
+            quantise(both[i][:], scales_early[:, 2 * P * i:2 * P * (i + 1)], src)
 
         def quantise_late(a, t0, t1, codes):
             for t in range(t0, t1):
@@ -288,49 +290,47 @@ def tile_list_peer_grading_kernel(tc, tab_words, tab_scales, offs, w1, pos1, pos
             nc.scalar.copy(out=h[0][:, HALF * n:HALF * (n + 1)], in_=quarters[n][:, 0:HALF])
         for a in range(PASSES):
             cast_early(a, 1, on_vector)
-        quantise(words1[:], scales_early[:, 2 * P:4 * P], woven1[:])
+        quantise_both(1, woven1[:])
         whole[0] = place([P, P1], F32, "second0", A)[:]
-        woven_mid = place([P, 2 * PASS], BF16, "woven_mid", B + EDGE)
-        woven[0, 2], woven[0, 3] = woven_mid[:, 0:PASS], woven_mid[:, PASS:2 * PASS]
+        woven2 = place([P, 2 * PASS], BF16, "woven2", B + EDGE)
+        woven[0, 2], woven[1, 2] = woven2[:, 0:PASS], woven2[:, PASS:2 * PASS]
         cast_early(0, 2, on_scalar)
-        cast_early(0, 3, on_pool)
+        cast_early(1, 2, on_pool)
         pick(0)
-        quantise(words_mid[:], scales_early[:, 4 * P:6 * P], woven_mid[:])
-        diff[0] = place([P, P1], F32, "diff0", D + KB)[:]
+        quantise_both(2, woven2[:])
+        diff[0] = place([P, P1], F32, "diff0", D)[:]
         subtract(0)
 
-        h[1] = place([P, S], F32, "h1", D - 4 * KB + EDGE)
+        h[1] = place([P, S], F32, "h1", D0 - 4 * KB + EDGE)
         first_product(1, False)
-        late = place([P, LATE], BF16, "late", C)
+        late = place([P, LATE], BF16, "late", LATE_AT)
         woven_late[0] = late[:, 0:2048]
-        woven[1, 3] = late[:, 1792:2304]
-        woven[1, 2] = late[:, 2240:2752]
-        whole[1] = late[:, 2688:3712].bitcast(F32)
-        cast_early(1, 2, on_scalar)
-        quantise_early(1, 2)
+        woven[0, 3], woven[1, 3] = late[:, 1792:2304], late[:, 2304:2816]
+        cast_early(0, 3, on_scalar)
         cast_early(1, 3, on_pool)
+        whole[1] = place([P, P1], F32, "second1", D + 2 * KB)[:]
         pick(1)
-        quantise_early(1, 3)
-        diff[1] = place([P, P1], F32, "diff1", D1)[:]
+        quantise_both(3, late[:, 1792:2816])
+        diff[1] = place([P, P1], F32, "diff1", D1 + 2 * EDGE)[:]
         subtract(1)
 
+        h[2] = place([P, S], F32, "h2", D1 - 4 * KB + EDGE)
+        first_product(2, False)
         cast_late(0, 0, P // 2, raw_late0[0], on_scalar)
-        h[2] = place([P, S], F32, "h2", E + EDGE)
-        h[3] = place([P, S], F32, "h3", E + 4 * KB + EDGE)
-        first_product(2)
+        h[3] = place([P, S], F32, "h3", E + EDGE)
         cast_late(0, P // 2, P, raw_late0[1], on_pool)
-        whole[2] = place([P, P1], F32, "second2", D1 + 2 * KB)[:]
+        whole[2] = place([P, P1], F32, "second2", D1 + 2 * KB + 2 * EDGE)[:]
         pick(2)
-        first_product(3)
+        first_product(3, False)
         pick(3)
         bounded[0] = place([P, P1], F32, "bounded0", E - 2 * KB + EDGE)[:]
         bound(0)
-        late1 = place([P, PACK * PASS], BF16, "late1", E - 6 * KB - 5 * EDGE)
+        late1 = place([P, PACK * PASS], BF16, "late1", E - 7 * KB + 3 * EDGE)
         woven_late[1] = late1[:]
         cast_late(1, POOL_SHARE, P, raw_late1[:, :, PACK * POOL_SHARE:PASS], on_scalar)
         cast_late(1, 0, POOL_SHARE, raw_late1[:, :, 0:PACK * POOL_SHARE], on_pool)
-        quantise_late(0, 0, 1, place([P, P], U32, "words04", D + KB))
-        diff[2] = place([P, P1], F32, "diff2", D + 3 * KB - EDGE)[:]
+        quantise_late(0, 0, 1, place([P, P], U32, "words04", D + EDGE))
+        diff[2] = place([P, P1], F32, "diff2", D - 2 * KB + EDGE)[:]
         subtract(2)
         quantise_late(1, 0, 1, tile([P, P], U32, "words14"))
         quantise_late(0, 1, PACK, place([P, 3 * P], U32, "words05", Y))

@@ -29,6 +29,7 @@ LAST = TILES - 1
 TAIL = P1 - P
 KB = 1024
 EDGE = 64
+WARM = 3
 CUT = 768
 LATE = 2816
 POOL_SHARE = 32
@@ -90,7 +91,8 @@ def tile_list_peer_grading_kernel(tc, tab_words, tab_scales, offs, w1, pos1, pos
         woven = {(a, 0): tile([P, PASS], BF16, "woven%d0" % a)[:] for a in range(PASSES)}
         for a in range(PASSES):
             woven[a, 1] = woven1[:, PASS * a:PASS * (a + 1)]
-        both = {1: tile([P, 2 * P], U32, "words1"), 2: tile([P, 2 * P], U32, "words2"),
+        words12 = tile([P, 4 * P], U32, "words12")
+        both = {1: words12[:, 0:2 * P], 2: words12[:, 2 * P:4 * P],
                 3: place([P, 2 * P], U32, "words3", E - 3 * KB + 2 * EDGE)}
         words = {(0, 0): tile([P, P], U32, "words00")[:], (1, 0): place([P, P], U32, "words10", B + 2 * KB)[:]}
         for i in (1, 2, 3):
@@ -139,8 +141,7 @@ def tile_list_peer_grading_kernel(tc, tab_words, tab_scales, offs, w1, pos1, pos
             nc.sync.dma_start(out=table_words[a][:], in_=tab_words[a].rearrange("p t i -> p (t i)").bitcast(I32))
 
         nc.sync.dma_start(offs_t[:], offs)
-        for a in range(PASSES):
-            nc.sync.dma_start(out=table_scales[a:32:PASSES, :].bitcast(I32), in_=tab_scales[a].bitcast(I32))
+        nc.sync.dma_start(out=table_scales[0:32, :].bitcast(I32), in_=tab_scales.rearrange("a q t -> q a t").bitcast(I32))
         load_words(0)
         load_early(0, 0)
         load_words(1)
@@ -180,7 +181,7 @@ def tile_list_peer_grading_kernel(tc, tab_words, tab_scales, offs, w1, pos1, pos
 
         def cast_early(a, i, copy, c0=0, c1=P):
             dst = woven[a, i][:, PACK * c0:PACK * c1]
-            if copy is not on_scalar:
+            if copy is on_pool:
                 copy(dst.rearrange("p (m j) -> p m j", j=PACK), raw[a, i][:, :, c0:c1].rearrange("p j m -> p m j"))
             else:
                 copy(dst.rearrange("p (m i j) -> p m j i", i=RUN, j=PACK),
@@ -223,8 +224,11 @@ def tile_list_peer_grading_kernel(tc, tab_words, tab_scales, offs, w1, pos1, pos
                                     rhs=moving(a, b0, b1).bitcast(FP8X4), rhs_scale=v_scales[:, a, b0:b1],
                                     start=(a == 0), stop=(a == PASSES - 1 and b1 == c1))
 
+        def h_bank(k):
+            return psum.tile([P, BANK], F32, name="h_bank%d" % k, tag="h_bank%d" % k)
+
         def first_product(i, ahead=True):
-            banks = [psum.tile([P, BANK], F32, name="h_bank", tag="h_bank", bufs=4) for u in range(2)]
+            banks = [h_bank(2 * (i % 2) + u) for u in range(2)]
             if ahead:
                 for u in range(2):
                     first_pass(banks[u], i, 0, BANK * u, BANK * (u + 1))
@@ -322,6 +326,10 @@ def tile_list_peer_grading_kernel(tc, tab_words, tab_scales, offs, w1, pos1, pos
         whole[2] = place([P, P1], F32, "second2", D1 + 2 * KB + 2 * EDGE)[:]
         pick(2)
         first_product(3, False)
+        idle = h_bank(3)
+        for n in range(WARM):
+            nc.tensor.matmul_mx(out=idle[:], lhsT=words[0, 2].bitcast(FP8X4), lhsT_scale=scales[0, 2],
+                                rhs=words12[:].bitcast(FP8X4), rhs_scale=scales_early[:, 2 * P:6 * P], start=True, stop=True)
         pick(3)
         bounded[0] = place([P, P1], F32, "bounded0", E - 2 * KB + EDGE)[:]
         bound(0)
@@ -386,7 +394,7 @@ def tile_list_peer_grading_kernel(tc, tab_words, tab_scales, offs, w1, pos1, pos
         nc.vector.tensor_copy(out=second_last[1], in_=h[LAST][:].indirect(pos2_t[:, HALF // LANES:P1 // LANES]))
         quantise_z(0, HALF, P1)
         y_bank = [psum.tile([P, BANK], F32, name="y_bank%d" % n, tag="y_bank%d" % n) for n in range(N // P)]
-        y_end = [psum.tile([P, BANK], F32, name="h_bank", tag="h_bank", bufs=4) for n in range(2)]
+        y_end = [h_bank(n) for n in range(2)]
         for half in (0, HALF):
             for n in range(N // P):
                 for c0 in (half, half + P):

from contextlib import ExitStack

import concourse.mybir as mybir

K, H, N, T, S, P1, P2 = 1024, 1024, 512, 2048, 1024, 512, 256
FLOPS = 2 * K * H * S + 2 * H * N * P1

F32 = mybir.dt.float32
BF16 = mybir.dt.bfloat16
I32 = mybir.dt.int32
U32 = mybir.dt.uint32
U16 = mybir.dt.uint16
U8 = mybir.dt.uint8
FP8X4 = mybir.dt.float8_e4m3fn_x4
FP4X4 = mybir.dt.float4_e2m1fn_x4
ALU = mybir.AluOpType
ACT = mybir.ActivationFunctionType

P = 128
PACK = 4
PASS = P * PACK
PASSES = 2
BANK = 512
LANES = 16
RUN = 4
HALF = P1 // 2
TILES = H // P
LAST = TILES - 1
TAIL = P1 - P
KB = 1024
EDGE = 64
WARM = 3
CUT = 768
LATE = 2816
POOL_SHARE = 32


def tile_list_peer_grading_kernel(tc, tab_words, tab_scales, offs, w1, pos1, pos2, gain,
                                            w2_words, w2_scales, pos3, pos4, out):
    nc = tc.nc
    with ExitStack() as ctx:
        keep = ctx.enter_context(tc.tile_pool(name="keep", bufs=1))
        placed = ctx.enter_context(tc.tile_pool(name="placed", bufs=1))
        psum = ctx.enter_context(tc.psum_pool(name="psum", bufs=1))

        def tile(shape, dtype, name, tag=None):
            return keep.tile(shape, dtype, name=name, tag=tag or name, align_bytes=64)

        def place(shape, dtype, name, offset):
            return placed.tile(shape, dtype, name=name, offset=offset, align_bytes=64)

        offs_t = tile([P, S // LANES], U16, "offs_t")
        pos1_t = tile([P, P1 // LANES], U16, "pos1_t")
        pos2_t = tile([P, P1 // LANES], U16, "pos2_t")
        pos3_t = tile([P, P2 // LANES], U16, "pos3_t")
        pos4_t = tile([P, P2 // LANES], U16, "pos4_t")
        table_words = [tile([P, T], I32, "table_words0"), place([P, T], I32, "table_words1", 4 * KB)]
        table_scales = tile([P, T], U8, "table_scales")
        v_words = [tile([P, S], U32, "v_words0"), tile([P, CUT], U32, "v_words1")]
        picked_scales = tile([P, S], U8, "picked_scales")
        v_scales = tile([P, PASSES, S], U8, "v_scales")
        gains = [tile([P, PACK], F32, "gain%d" % a) for a in range(PASSES)]
        w2_codes = tile([P, PASSES, 2 * N], U8, "w2_codes")
        w2_bytes = tile([P, PASSES, N], U8, "w2_bytes")

        Z = 0
        A = 2 * KB
        B = A + 10 * KB - EDGE
        LATE_AT = B + 2 * KB
        D0 = B + 12 * KB
        D = D0 + 6 * KB
        D1 = D + 8 * KB
        W = D1 + 5 * KB
        E = W + 7 * KB
        F = E + 9 * KB
        Y = F + 8 * KB - EDGE
        X = F + 18 * KB
        raw = {(a, i): tile([P, PACK, P], F32, "raw%d%d" % (a, i)) for a, i in ((0, 0), (0, 1))}
        raw[1, 0] = place([P, PACK, P], F32, "raw10", Z)
        v_end = place([P, S - CUT], U32, "v_end", Z)
        raw[1, 1] = place([P, PACK, P], F32, "raw11", A)
        raw[0, 2] = place([P, PACK, P], F32, "raw02", D0)
        raw[1, 2] = place([P, PASS + 32], F32, "raw12", D)[:, 0:PASS].rearrange("p (j c) -> p j c", j=PACK)
        for a in range(PASSES):
            raw[a, 3] = place([P, PACK, P], F32, "raw%d3" % a, D1 + 2 * KB * a)
        raw_late0 = [place([P, S + 32], F32, "raw_late00", E)[:, 0:S].rearrange("p (j c) -> p j c", j=PACK),
                     place([P, PACK, 2 * P], F32, "raw_late01", D - 4 * KB)[:]]
        raw_late1 = place([P, PACK, PASS], F32, "raw_late1", F)

        woven1 = place([P, 2 * PASS], BF16, "woven1", B)
        woven = {(a, 0): tile([P, PASS], BF16, "woven%d0" % a)[:] for a in range(PASSES)}
        for a in range(PASSES):
            woven[a, 1] = woven1[:, PASS * a:PASS * (a + 1)]
        words12 = tile([P, 4 * P], U32, "words12")
        both = {1: words12[:, 0:2 * P], 2: words12[:, 2 * P:4 * P],
                3: place([P, 2 * P], U32, "words3", E - 3 * KB + 2 * EDGE)}
        words = {(0, 0): tile([P, P], U32, "words00")[:], (1, 0): place([P, P], U32, "words10", B + 2 * KB)[:]}
        for i in (1, 2, 3):
            for a in range(PASSES):
                words[a, i] = both[i][:, P * a:P * (a + 1)]
        scales_early = tile([P, TILES * P], U8, "scales_early")
        scales = {(a, i): scales_early[:, P * (2 * i + a):P * (2 * i + a + 1)] for a in range(PASSES) for i in range(PACK)}
        words_late = {}
        scales_late = [tile([P, PASS], U8, "scales_late%d" % a) for a in range(PASSES)]
        h = {i: tile([P, S], F32, "h%d" % i) for i in (0, 4, 5, 6, 7)}

        slots = tile([P, PACK + 1, P1], BF16, "slots")
        z_halves = tile([P, 2, PACK, HALF], BF16, "z_halves")
        spent = z_halves[:].rearrange("p u t c -> p (u t c)").bitcast(F32)
        z_planes = [None, slots[:, 1:PACK + 1, :]]
        z_woven = {1: tile([P, P1 * PACK], BF16, "z_woven1")}
        flat = slots[:].rearrange("p s c -> p (s c)")
        whole = {}
        whole[3] = tile([P, P1], F32, "second3")[:]
        whole[4] = tile([P, P1], F32, "second4")[:]
        whole[5] = flat[:, P1:3 * P1].bitcast(F32)
        second_last = [tile([P, HALF], F32, "second7")[:], spent[:, 0:HALF]]
        last_front = spent[:, HALF:P1]
        diff = {}
        bounded = {}

        z_words = [tile([P, P1], U32, "z_words%d" % a) for a in range(PASSES)]
        z_scales = [tile([P, P1], U8, "z_scales%d" % a) for a in range(PASSES)]
        y = [tile([P, P1], F32, "y%d" % n) for n in range(N // P)]
        right = [tile([P, P2], F32, "right%d" % n) for n in range(N // P)]
        one_plus = [tile([P, P2], F32, "one_plus%d" % n) for n in range(N // P)]
        result = [tile([P, P2], F32, "result%d" % n) for n in range(N // P)]

        for p0, p1 in ((32, 64), (64, P)):
            nc.vector.memset(table_scales[p0:p1, :].bitcast(I32), 0)
        nc.vector.memset(v_scales[:].rearrange("p a n -> p (a n)").bitcast(I32), 0)
        nc.vector.memset(w2_bytes[:].rearrange("p a n -> p (a n)").bitcast(I32), 0)

        def load_w1(dst, a, c0, c1):
            nc.sync.dma_start(out=dst[:], in_=w1[PASS * a:PASS * (a + 1), c0:c1].rearrange("(p j) c -> p j c", j=PACK))

        def load_early(a, i):
            load_w1(raw[a, i], a, P * i, P * (i + 1))

        def load_words(a):
            nc.sync.dma_start(out=table_words[a][:], in_=tab_words[a].rearrange("p t i -> p (t i)").bitcast(I32))

        nc.sync.dma_start(offs_t[:], offs)
        nc.sync.dma_start(out=table_scales[0:32, :].bitcast(I32), in_=tab_scales.rearrange("a q t -> q a t").bitcast(I32))
        load_words(0)
        load_early(0, 0)
        load_words(1)
        nc.vector.tensor_copy(out=picked_scales[:], in_=table_scales[:].indirect(offs_t[:]))
        for q in (0, 2, 1, 3):
            nc.sync.dma_start(out=v_scales[32 * q:32 * q + 4, :, :].bitcast(I32),
                              in_=picked_scales[8 * q:8 * q + 8, :].bitcast(I32))
        load_early(1, 0)
        load_early(0, 1)
        load_early(1, 1)
        nc.sync.dma_start(pos2_t[:], pos2)
        nc.sync.dma_start(pos1_t[:], pos1)
        for i in (2, 3):
            for a in range(PASSES):
                load_early(a, i)
        for u in range(2):
            load_w1(raw_late0[u], 0, PASS + 2 * P * u, PASS + 2 * P * (u + 1))
        load_w1(raw_late1, 1, PASS, H)
        with nc.allow_non_contiguous_dma(reason="one gain to a partition"):
            nc.sync.dma_start(out=gains[0][:], in_=gain[0:PASS].rearrange("(i p) -> p i", p=P))
        nc.sync.dma_start(out=gains[1][:], in_=gain[PASS:H].rearrange("(p t) -> p t", t=PACK))
        nc.sync.dma_start(out=w2_codes[:].bitcast(I32), in_=w2_words.rearrange("a p b -> p a b").bitcast(I32))
        for q in (0, 2, 1, 3):
            nc.sync.dma_start(out=w2_bytes[32 * q:32 * q + 4, :, :].bitcast(I32),
                              in_=w2_scales[:, 4 * q:4 * q + 4, :].rearrange("a r n -> r a n").bitcast(I32))
        nc.sync.dma_start(pos4_t[:], pos4)
        nc.sync.dma_start(pos3_t[:], pos3)

        def on_scalar(out, in_):
            nc.scalar.copy(out=out, in_=in_)

        def on_vector(out, in_):
            nc.vector.tensor_copy(out=out, in_=in_)

        def on_pool(out, in_):
            nc.gpsimd.tensor_scalar(out, in_, 1.0, 0.0, ALU.mult, ALU.add)

        def cast_early(a, i, copy, c0=0, c1=P):
            dst = woven[a, i][:, PACK * c0:PACK * c1]
            if copy is on_pool:
                copy(dst.rearrange("p (m j) -> p m j", j=PACK), raw[a, i][:, :, c0:c1].rearrange("p j m -> p m j"))
            else:
                copy(dst.rearrange("p (m i j) -> p m j i", i=RUN, j=PACK),
                     raw[a, i][:, :, c0:c1].rearrange("p j (m i) -> p m j i", i=RUN))

        woven_late = {}

        def cast_late(a, m0, m1, src, copy):
            walk = "p m t j" if copy is on_pool else "p m j t"
            dst = woven_late[a].rearrange("p (t m j) -> " + walk, t=PACK, j=PACK)[:, m0:m1, :, :]
            copy(dst, src.rearrange("p j (m t) -> " + walk, t=PACK))

        def quantise(codes, planes, src):
            nc.vector.quantize_mx(out=codes.bitcast(FP8X4), scales=planes, in_=src)

        def quantise_early(a, i):
            quantise(words[a, i], scales[a, i], woven[a, i])

        def quantise_both(i, src):
            quantise(both[i][:], scales_early[:, 2 * P * i:2 * P * (i + 1)], src)

        def quantise_late(a, t0, t1, codes):
            for t in range(t0, t1):
                words_late[a, t] = codes[:, P * (t - t0):P * (t - t0 + 1)]
            quantise(codes[:], scales_late[a][:, P * t0:P * t1], woven_late[a][:, PASS * t0:PASS * t1])

        def stationary(i, a):
            if i < PACK:
                return words[a, i], scales[a, i]
            return words_late[a, i - PACK], scales_late[a][:, P * (i - PACK):P * (i - PACK + 1)]

        def moving(a, c0, c1):
            return v_end[:, c0 - CUT:c1 - CUT] if a == 1 and c0 >= CUT else v_words[a][:, c0:c1]

        def first_pass(bank, i, a, c0, c1):
            codes, planes = stationary(i, a)
            cuts = (c0, CUT, c1) if a == 1 and c0 < CUT < c1 else (c0, c1)
            for b0, b1 in zip(cuts, cuts[1:]):
                nc.tensor.matmul_mx(out=bank[:, b0 - c0:b1 - c0], lhsT=codes.bitcast(FP8X4), lhsT_scale=planes,
                                    rhs=moving(a, b0, b1).bitcast(FP8X4), rhs_scale=v_scales[:, a, b0:b1],
                                    start=(a == 0), stop=(a == PASSES - 1 and b1 == c1))

        def h_bank(k):
            return psum.tile([P, BANK], F32, name="h_bank%d" % k, tag="h_bank%d" % k)

        def first_product(i, ahead=True):
            banks = [h_bank(2 * (i % 2) + u) for u in range(2)]
            if ahead:
                for u in range(2):
                    first_pass(banks[u], i, 0, BANK * u, BANK * (u + 1))
            for u in range(2):
                if not ahead:
                    first_pass(banks[u], i, 0, BANK * u, BANK * (u + 1))
                first_pass(banks[u], i, 1, BANK * u, BANK * (u + 1))
                nc.scalar.copy(out=h[i][:, BANK * u:BANK * (u + 1)], in_=banks[u][:])

        def pick(i):
            nc.vector.tensor_copy(out=whole[i], in_=h[i][:].indirect(pos2_t[:]))

        def subtract(i):
            nc.vector.tensor_tensor(diff[i], h[i][:].indirect(pos1_t[:]), whole[i], ALU.subtract)

        def bound(i):
            nc.scalar.activation(out=bounded[i], in_=diff[i], func=ACT.Tanh)

        z_rows = {}

        def weigh(i, on_gpsimd):
            a, t = divmod(i, PACK)
            dst = z_rows[t] if a == 0 else z_planes[a][:, t, 0:TAIL]
            src = bounded[i] if a == 0 else bounded[i][:, 0:TAIL]
            if on_gpsimd:
                nc.gpsimd.tensor_scalar(dst, src, gains[a][:, t:t + 1], 0.0, ALU.mult, ALU.add)
            else:
                nc.scalar.activation(out=dst, in_=src, func=ACT.Copy, scale=gains[a][:, t:t + 1])
            if a == 0:
                for u in range(2):
                    nc.sync.dma_start(out=z_halves[32 * i:32 * (i + 1), u, :, :], in_=z_rows[i][:, HALF * u:HALF * (u + 1)])

        def weave_z(a, c0, c1, copy):
            copy(out=z_woven[a][:, PACK * c0:PACK * c1].rearrange("p (c i t) -> p c t i", i=RUN, t=PACK),
                 in_=(z_halves[:, c0 // HALF, :, :] if a == 0 else z_planes[a][:, :, c0:c1]).rearrange("p t (c i) -> p c t i", i=RUN))

        def quantise_z(a, c0, c1):
            quantise(z_words[a][:, c0:c1], z_scales[a][:, c0:c1], z_woven[a][:, PACK * c0:PACK * c1])

        def second_product(n, a, c0, c1, start, stop):
            bank = y_end[n] if n < 2 and c0 == HALF else y_bank[n]
            nc.tensor.matmul_mx(out=bank[:, c0:c1], lhsT=w2_codes[:, a, 2 * P * n:2 * P * (n + 1)].bitcast(FP4X4),
                                lhsT_scale=w2_bytes[:, a, P * n:P * (n + 1)],
                                rhs=z_words[a][:, c0:c1].bitcast(FP8X4), rhs_scale=z_scales[a][:, c0:c1],
                                start=start, stop=stop)

        def pick_words(a, c0, c1):
            nc.vector.tensor_copy(out=moving(a, c0, c1),
                                  in_=table_words[a][:].bitcast(U32).indirect(offs_t[:, c0 // LANES:c1 // LANES]))

        pick_words(0, 0, S)
        cast_early(0, 0, on_scalar)
        quantise_early(0, 0)
        pick_words(1, 0, CUT)
        cast_early(1, 0, on_scalar)
        quantise_early(1, 0)
        pick_words(1, CUT, S)
        quarters = [psum.tile([P, BANK], F32, name="quarter%d" % n, tag="y_bank%d" % n) for n in range(PACK)]
        for n in range(PACK):
            first_pass(quarters[n], 0, 0, HALF * n, HALF * (n + 1))
        for n in range(PACK):
            first_pass(quarters[n], 0, 1, HALF * n, HALF * (n + 1))
            nc.scalar.copy(out=h[0][:, HALF * n:HALF * (n + 1)], in_=quarters[n][:, 0:HALF])
        for a in range(PASSES):
            cast_early(a, 1, on_vector)
        quantise_both(1, woven1[:])
        whole[0] = place([P, P1], F32, "second0", A)[:]
        woven2 = place([P, 2 * PASS], BF16, "woven2", B + EDGE)
        woven[0, 2], woven[1, 2] = woven2[:, 0:PASS], woven2[:, PASS:2 * PASS]
        cast_early(0, 2, on_scalar)
        cast_early(1, 2, on_pool)
        pick(0)
        quantise_both(2, woven2[:])
        diff[0] = place([P, P1], F32, "diff0", D)[:]
        subtract(0)

        h[1] = place([P, S], F32, "h1", D0 - 4 * KB + EDGE)
        first_product(1, False)
        late = place([P, LATE], BF16, "late", LATE_AT)
        woven_late[0] = late[:, 0:2048]
        woven[0, 3], woven[1, 3] = late[:, 1792:2304], late[:, 2304:2816]
        cast_early(0, 3, on_scalar)
        cast_early(1, 3, on_pool)
        whole[1] = place([P, P1], F32, "second1", D + 2 * KB)[:]
        pick(1)
        quantise_both(3, late[:, 1792:2816])
        diff[1] = place([P, P1], F32, "diff1", D1 + 2 * EDGE)[:]
        subtract(1)

        h[2] = place([P, S], F32, "h2", D1 - 4 * KB + EDGE)
        first_product(2, False)
        cast_late(0, 0, P // 2, raw_late0[0], on_scalar)
        h[3] = place([P, S], F32, "h3", E + EDGE)
        cast_late(0, P // 2, P, raw_late0[1], on_pool)
        whole[2] = place([P, P1], F32, "second2", D1 + 2 * KB + 2 * EDGE)[:]
        pick(2)
        first_product(3, False)
        idle = h_bank(3)
        for n in range(WARM):
            nc.tensor.matmul_mx(out=idle[:], lhsT=words[0, 2].bitcast(FP8X4), lhsT_scale=scales[0, 2],
                                rhs=words12[:].bitcast(FP8X4), rhs_scale=scales_early[:, 2 * P:6 * P], start=True, stop=True)
        pick(3)
        bounded[0] = place([P, P1], F32, "bounded0", E - 2 * KB + EDGE)[:]
        bound(0)
        late1 = place([P, PACK * PASS], BF16, "late1", E - 7 * KB + 3 * EDGE)
        woven_late[1] = late1[:]
        cast_late(1, POOL_SHARE, P, raw_late1[:, :, PACK * POOL_SHARE:PASS], on_scalar)
        cast_late(1, 0, POOL_SHARE, raw_late1[:, :, 0:PACK * POOL_SHARE], on_pool)
        quantise_late(0, 0, 1, place([P, P], U32, "words04", D + EDGE))
        diff[2] = place([P, P1], F32, "diff2", D - 2 * KB + EDGE)[:]
        subtract(2)
        quantise_late(1, 0, 1, tile([P, P], U32, "words14"))
        quantise_late(0, 1, PACK, place([P, 3 * P], U32, "words05", Y))
        quantise_late(1, 1, 2, place([P, P], U32, "words15", X))
        quantise_late(1, 2, PACK, place([P, 2 * P], U32, "words16", X + 2 * KB))
        diff[3] = place([P, P1], F32, "diff3", F + 6 * KB - EDGE)[:]
        subtract(3)
        bounded[1] = place([P, P1], F32, "bounded1", F)[:]
        bounded[2] = place([P, P1], F32, "bounded2", F + 2 * KB)[:]
        for i in range(3):
            z_rows[i] = place([P, P1], BF16, "z_rows%d" % i, W + KB * (i + 1))[:]

        bound(1)
        bound(2)
        weigh(0, True)
        weigh(1, True)
        weigh(2, True)
        first_product(4)
        pick(4)
        first_product(5, False)
        pick(5)
        bounded[3] = place([P, P1], F32, "bounded3", X)[:]
        bound(3)
        diff[4] = place([P, P1], F32, "diff4", Y - 2 * KB + EDGE)[:]
        diff[5] = place([P, P1], F32, "diff5", Y + KB + KB // 2 - EDGE)[:]
        strip = tile([P, PACK * P1], F32, "strip")
        bounded_late = strip[:].rearrange("p (t c) -> p t c", t=PACK)
        for t in range(PACK):
            bounded[PACK + t] = bounded_late[:, t, :]
        z_rows[3] = bounded[6][:, 0:HALF].bitcast(BF16)
        first_product(6, False)
        weigh(3, False)
        first_product(LAST, False)
        subtract(4)
        subtract(5)
        whole[6] = place([P, P1], F32, "second6", X + 2 * KB)[:]
        pick(6)
        nc.vector.tensor_copy(out=second_last[0], in_=h[LAST][:].indirect(pos2_t[:, 0:HALF // LANES]))
        bound(4)
        diff[6] = place([P, P1], F32, "diff6", Y - 2 * KB + 2 * EDGE)[:]
        subtract(6)
        weigh(4, True)

        bound(5)
        weigh(5, True)
        z_woven[0] = place([P, P1 * PACK], BF16, "z_woven0", Y - 6 * KB + 2 * EDGE)
        weave_z(0, 0, HALF, nc.scalar.copy)
        weave_z(0, HALF, P1, nc.scalar.copy)
        bound(6)

        quantise_z(0, 0, HALF)
        nc.vector.tensor_tensor(last_front, h[LAST][:].indirect(pos1_t[:, 0:HALF // LANES]), second_last[0], ALU.subtract)
        nc.vector.tensor_copy(out=second_last[1], in_=h[LAST][:].indirect(pos2_t[:, HALF // LANES:P1 // LANES]))
        quantise_z(0, HALF, P1)
        y_bank = [psum.tile([P, BANK], F32, name="y_bank%d" % n, tag="y_bank%d" % n) for n in range(N // P)]
        y_end = [h_bank(n) for n in range(2)]
        for half in (0, HALF):
            for n in range(N // P):
                for c0 in (half, half + P):
                    second_product(n, 0, c0, c0 + P, c0 == 0 or (n < 2 and c0 == HALF), False)
        last_back = spent[:, P1:P1 + HALF]
        for c0 in (HALF, TAIL):
            nc.vector.tensor_tensor(last_back[:, c0 - HALF:c0 - HALF + P], h[LAST][:].indirect(pos1_t[:, c0 // LANES:(c0 + P) // LANES]),
                                    second_last[1][:, c0 - HALF:c0 - HALF + P], ALU.subtract)
        nc.scalar.activation(out=bounded[LAST][:, 0:HALF], in_=last_front, func=ACT.Tanh)
        weigh(6, False)
        nc.scalar.activation(out=z_planes[1][:, PACK - 1, 0:HALF], in_=bounded[LAST][:, 0:HALF],
                             func=ACT.Copy, scale=gains[1][:, PACK - 1:PACK])
        for c0 in (HALF, TAIL):
            nc.scalar.activation(out=bounded[LAST][:, c0:c0 + P], in_=last_back[:, c0 - HALF:c0 - HALF + P], func=ACT.Tanh)
        nc.scalar.activation(out=z_planes[1][:, PACK - 1, HALF:TAIL], in_=bounded[LAST][:, HALF:TAIL],
                             func=ACT.Copy, scale=gains[1][:, PACK - 1:PACK])
        weave_z(1, 0, HALF, nc.vector.tensor_copy)
        weave_z(1, HALF, TAIL, nc.scalar.copy)
        nc.vector.tensor_tensor(z_woven[1][:, PACK * TAIL:PACK * P1].rearrange("p (c i t) -> p c t i", i=2, t=PACK),
                                bounded_late[:, :, TAIL:P1].rearrange("p t (c i) -> p c t i", i=2),
                                gains[1][:].unsqueeze(1).unsqueeze(3).to_broadcast([P, P // 2, PACK, 2]), ALU.mult)
        quantise_z(1, 0, HALF)
        quantise_z(1, TAIL, P1)
        quantise_z(1, HALF, TAIL)
        for n in range(2):
            for c0 in (0, P, TAIL):
                second_product(n, 1, c0, c0 + P, False, c0 == TAIL)
        for n in range(2):
            second_product(n, 1, HALF, TAIL, False, True)
        for n in (2, 3):
            second_product(n, 1, 0, P1, False, True)

        for n in range(N // P):
            if n < 2:
                nc.scalar.copy(out=y[n][:, 0:HALF], in_=y_bank[n][:, 0:HALF])
                nc.scalar.copy(out=y[n][:, TAIL:P1], in_=y_bank[n][:, TAIL:P1])
                nc.scalar.copy(out=y[n][:, HALF:TAIL], in_=y_end[n][:, HALF:TAIL])
            else:
                nc.scalar.copy(out=y[n][:], in_=y_bank[n][:])
            nc.vector.tensor_copy(out=right[n][:], in_=y[n][:].indirect(pos4_t[:]))
        for n in range(N // P):
            nc.scalar.activation(out=one_plus[n][:], in_=right[n][:], func=ACT.Copy, bias=1.0)
            nc.vector.tensor_tensor(result[n][:], y[n][:].indirect(pos3_t[:]), one_plus[n][:], ALU.mult)
            nc.sync.dma_start(out=out[P * n:P * (n + 1), :], in_=result[n][:])
